import numpy as np, ml_dtypes
CORES = [10,34,74,98]
N = 4
BF = ml_dtypes.bfloat16
V, L, T, RO, MIN = 8192, 256, 16, 3, 7
B, S = T // 16, V // L
def place(n, u, kk):
    return (((n * (2 * u + 1)) >> 5) + n + kk) & (V - 1)
def pack(X, A, z, w):
    a = np.ascontiguousarray(A.reshape(N, 8, B, 16, L).transpose(0, 1, 3, 2, 4)).reshape(N, 128, B * L)
    return {"xt": np.ascontiguousarray(X.reshape(N, 128, V)).astype(np.float32).astype(BF), "am": a.astype(np.int32),
            "zv": np.ascontiguousarray(z.reshape(N, 128, L)).astype(np.float32).astype(BF), "wt": np.ascontiguousarray(w.reshape(N, 128, 1)).astype(np.int32)}
def pools(rng, sizes):
    m = rng.choice(np.array(sizes), (N, 8, 1, L)); pool = rng.integers(0, V, (N, 8, T, L))
    return np.take_along_axis(pool, rng.integers(0, m, (N, 8, T, L)), 2)
def setup_inputs(rng):
    base = rng.integers(0, 256, (N, 8, 16, 1)).astype(np.int16); share = rng.choice(np.array([0.3, 0.5, 0.7], np.float32), (N, 8, 1, 1))
    X = np.where(rng.random((N, 8, 16, V), dtype=np.float32) < share, base, rng.integers(0, 256, (N, 8, 16, V), dtype=np.int16))
    return pack(X, pools(rng, [1, 2, 3, T, T, T, T, T]), rng.integers(0, 256, (N, 8, 16, L)), rng.integers(0, 16, (N, 8, 16)))
def setup_inputs_spread(rng):
    X = np.minimum(np.exp2(8 * rng.random((N, 8, 1, V))) * rng.random((N, 8, 16, V)), 255).astype(np.int16)
    A = np.exp2((V.bit_length() - 1) * rng.random((N, 8, T, L))).astype(np.int64) - 1
    A = np.where(rng.random((N, 8, T, L)) < rng.random((N, 8, 1, L)), V - 1 - A, A)
    z = np.minimum(np.exp2(8 * rng.random((N, 8, 1, L))) * rng.random((N, 8, 16, L)), 255).astype(np.int64)
    w = np.minimum(np.exp2(4 * rng.random((N, 8, 1))) * rng.random((N, 8, 16)), 15).astype(np.int64)
    return pack(X, A, z, w)
def setup_inputs_ends(rng):
    kd = rng.integers(0, 8, (N, 8, 1, V)); X = 255 * rng.integers(0, 2, (N, 8, 16, V), dtype=np.int16)
    kd[N - 1] = np.maximum(kd[N - 1], 2)
    X = np.where(kd == 0, 0, np.where(kd == 1, 255, X))
    full = np.all(X[N - 1] == 255, axis=1); X[N - 1, :, 15] = np.where(full, 0, X[N - 1, :, 15])
    X[::2, :, :, 0] = 255; X[1::2, :, :, 0] = 0; X[N - 1, :, :, 0] = 255
    c1 = place(V - 1, 1023, 0); X[:, 7, :, c1] = 255; X[::2, 7, :, c1] = 0; X[N - 1, 7, :, c1] = 0
    A = (V - 1) * (rng.random((N, 8, T, L)) < rng.choice(np.array([0.1, 0.5, 0.9]), (N, 8, 1, L))).astype(np.int64)
    A[:, :, 0, L - 1] = V - 1; A[:, :, T - 1, L - 1] = V - 1; A[:, :, T - 2, L - 1] = 0
    one = (V - 1) * rng.integers(0, 2, (8, 1, L)); one[:, :, 0] = 0; one[:, :, L - 1] = V - 1
    A[N - 2] = one; A[N - 1] = V - 1; A[N - 1, :, T - 1] = 0
    zk = rng.integers(0, 4, (N, 8, 1, L)); zk[..., 0] = 1; zk[..., 1] = 0; zk[..., L - 2] = 1
    z = np.where(zk == 0, 0, np.where(zk == 1, 255, 255 * rng.integers(0, 2, (N, 8, 16, L))))
    vec = np.array([255] * 13 + [30, 0, 0]); o = np.argsort(rng.random((N, 16, L)), axis=1)
    hit = rng.random((N, 1, L)) < 0.125; hit[..., L - 1] = True; hit[..., 0] = False; hit[..., 1] = False; hit[..., L - 2] = False
    z[:, 7] = np.where(hit, vec[o], z[:, 7])
    w = 15 * rng.integers(0, 2, (N, 8, 16)); w[:, 7] = 15; w[::2, 0] = 0
    return pack(X, A, z, w)
def setup_inputs_corners(rng):
    X = rng.integers(0, 256, (N, 8, 16, V), dtype=np.int16); c = np.arange(V); base = rng.choice(np.array([0, 1, 100, 255]), (N, 8, 16))
    prs = [(0, 1), (14, 15), (0, 15), (7, 8), (3, 4), (6, 9), (2, 12), (8, 15)]
    for q in range(N):
        o = rng.permutation(8)
        for g in range(8):
            p0, p1 = prs[int(o[g])]
            X[q, g, :p1] = base[q, g, :p1, None]
            X[q, g, p0] = (c >> 8) + (0 if rng.random() < 0.5 else 256 - (V >> 8)); X[q, g, p1] = c & 255
    zk = rng.integers(0, 4, (N, 8, 1, L))
    z = np.where(zk == 0, 0, np.where(zk == 1, 255, rng.integers(0, 256, (N, 8, 16, L))))
    wk = rng.integers(0, 4, (N, 8, 1)); w = np.where(wk == 0, 0, np.where(wk == 1, 15, rng.integers(0, 16, (N, 8, 16))))
    r = rng.permutation(N); z[r[0]] = 0; w[r[0]] = rng.integers(1, 16, (8, 16)); w[r[1]] = 0
    s = rng.choice(np.array([1, 2, T // 2, T // 2 + 1, T - 1, T]), (N, 8, 1, L))
    s[r[0]] = 1; s[r[1]] = 1; s[r[1], 7, 0, L - 1] = 2; s[r[2]] = T
    k = np.arange(T).reshape(1, 1, T, 1); h = V // 16 * 15 // T
    nm = k * h + rng.integers(0, h, (N, 8, T, L))
    u = np.sum(w[..., None] * z, axis=2, keepdims=True) & 1023
    nm = np.take_along_axis(nm, np.argsort(place(nm, u, 0), axis=2, kind="stable"), 2)
    A = np.take_along_axis(nm, np.where(k < T - s, k, 2 * T - 1 - s - k), 2)
    return pack(X, A, z, w)
def setup_inputs_ties(rng):
    base = rng.integers(1, 255, (N, 8, 16, 1)); base[:, 1::2] = rng.choice(np.array([1, 254]), (N, 4, 16, 1)); base = base.astype(np.int16)
    X = base + np.where(rng.random((N, 8, 16, V), dtype=np.float32) < 0.03, rng.integers(-1, 2, (N, 8, 16, V), dtype=np.int16), 0)
    A = pools(rng, [1, 2, T, T]); A[:, 0] = A[:, 0, :, :1]
    n = rng.choice(np.array([0, MIN - 1, MIN, MIN, MIN + 1, 16]), (N, 8, 1, L)); o = np.argsort(np.argsort(rng.random((N, 8, 16, L)), axis=2), axis=2)
    return pack(X, A, base.astype(np.int64) - (o >= n), rng.integers(0, 16, (N, 8, 16)))
def setup_inputs_few(rng):
    base = rng.integers(0, 256, (N, 8, 16, 1)).astype(np.int16)
    X = np.where(rng.random((N, 8, 16, V), dtype=np.float32) < 0.4, base, rng.integers(0, 256, (N, 8, 16, V), dtype=np.int16))
    A = pools(rng, [1, 2, 3, T, T, T, T, T]); w = rng.integers(0, 16, (N, 8, 16))
    q = int(rng.integers(0, N)); p = (q + 1) % N; a = rng.permutation(3) + 1
    near = [(q - d) % N for d in range((RO - 2) * (RO - 1) // 2 + 1)]
    A[near] = rng.integers(0, V, (8, 1, L)); A[p] = rng.integers(0, V, (8, 1, L))
    w[q] = 0; w[p] = 0
    nm = np.arange(V); rest = place(nm, 0, 0) % S; ok = (rest >= 1) & (rest <= S - 4)
    lows, highs = nm[ok & (nm < V // 4)], nm[ok & (nm >= V // 2) & (nm < 3 * V // 4)]
    for r, rs, kinds in ((q, near, np.repeat(np.arange(RO - 1), a[:RO - 1])), (p, [p], np.zeros(int(a[2]), np.int64))):
        for g, t in zip(rng.permutation(8), kinds):
            i = int(rng.integers(0, L)); n, m = int(rng.choice(lows)), int(rng.choice(highs))
            if rng.random() < 0.5: n, m = m, n
            for v in rs: A[v, g, :, i] = n
            A[r, g, 0, i] = m
            for j in range(int(t) + 1):
                k = 0 if j == 0 else int(a[j - 1])
                X[r, g, 0, place(n, 0, k)] = 0 if j < t else 255
                X[r, g, 0, place(m, 0, k)] = 255 if j < t else 0
    return pack(X, A, rng.integers(0, 256, (N, 8, 16, L)), w)
def check_inputs(d):
    bad = []
    for k, lo, hi in (("xt", 0, 255), ("am", 0, V - 1), ("zv", 0, 255), ("wt", 0, 15)):
        v = np.asarray(d[k]).astype(np.float64)
        if not (np.min(v) >= lo and np.max(v) <= hi and np.all(v == np.floor(v))): bad.append("range of " + k)
    return bad
def pick(X, c):
    return np.take_along_axis(X, c.reshape(N, 8, 1, T * L), 3).reshape(N, 8, 16, T, L)
def keys(v):
    out = []
    for b in (0, 8):
        h = np.zeros((N, 8, T, L), np.uint64)
        for p in range(b, b + 8): h = (h << np.uint64(8)) | v[:, :, p].astype(np.uint64)
        out.append(h)
    return out
def below(h, l, h0, l0):
    return (h < h0) | ((h == h0) & (l < l0))
def close(n, keep):
    o = np.argsort(~keep, axis=2, kind="stable")
    return np.where(np.take_along_axis(keep, o, 2), np.take_along_axis(n, o, 2), -1)
def reference(xt, am, zv, wt):
    X = xt.astype(np.float32).astype(np.int32).reshape(N, 8, 16, V)
    A = am.astype(np.int64).reshape(N, 8, 16, B, L).transpose(0, 1, 3, 2, 4).reshape(N, 8, T, L)
    z = zv.astype(np.float32).astype(np.int64).reshape(N, 8, 16, L); w = wt.astype(np.int64).reshape(N, 8, 16, 1)
    kk = np.zeros((N, 1, 1, 1), np.int64); lane = np.arange(L).reshape(1, 1, 1, L); row = np.arange(T).reshape(1, 1, T, 1)
    for t in range(RO):
        u = np.sum(w * z, axis=2, keepdims=True) & 1023
        x = pick(X, place(A, u, kk)); ha, la = keys(x)
        live = np.ones((N, 8, T, L), bool); mh, ml = ha[:, :, T - 1], la[:, :, T - 1]
        for k in range(T - 2, -1, -1):
            less = below(ha[:, :, k], la[:, :, k], mh, ml); live[:, :, k] = ~less
            mh = np.where(less, mh, ha[:, :, k]); ml = np.where(less, ml, la[:, :, k])
        alpha = close(A, live)
        first = np.argmax(live, axis=2)
        M = np.take_along_axis(x, first[:, :, None, None, :], 3)[:, :, :, 0]
        beta = np.stack([alpha[(q - 1 - t % (N - 1)) % N] for q in range(N)]); has = beta >= 0
        y = pick(X, place(np.maximum(beta, 0), u, kk)); hy, ly = keys(y)
        front = np.sum(z >= M, axis=2, keepdims=True) >= MIN
        ka = live & ~below(ha, la, hy[:, :, :1], ly[:, :, :1]); kb = has & ~below(hy, ly, mh[:, :, None], ml[:, :, None])
        names = np.where(front, np.concatenate([A, beta], axis=2), np.concatenate([beta, A], axis=2))
        keep = np.where(front, np.concatenate([ka, has], axis=2), np.concatenate([kb, live], axis=2))
        new = close(names, keep)[:, :, :T]
        A = np.where(new >= 0, new, (((A * u) >> 5) + 37 * row + u) & (V - 1))
        col = np.broadcast_to(S * lane + (u & (S - 1)), (N, 8, 16, L))
        np.put_along_axis(X, col, ((np.take_along_axis(X, col, 3) + M) >> 1).astype(np.int32), 3)
        z = np.abs(z - y[:, :, :, 0])
        kk = np.sum(~live, axis=(1, 2, 3)).reshape(N, 1, 1, 1)
    yx = np.sum(X.reshape(N, 128, 4, V // 4), axis=2)
    ya = A.reshape(N, 8, B, 16, L).transpose(0, 1, 3, 2, 4).reshape(N, 128, B * L)
    return {"yx": yx.astype(np.float32), "ya": np.ascontiguousarray(ya).astype(np.float32), "yz": z.reshape(N, 128, L).astype(np.float32)}

@@ -1,0 +1,632 @@
+from concourse.bass import DstId, RemoteDMATransfer
+from concourse.mybir import dt, AluOpType, AxisListType, ActivationFunctionType
+
+V, L, RO, N = 8192, 256, 3, 4
+F32, BF, I32, U16 = "float32", "bfloat16", "int32", "uint16"
+
+
+def _sb(n, d):
+    return ("sbuf", [128, n], d)
+
+
+SCRATCH = {
+    "X": _sb(V, BF), "xg": _sb(4096, BF), "yg": _sb(4096, BF), "yxs": _sb(2048, F32),
+    "ami": _sb(256, I32), "wti": _sb(4, I32), "Z": _sb(256, BF), "Zb": _sb(256, BF), "zf": _sb(256, F32),
+    "nf": _sb(4 * 256, F32), "bn": _sb(3 * 256, F32), "dA": _sb(3 * 256, BF), "dB": _sb(3 * 256, BF),
+    "offx": _sb(256, U16), "offy": _sb(256, U16), "offm": _sb(48, U16), "offb": _sb(48, U16),
+    "offc": _sb(32, U16), "D": _sb(256, F32),
+    "si": _sb(256, I32), "ui": _sb(256, I32), "t5": _sb(256, I32),
+    "p1": _sb(512, F32), "p2": _sb(512, I32), "p3": _sb(512, I32),
+    "f1": _sb(256, I32), "f2": _sb(256, I32), "fb": _sb(256, F32),
+    "tt": _sb(256, F32), "S": _sb(256, F32), "pen": _sb(256, BF),
+    "c1": _sb(512, BF), "ee": _sb(576, BF), "sg": _sb(512, BF), "xo": _sb(256, BF),
+    "Mb": _sb(256, BF), "Yb": _sb(256, BF), "ge": _sb(256, BF), "TH": _sb(512, BF),
+    "CD": _sb(128, F32), "oneF": _sb(128, F32),
+    "DS": _sb(4 * 768, BF), "keep": _sb(512, BF), "kf": _sb(512, BF),
+    "k1": _sb(512, I32), "k2": _sb(512, I32), "va": _sb(512, F32), "vb": _sb(512, F32), "mg": _sb(256, F32),
+    "r1": _sb(256, I32), "r2": _sb(256, I32), "yas": _sb(256, F32),
+    "ci": _sb(16, I32), "cj": _sb(16, I32), "cf": _sb(16, F32), "xs": _sb(256, F32), "xi": _sb(256, I32),
+    "xn": _sb(256, F32), "junk": _sb(256, F32), "K32": _sb(4, F32),
+    "lin": _sb(256, F32), "idq": _sb(768, F32), "srev": _sb(256, F32), "gl": _sb(256, F32), "cm16": _sb(128, F32),
+    "pi": _sb(16, I32), "col": _sb(32, F32), "c32": _sb(32, F32),
+    "IB": _sb(10 * 128, BF), "IF": _sb(128, F32), "PP": _sb(128, F32), "Wrep": _sb(768, BF), "Wk": _sb(48, BF),
+    "blk": _sb(128, BF), "Wblk": _sb(128, BF), "Wband": _sb(144, BF), "diag": _sb(128, BF), "seg": _sb(128, BF),
+    "d0": _sb(128, BF), "ones": _sb(256, BF), "cc": _sb(128, BF), "rows": _sb(272, BF),
+    "mG": _sb(264, BF), "Tri": _sb(264, BF), "D16": _sb(264, BF), "D8": _sb(264, BF), "Prm": _sb(264, F32),
+    "tmp": _sb(264, F32), "tm2": _sb(264, F32),
+}
+PSUM = ("xa0", "xa1", "b0", "ya0", "ya1", "b1", "m0", "m1")
+for _b in PSUM:
+    SCRATCH[_b] = ("psum", [128, 512], F32)
+
+SEMAPHORES = (["eV", "eA", "eP", "eG", "sent"] + ["d%d" % i for i in range(16)]
+              + ["%s%d" % (s, i) for s in ("rn", "rd", "ro") for i in range(6)])
+
+CY, PECY, FIX, LAT, GA = 1.04, 0.55, 60.0, 90.0, 1.56
+GSPLIT = 4
+GX = (("A", "A"), ("A", "A"))
+GY = (("A", "A"), ("A", "A"))
+GALT = 0.0
+RENG = "AV"
+DENG = ("A", "AV")
+MODPE = False
+LEAD = 5000.0
+SEED, NOISE = 1, 800.0
+FALT = 300.0
+PASSES = 350
+SLACK = 2500.0
+
+
+def meets(x, y):
+    if x[1] <= y[0] or y[1] <= x[0]:
+        return False
+    return not (x[2] == y[2] and x[2] > 1 and x[0] % x[2] != y[0] % y[2])
+
+
+def brev(x):
+    return ((x & 1) << 3) | ((x & 2) << 1) | ((x & 4) >> 1) | ((x & 8) >> 3)
+
+
+def plan_order(ops):
+    hist = {}
+    for i, o in enumerate(ops):
+        deps = set(o["after"])
+        for x in o["r"]:
+            for (j, w, y) in hist.get(x[0], []):
+                if w and meets(x[1:], y):
+                    deps.add(j)
+        for x in o["w"]:
+            for (j, w, y) in hist.get(x[0], []):
+                if meets(x[1:], y):
+                    deps.add(j)
+        for x in o["w"]:
+            hist[x[0]] = [e for e in hist.get(x[0], [])
+                          if not (x[1] <= e[2][0] and e[2][1] <= x[2] and (x[3] == 1 or x[1:] == e[2]))]
+        for x in o["r"]:
+            hist.setdefault(x[0], []).append((i, False, x[1:]))
+        for x in o["w"]:
+            hist.setdefault(x[0], []).append((i, True, x[1:]))
+        deps.discard(i)
+        o["deps"] = sorted(deps)
+        o["banks"] = sorted(set(x[0] for x in o["r"] + o["w"] if x[0] in PSUM))
+    n = len(ops)
+    succ = [[] for _ in range(n)]
+    for i, o in enumerate(ops):
+        for d in o["deps"]:
+            succ[d].append(i)
+    pr = [0.0] * n
+    for i in range(n - 1, -1, -1):
+        pr[i] = ops[i]["cost"] + ops[i]["lat"] + max([LAT + pr[s] for s in succ[i]] + [0.0])
+    x = SEED
+    for i in range(n):
+        x = (x * 1103515245 + 12345) % 2147483648
+        pr[i] += NOISE * (x / 2147483648.0) - LEAD * ops[i]["half"]
+    pred = [o["deps"] for o in ops]
+
+    def tail(lst, t):
+        k = len(lst)
+        while k and lst[k - 1][1] > t:
+            k -= 1
+        return lst[k:]
+
+    def put(lst, v):
+        k = len(lst)
+        while k and lst[k - 1][0] > v[0]:
+            k -= 1
+        lst.insert(k, v)
+
+    def place(pred, succ, pr, back):
+        left = [len(p) for p in pred]
+        ready = [i for i in range(n) if left[i] == 0]
+        end, on, busy = [0.0] * n, [None] * n, {}
+        while ready:
+            i = max(ready, key=lambda j: pr[j])
+            o = ops[i]
+            c = o["cost"]
+            if back:
+                t0 = max([end[d] + LAT for d in pred[i]] + [0.0]) + o["lat"]
+            else:
+                t0 = max([end[d] + ops[d]["lat"] + LAT for d in pred[i]] + [0.0])
+            best = None
+            for e in o["eng"]:
+                iv = tail(busy.get(e, []), t0)
+                if o["banks"]:
+                    for b in o["banks"]:
+                        iv = iv + [(a - LAT, z + LAT) for (a, z, e2) in tail(busy.get(b, []), t0 - LAT) if e2 != e]
+                    iv.sort()
+                st = t0
+                for (a, z) in iv:
+                    if a >= st + c:
+                        break
+                    st = max(st, z)
+                key = st + (0.0 if e == o["eng"][0] else o["alt"])
+                if best is None or key < best[0]:
+                    best = (key, e, st)
+            _, e, st = best
+            on[i], end[i] = e, st + c
+            put(busy.setdefault(e, []), (st, st + c))
+            for b in o["banks"]:
+                put(busy.setdefault(b, []), (st, st + c, e))
+            ready.remove(i)
+            for s in succ[i]:
+                left[s] -= 1
+                if left[s] == 0:
+                    ready.append(s)
+        return end, on
+
+    best = None
+    for it in range(PASSES):
+        end, on = place(pred, succ, pr, False)
+        span = max(end[i] + ops[i]["lat"] for i in range(n))
+        if best is None or span <= best[0] + SLACK * (1.0 - it / PASSES):
+            cur = (span, end, on)
+            if best is None or span < best[0]:
+                best = cur
+        back = []
+        for i in range(n):
+            x = (x * 1103515245 + 12345) % 2147483648
+            back.append(cur[1][i] + ops[i]["lat"] + NOISE * (x / 2147483648.0))
+        pr, _ = place(succ, pred, back, True)
+    span, end, on = best
+    for i, o in enumerate(ops):
+        o["on"], o["st"] = on[i], end[i] - o["cost"]
+    return sorted(range(n), key=lambda j: (ops[j]["st"], j)), span
+
+
+def build(g, core, T, topo):
+    rank = T.rank_of(core)
+    A, AF = AluOpType, ActivationFunctionType
+    Q = {"V": g.vector, "A": g.scalar, "P": g.tensor, "G": g, "S": g.sync}
+    ops = []
+    ndma = [0]
+    cur = [0]
+
+    def R(nm, lo=0, hi=None, step=1, p=None):
+        if hi is None:
+            hi = SCRATCH[nm][1][1]
+        t = T[nm]
+        ap = t[:, lo:hi:step] if p is None else t[p[0]:p[1], lo:hi:step]
+        return (ap, (nm, lo, hi, step), len(range(lo, hi, step)), SCRATCH[nm][2] in (BF, U16), nm in PSUM)
+
+    def add(eng, fn, r, w, cost, lat=0.0, sem=None, cnt=0, after=(), alt=0.0):
+        ops.append({"eng": eng, "fn": fn, "r": [x[1] for x in r], "w": [x[1] for x in w], "cost": cost, "lat": lat,
+                    "sem": sem, "cnt": cnt, "after": list(after), "alt": alt, "half": cur[0]})
+        return len(ops) - 1
+
+    def vc(n, f=1.0):
+        return FIX + max(n * f, 32) * CY
+
+    def sc(x):
+        return x[0] if isinstance(x, tuple) else x
+
+    def tup(*xs):
+        return [x for x in xs if isinstance(x, tuple)]
+
+    def ts(o, i, s1, op0, s2=None, op1=None):
+        fl = all(SCRATCH[x[1][0]][2] in (F32, BF) for x in (o, i))
+        affine = fl and ((op0 == A.mult and (op1 is None or op1 == A.add)) or (op0 == A.add and op1 is None))
+
+        def fn(e):
+            if e == "A":
+                if op0 == A.add:
+                    return g.scalar.activation(o[0], i[0], AF.Identity, bias=sc(s1))
+                return g.scalar.activation(o[0], i[0], AF.Identity, bias=0.0 if op1 is None else sc(s2), scale=sc(s1))
+            if op1 is None:
+                return g.vector.tensor_scalar(o[0], i[0], sc(s1), None, op0)
+            return g.vector.tensor_scalar(o[0], i[0], sc(s1), sc(s2), op0, op1)
+        return add("AV" if affine else "V", fn, tup(i, s1, s2), [o], vc(i[2], 0.5 if o[3] and i[3] else 1.0), alt=FALT)
+
+    def tt(o, a, b, op):
+        return add("V", lambda e: g.vector.tensor_tensor(o[0], a[0], b[0], op), [a, b], [o],
+                   vc(a[2], 1.0 if a[4] or b[4] else 2.0))
+
+    def cp(o, i, eng="V"):
+        def fn(e):
+            if e == "A":
+                return g.scalar.activation(o[0], i[0], AF.Identity)
+            return g.vector.tensor_copy(o[0], i[0])
+        return add(eng, fn, [i], [o], vc(i[2]), alt=FALT if eng == "AV" else 0.0)
+
+    def scan(o, a, b, op0, op1, init=0.0):
+        return add("V", lambda e: g.vector.tensor_tensor_scan(o[0], a[0], b[0], init, op0, op1), [a, b], [o],
+                   vc(a[2], 0.5 if o[3] and a[3] and b[3] else 1.0))
+
+    def act(o, i, func, bias=0.0, scale=1.0, acc=None):
+        def fn(e):
+            if acc is None:
+                return g.scalar.activation(o[0], i[0], func, bias=sc(bias), scale=scale)
+            return g.scalar.activation(o[0], i[0], func, bias=sc(bias), scale=scale, accum_out=acc[0])
+        return add("A", fn, tup(i, bias), tup(o, acc), vc(i[2]))
+
+    def mset(o, c):
+        return add("V", lambda e: g.vector.memset(o[0], c), [], [o], vc(o[2], 0.5 if o[3] else 1.0))
+
+    def iota(o, pat, base=0, cm=0):
+        def fn(e):
+            if SCRATCH[o[1][0]][2] == I32:
+                return g.iota(o[0], pat, base, cm)
+            return g.iota(o[0], pat, base, cm, allow_small_or_imprecise_dtypes=True)
+        return add("G", fn, [], [o], 150 + 2 * o[2] * CY)
+
+    def mm(lst, start=True, stop=True, wr=None, after=()):
+        def fn(e):
+            ins = None
+            for k, (o, l, r) in enumerate(lst):
+                ins = g.tensor.matmul(o[0], l[0], r[0], start and k == 0, stop and k == len(lst) - 1)
+            return ins
+        cost = sum(max(64, r[2]) * (1 if r[3] else 4) * PECY for (o, l, r) in lst) + 40
+        return add("P", fn, [x[1] for x in lst] + [x[2] for x in lst], wr or [x[0] for x in lst], cost, after=after)
+
+    def relu(o, i):
+        def fn(e):
+            if e == "A":
+                return g.scalar.activation(o[0], i[0], AF.Relu)
+            return g.vector.tensor_scalar(o[0], i[0], 0.0, None, A.max)
+        return add(RENG, fn, [i], [o], vc(i[2]))
+
+    def gather(o, win, off, bias=None, eng="AV", alt=0.0):
+        def fn(e):
+            src = win[0].indirect(off[0])
+            if e == "A":
+                if bias is None:
+                    return g.scalar.activation(o[0], src, AF.Identity)
+                return g.scalar.activation(o[0], src, AF.Identity, bias=bias[0])
+            if bias is None:
+                return g.vector.tensor_copy(o[0], src)
+            return g.vector.tensor_scalar(o[0], src, bias[0], None, A.add)
+        return add(eng, fn, tup(win, off, bias), [o], vc(o[2], GA), alt=alt)
+
+    def dma(eng, o, i, r, w, lat):
+        s = "d%d" % ndma[0]
+        ndma[0] += 1
+        return add(eng, lambda e: Q[e].dma_start(o, i), r, w, 60.0, lat=lat, sem=s, cnt=16)
+
+    nsent = [0]
+
+    def send(src, dst, sem, to, lat):
+        rid, pid, _ = topo.addr(to)
+        mask = topo.mask(core, to)
+        ne = len(topo.engines(core, to))
+        nsent[0] += ne
+        i = add("G", lambda e: g.remote_dma(dst[0], src[0], T.sem[sem], T.sem.sent, pid, rid, mask), [src], [],
+                300.0, sem="-")
+        add("N", None, [], [dst], 1.0, lat=lat, sem=sem, cnt=ne, after=[i])
+
+    C = lambda j: R("col", j, j + 1)
+    PI = lambda j: R("pi", j, j + 1)
+    IB = lambda j: R("IB", 128 * j, 128 * j + 128)
+
+    dma("S", T.ami[:], T.am[:], [], [R("ami")], 2000.0)
+    dma("S", T.Z[:], T.zv[:], [], [R("Z")], 2000.0)
+    dma("S", T.wti[:, 0:1], T.wt[:], [], [R("wti")], 2000.0)
+    dma("A", T.X[:], T.xt[:], [], [R("X")], 8000.0)
+
+    iota(PI(0), [[0, 1]], 0, 1)
+    iota(R("lin"), [[1, 256]])
+    iota(R("idq"), [[1, 48], [0, 16]])
+    for q in range(4):
+        iota(R("srev", 64 * q, 64 * q + 64), [[4, 2], [8, 2], [0, 16]], (q >> 1) + 2 * (q & 1))
+    iota(R("gl"), [[0, 16], [1, 16]])
+    iota(R("c32", 0, 16), [[512, 16]])
+    iota(R("c32", 16, 32), [[0, 4], [512, 4]])
+    ts(PI(1), PI(0), 15, A.bitwise_and)
+    ts(PI(2), PI(0), 4, A.arith_shift_right)
+    cp(C(0), PI(0)); cp(C(1), PI(1)); cp(C(2), PI(2))
+    ts(PI(3), PI(1), 11.0, A.mult)
+    ts(PI(4), PI(3), 5, A.arith_shift_right)
+    cp(C(3), PI(4))
+    ts(C(4), C(3), -3.0, A.mult, C(1), A.add)
+    ts(C(5), C(3), 8.0, A.mult, C(2), A.add)
+    ts(C(6), C(4), 0.0, A.is_equal, -65535.0, A.mult)
+    ts(C(7), C(4), 1.0, A.is_equal, -255.0, A.mult)
+    ts(C(8), C(6), C(7), A.add, -1.0, A.add)
+    ts(C(9), C(4), 2.0, A.is_equal)
+    ts(C(10), C(1), 15.0, A.is_equal, C(9), A.add)
+    BIAS = C(24)
+    ts(BIAS, C(10), -1.0, A.mult, -255.0, A.add)
+    ts(C(11), BIAS, 0.5, A.mult, 0.25, A.add)
+    ts(C(23), BIAS, 0.5, A.add)
+    ts(C(12), C(1), 16.0, A.mult)
+    ts(C(13), C(1), 32.0, A.mult)
+    ts(C(14), C(2), 16.0, A.mult)
+    ts(C(15), C(14), 15.0, A.add)
+    ts(C(16), C(2), 8.0, A.add)
+    ts(C(17), C(1), -1.0, A.mult, 15.0, A.add)
+    cp(C(18), R("wti", 0, 1))
+    ts(R("IF"), R("lin", 0, 128), C(0), A.is_equal)
+    ts(IB(0), R("lin", 0, 128), C(0), A.is_equal)
+    for j, c in ((1, -1.0), (2, -2.0 ** 86), (3, 2.0 ** -10), (4, -8.0)):
+        ts(IB(j), IB(0), c, A.mult)
+    ts(R("Wk"), R("lin", 0, 48), C(5), A.is_equal, C(8), A.mult)
+    for j in range(6):
+        ts(R("Wk", 8 * j, 8 * j + 8), R("Wk", 8 * j, 8 * j + 8), -2.0 ** (50 - 26 * j), A.mult)
+    add("V", lambda e: g.vector.tensor_reduce(T.col[:, 25:26], T.Wk[:], AxisListType.X, A.add, negate=True),
+        [R("Wk")], [C(25)], vc(48))
+    ts(R("Wrep"), R("idq"), C(5), A.is_equal, C(25), A.mult)
+    ts(R("blk"), R("idq", 0, 128), C(2), A.is_equal)
+    ts(R("Wblk"), R("idq", 0, 128), C(2), A.is_equal, C(18), A.mult)
+    ts(R("Wband"), R("lin", 0, 144), C(15), A.is_equal, C(18), A.mult)
+    ts(R("diag", 0, 16), R("gl", 0, 16), C(1), A.is_equal)
+    ts(R("seg"), R("gl", 0, 128), 0.0, A.is_equal, -2.0 ** 90, A.mult)
+    tt(R("tmp", 0, 16), R("diag", 0, 16), R("srev", 0, 256, 16), A.mult)
+    add("V", lambda e: g.vector.tensor_reduce(T.col[:, 19:20], T.tmp[:, 0:16], AxisListType.X, A.add),
+        [R("tmp", 0, 16)], [C(19)], vc(16))
+    ts(C(20), C(19), C(14), A.add)
+    ts(R("PP"), R("lin", 0, 128), C(20), A.is_equal)
+    ts(C(21), C(19), 1184.0, A.mult)
+    KM, KMASK = float(0x1111 << 12), (1 << 24) | (1 << 21) | (1 << 18) | (1 << 15)
+    ts(PI(5), C(19), KM, A.mult)
+    ts(PI(6), PI(5), KMASK, A.bitwise_and)
+    ts(C(22), PI(6), -1.0, A.mult, 2.0 ** 24 - 8192.0, A.add)
+    ts(R("CD"), R("IF"), C(22), A.mult)
+    mset(R("oneF"), 1.0)
+    mset(R("d0", 0, 1), 0.0)
+    tt(R("d0", 1, 16), R("srev", 16, 256, 16), R("srev", 0, 240, 16), A.subtract)
+    for w_ in (16, 32, 64):
+        cp(R("d0", w_, 2 * w_), R("d0", 0, w_))
+    mset(R("ones"), 1.0)
+    mset(R("cc", p=(0, 32)), -2.0 ** 19)
+    mset(R("cc", p=(32, 64)), 384.0)
+    mset(R("rows", 0, 256), -0.5)
+    ts(R("rows", 256, 272), R("lin", 0, 16), 256.0, A.mult)
+    ts(R("c32"), R("c32"), C(13), A.add)
+    for nm in ("mG", "Tri", "D8", "Prm"):
+        mset(R(nm, 256, 264), 0.0)
+    ts(R("mG", 0, 256), R("gl"), C(16), A.is_equal)
+    ts(R("tmp", 0, 256), R("srev"), C(17), A.is_equal, 8192.0, A.mult)
+    tt(R("D8", 0, 256), R("tmp", 0, 256), R("mG", 0, 256), A.mult)
+    ts(R("tm2", 0, 256), R("srev"), C(17), A.is_gt, 0.5, A.mult)
+    ts(R("tmp", 0, 256), R("tmp", 0, 256), C(1), A.mult, -0.5 / 8192, A.mult)
+    tt(R("tmp", 0, 256), R("tmp", 0, 256), R("tm2", 0, 256), A.add)
+    tt(R("Tri", 0, 256), R("tmp", 0, 256), R("mG", 0, 256), A.mult)
+    ts(R("tm2", 0, 256), R("idq", 0, 256), C(1), A.is_equal)
+    tt(R("Prm", 0, 256), R("tm2", 0, 256), R("mG", 0, 256), A.mult)
+    mset(R("tt"), -2.0 ** 90)
+    mset(R("ee"), 0.0)
+    mset(R("K32", 0, 1), 135168.0)
+    ts(R("junk"), R("ami"), -4096.0, A.add)
+    for h in range(2):
+        mm([(R("m%d" % h, 0, 128), R("PP"), R("junk", 128 * h, 128 * h + 128))])
+        cp(R("nf", 128 * h, 128 * h + 128), R("m%d" % h, 0, 128), "AV")
+
+    def plane(h, j, lo=0, hi=128):
+        if j < 4:
+            return R("xa%d" % h, 128 * j + lo, 128 * j + hi)
+        return R("b%d" % h, 128 * (j - 4) + lo, 128 * (j - 4) + hi)
+
+    def offsets(src, off, M, tmp, h):
+        tt(R("p1", tmp, tmp + 128), src, R(M, 128, 256), A.mult)
+        tt(R("p2", tmp, tmp + 128), R("p1", tmp, tmp + 128), R(M, 256, 384), A.add)
+        ts(R("p3", tmp, tmp + 128), R("p2", tmp, tmp + 128), 5, A.arith_shift_right, V - 1, A.bitwise_and)
+        cp(R(off, 128 * h, 128 * h + 128), R("p3", tmp, tmp + 128))
+
+    def items(off, buf, h, eng):
+        w_ = 128 // GSPLIT
+        for q in range(GSPLIT):
+            lo = 128 * h + w_ * q
+            gather(R(buf, 16 * lo, 16 * (lo + w_)), R("X"), R(off, lo, lo + w_), BIAS, eng[q % len(eng)], alt=GALT)
+
+    def keys(buf, bank, h, part, stop):
+        n = (32, 16)[part]
+        mm([(R(bank, k, 16 * n, 16), R(buf, 2048 * h + 15 - brev(k), 2048 * h + 2048, 16),
+             R("Wk", 32 * part, 32 * part + n)) for k in range(16)], stop=stop, wr=[R(bank)])
+
+    def diffs(piv, a, h, ds):
+        mm([(R(a + str(h)), piv, R("Wrep", 0, 512))], start=False)
+        mm([(R("b%d" % h, 0, 256), piv, R("Wrep", 512, 768))], start=False)
+        cp(R("DS", ds, ds + 512), R(a + str(h)), DENG[0])
+        cp(R("DS", ds + 512, ds + 768), R("b%d" % h, 0, 256), DENG[1])
+
+    def fix(q):
+        off = T.offc[:, 16 + 4 * q:20 + 4 * q]
+        a, b = R("xs", 64 * q, 64 * q + 64), R("xn", 64 * q, 64 * q + 64)
+        add("V", lambda e: g.vector.tensor_tensor(a[0], T.yxs[:].indirect(off), b[0], A.add),
+            [R("yxs"), R("offc", 16, 32), b], [a], vc(64, GA))
+        add("V", lambda e: g.vector.tensor_copy(T.yxs[:].indirect(off), a[0]),
+            [a, R("offc", 16, 32)], [R("yxs")], vc(64, 3.8))
+
+    def order_sum(out, ds, dead, th):
+        mm([(out, R("DS", ds + 128 * j, ds + 128 * j + 128), IB(0)) for j in range(6)]
+           + [(out, dead, IB(2)), (out, IB(3), th)])
+
+    for t in range(RO):
+        to = T.cores[(rank + 1 + t % (N - 1)) % N]
+        H = range(2)
+        ln = lambda nm, h, base=0: R(nm, base + 128 * h, base + 128 * h + 128)
+        for h in H:
+            send(ln("nf", h, 256 * t), ln("bn", h, 256 * t), "rn%d" % (2 * t + h), to, 3500.0)
+        for h in H:
+            cur[0] = h
+            M = "m%d" % h
+            mm([(R(M, 0, 128), R("Wblk"), ln("Z", h))])
+            cp(ln("si", h), R(M, 0, 128))
+            ts(ln("ui", h), ln("si", h), 1023, A.bitwise_and)
+            ts(ln("t5", h), ln("si", h), 31, A.bitwise_and)
+            ts(R(M, 128, 256), ln("ui", h), 2.0, A.mult, 33.0, A.add)
+            ts(R(M, 256, 384), ln("t5", h), 8192.0, A.mult, R("K32", t, t + 1), A.add)
+            offsets(ln("nf", h, 256 * t), "offx", M, 128 * h, h)
+        mm([(R("m0", 384, 400), R("Wband", 15 - il, 143 - il), R("Z", il, 256, 16)) for il in range(16)])
+        cp(R("ci"), R("m0", 384, 400))
+        ts(R("cj"), R("ci"), 31, A.bitwise_and)
+        tt(R("cf"), R("cj"), R("c32", 0, 16), A.add)
+        cp(R("offc", 0, 16), R("cf"))
+        if t == RO - 1:
+            tt(R("cf"), R("cj"), R("c32", 16, 32), A.add)
+            cp(R("offc", 16, 32), R("cf"))
+            for q in range(4):
+                bk = "ya%d" % (q & 1)
+                mm([(R(bk), IB(0), R("X", 2048 * a + 512 * q, 2048 * a + 512 * q + 512)) for a in range(4)])
+                cp(R("yxs", 512 * q, 512 * q + 512), R(bk), "AV")
+        for h in H:
+            cur[0] = h
+            items("offx", "xg", h, GX[h])
+            keys("xg", "xa%d" % h, h, 0, True)
+            keys("xg", "b%d" % h, h, 1, True)
+            offsets(ln("bn", h, 256 * t), "offy", "m%d" % h, 256 + 128 * h, h)
+            items("offy", "yg", h, GY[h])
+            keys("yg", "ya%d" % h, h, 0, False)
+        for h in H:
+            cur[0] = h
+            M = "m%d" % h
+            act(R(M, 0, 128), ln("nf", h, 256 * t), AF.Identity, bias=4128.0)
+            tt(ln("f1", h), ln("ui", h), R(M, 0, 128), A.mult)
+            ts(ln("f2", h), ln("f1", h), C(21), A.add)
+            ts(ln("f1", h), ln("f2", h), 5, A.arith_shift_right, V - 1, A.bitwise_and)
+            for j in range(6):
+                Kp = plane(h, j)
+                sg = R("seg", 1, 128) if j == 0 else R("S", 128 * h + 1, 128 * h + 128)
+                scan(R("tt", 128 * h + 1, 128 * h + 128), plane(h, j, 0, 127), sg, A.max, A.min, -2.0 ** 90)
+                if j < 5:
+                    tt(ln("D", h), Kp, ln("tt", h), A.subtract)
+                    if RENG == "V":
+                        tt(ln("S", h), ln("tt", h), Kp, A.subtract)
+                    elif RENG == "A":
+                        act(ln("S", h), ln("D", h), AF.Identity, scale=-1.0)
+                    else:
+                        ts(ln("S", h), ln("D", h), -1.0, A.mult)
+                    tt(plane(h, j + 1), plane(h, j + 1), ln("D", h), A.min)
+                else:
+                    tt(ln("dA", h, 256 * t), Kp, ln("tt", h), A.is_lt)
+            dead, eb, om = ln("dA", h, 256 * t), 144 * h, 16 * t + 8 * h
+            scan(ln("c1", h), R("d0"), dead, A.add, A.mult)
+            cp(R("ee", eb + 16, eb + 144, 16), R("c1", 128 * h + 15, 128 * h + 128, 16), "VA")
+            mm([(R(M, 0, 8), R("ones", 0, 128, p=(0, 1)), R("rows", 256, 264, p=(0, 1)))]
+               + [(R(M, 0, 8), R("ee", eb + 16 - il, eb + 144 - il), R("IB", il, 128, 16)) for il in range(16)])
+            ts(R("offm", om, om + 8), R(M, 0, 8), C(12), A.add)
+            send(R("offm", om, om + 8), R("offb", om, om + 8), "ro%d" % (2 * t + h), to, 2200.0)
+            send(dead, ln("dB", h, 256 * t), "rd%d" % (2 * t + h), to, 2500.0)
+            gather(ln("Mb", h), R("xg", 2048 * h, 2048 * h + 2048), R("offm", om, om + 8), alt=FALT)
+            keys("yg", "b%d" % h, h, 1, False)
+            keys("xg", "xa%d" % h, h, 0, False)
+            W = R(M, 384, 512)
+            mm([(W, IB(0), ln("Z", h)), (W, IB(1), ln("Mb", h))])
+            act(ln("ge", h), W, AF.Sign, bias=C(23))
+            mm([(W, R("blk"), ln("ge", h))])
+            act(R("TH", 256 * h, 256 * h + 128), W, AF.Relu, bias=-2.0 ** 90, scale=-2.0 ** 89)
+            act(R("TH", 256 * h + 128, 256 * h + 256), W, AF.Relu, bias=2.0 ** 91, scale=2.0 ** 89)
+            diffs(ln("Mb", h), "ya", h, 768 * (2 + h))
+            keys("xg", "b%d" % h, h, 1, False)
+            P = R("ya%d" % h, 0, 256)
+            mm([(P, R("cc", p=(0, 64)), R("ones", p=(0, 64))), (P, ln("nf", h, 256 * t), R("Prm", 8, 264)),
+                (P, ln("bn", h, 256 * t), R("Prm", 0, 256))], stop=False,
+               wr=[R("ya%d" % h)])
+        cur[0] = 0
+        gather(R("xo"), R("X"), R("offc", 0, 16), alt=FALT)
+        for h in H:
+            W = R("m%d" % h, 384, 512)
+            mm([(W, IB(0), ln("xo", h)), (W, IB(0), ln("Mb", h))])
+            ts(ln("xi", h), W, 0.5, A.mult, C(11), A.subtract)
+        if t < RO - 1:
+            add("V", lambda e: g.vector.tensor_copy(T.X[:].indirect(T.offc[:, 0:16]), T.xi[:]),
+                [R("xi"), R("offc", 0, 16)], [R("X")], vc(256, 3.8))
+            mm([(R("m0", 384, 512), R("ones", 0, 128), ln("dA", h, 256 * t)) for h in H])
+            act(R("junk", 0, 128), R("m0", 384, 512), AF.Identity, bias=1056.0, scale=32.0, acc=R("K32", t + 1, t + 2))
+        else:
+            tt(R("xn"), R("xi"), R("xo"), A.subtract)
+            for q in range(4):
+                fix(q)
+            for q in range(2):
+                dma("SA"[q], T.yx[:, 1024 * q:1024 * q + 1024], T.yxs[:, 1024 * q:1024 * q + 1024], [R("yxs")], [], 4000.0)
+        for h in H:
+            cur[0] = h
+            M, om = "m%d" % h, 16 * t + 8 * h
+            gather(ln("Yb", h), R("yg", 2048 * h, 2048 * h + 2048), R("offb", om, om + 8), alt=FALT)
+            order_sum(R(M, 256, 384), 768 * (2 + h), ln("dB", h, 256 * t), R("TH", 256 * h + 128, 256 * h + 256))
+            diffs(ln("Yb", h), "xa", h, 768 * h)
+            order_sum(R(M, 128, 256), 768 * h, ln("dA", h, 256 * t), R("TH", 256 * h, 256 * h + 128))
+            W = R(M, 384, 512)
+            mm([(W, IB(0), ln("Z", h)), (W, IB(1), ln("Yb", h))])
+            act(ln("Z" if t < RO - 1 else "zf", h), W, AF.Abs, bias=BIAS)
+        if t == RO - 1:
+            dma("S", T.yz[:], T.zf[:], [R("zf")], [], 2000.0)
+        for h in H:
+            cur[0] = h
+            M = "m%d" % h
+            w2 = lambda nm, lo=0, hi=256, st=1: R(nm, 256 * h + lo, 256 * h + hi, st)
+            act(w2("keep"), R(M, 128, 384), AF.Sign, bias=2.0 ** -84)
+            tt(w2("kf"), R(M, 128, 384), w2("TH"), A.is_ge)
+            XA, YA = "xa%d" % h, "ya%d" % h
+            Tt, P, O = R(XA, 0, 256), R(YA, 0, 256), R(XA, 256, 384)
+            kA, kB, fA, fB = w2("keep", 0, 128), w2("keep", 128, 256), w2("kf", 0, 128), w2("kf", 128, 256)
+            tgt = lambda o: [(o, R("ones", 0, 128, p=(0, 1)), R("rows", 0, 256, p=(0, 1))), (o, kA, R("Tri", 8, 264)),
+                             (o, kB, R("Tri", 0, 256)), (o, fB, R("mG", 8, 264)), (o, fA, R("mG", 0, 256))]
+            mm(tgt(Tt)[0 if MODPE else 1:], wr=[R(XA)])
+            if MODPE:
+                T2 = R("b%d" % h, 0, 256)
+                mm(tgt(T2), stop=False, wr=[R("b%d" % h)])
+                act(w2("sg"), Tt, AF.Sign, bias=-7.5)
+                mm([(T2, IB(4), w2("sg"))], start=False)
+                ts(w2("k1"), T2, KM, A.mult)
+            else:
+                ts(w2("k1"), Tt, 7.5, A.add)
+                ts(w2("k2"), w2("k1"), 15, A.bitwise_and)
+                ts(w2("k1"), w2("k2"), KM, A.mult)
+            mm([(P, kA, R("D8", 8, 264)), (P, kB, R("D8", 0, 256)), (P, fA, R("D8", 8, 264)),
+                (P, fB, R("D8", 0, 256))], start=False)
+            mm([(O, R("CD"), R("oneF"))], stop=False, wr=[R(XA)])
+            ts(w2("k2"), w2("k1"), KMASK, A.bitwise_and)
+            lo = lambda s, a=0, b=128, st=1: R("va", 256 * h + 128 * s + a, 256 * h + 128 * s + b, st)
+            hi = lambda s, a=0, b=128, st=1: R(YA, 256 + 128 * s + a, 256 + 128 * s + b, st)
+            tt(lo(0), w2("k2", 0, 128), R(YA, 0, 128), A.add)
+            tt(hi(0), w2("k2", 128, 256), R(YA, 128, 256), A.add)
+            for st in range(4):
+                s, d = st & 1, 1 - (st & 1)
+                for q, dst in ((0, lo), (1, hi)):
+                    tt(dst(d, 0, 128, 2), lo(s, 64 * q, 64 * q + 64), hi(s, 64 * q, 64 * q + 64), A.min)
+                    tt(dst(d, 1, 128, 2), lo(s, 64 * q, 64 * q + 64), hi(s, 64 * q, 64 * q + 64), A.max)
+            tt(ln("mg", h), lo(0), hi(0), A.max)
+            mm([(O, ln("mg", h), R("IF"))], start=False)
+            tt(ln("r1", h), ln("f1", h), O, A.max)
+            ts(ln("r2", h), ln("r1", h), V - 1, A.bitwise_and)
+            if t < RO - 1:
+                ts(ln("nf", h, 256 * (t + 1)), ln("r2", h), -4096.0, A.add)
+            else:
+                cp(ln("nf", h, 256 * (t + 1)), ln("r2", h))
+                mm([(R(M, 0, 128), R("PP"), ln("nf", h, 256 * (t + 1)))])
+                cp(ln("yas", h), R(M, 0, 128), "AV")
+                dma("S", T.ya[:, 128 * h:128 * h + 128], T.yas[:, 128 * h:128 * h + 128], [ln("yas", h)], [], 2000.0)
+    return ops, nsent[0], Q
+
+
+def rank_program(g, core, T, topo):
+    if T.rank_of(core) is None:
+        return
+    ops, nsent, Q = build(g, core, T, topo)
+    order, _ = plan_order(ops)
+    count = {"V": 0, "A": 0, "P": 0, "G": 0}
+    seen = {}
+    bank = {}
+
+    def wait(e, sem, n):
+        if seen.get((e, sem), 0) < n:
+            Q[e].wait_ge(T.sem[sem], n)
+            seen[(e, sem)] = n
+
+    for i in order:
+        o = ops[i]
+        e = o["on"]
+        if e == "N":
+            continue
+        need = list(o["deps"])
+        for b in o["banks"]:
+            need += [j for e2, j in bank.get(b, {}).items() if e2 != e]
+            bank.setdefault(b, {})[e] = i
+        want = {}
+        for d in need:
+            s, n = ops[d]["sem"], ops[d]["cnt"]
+            want[s] = max(want.get(s, 0), n)
+        for s, n in sorted(want.items()):
+            wait(e, s, n)
+        ins = o["fn"](e)
+        if o["sem"] is None:
+            count[e] += 1
+            o["sem"], o["cnt"] = "e" + e, count[e]
+            ins.then_inc(T.sem["e" + e], 1)
+        elif o["sem"] != "-":
+            ins.then_inc(T.sem[o["sem"]], 16)
+    for e in ("V", "A", "P", "G"):
+        wait("G", "e" + e, count[e])
+    wait("G", "sent", nsent)
+    for o in ops:
+        if o["sem"] != "-":
+            wait("G", o["sem"], o["cnt"])

@@ -42,19 +42,22 @@ for _b in PSUM:
 SEMAPHORES = (["eV", "eA", "eP", "eG", "sent"] + ["d%d" % i for i in range(16)]
               + ["%s%d" % (s, i) for s in ("rn", "rd", "ro") for i in range(6)])
 
-CY, PECY, FIX, LAT, GA = 1.04, 0.55, 60.0, 90.0, 1.56
-GSPLIT = 4
+CY, PECY, FIX, LAT, GA = 0.95, 0.48, 50.0, 120.0, 1.56
+GSPLIT = 2
 GX = (("A", "A"), ("A", "A"))
 GY = (("A", "A"), ("A", "A"))
+GX0 = (("A", "V"), ("A", "A"))
 GALT = 0.0
 RENG = "AV"
 DENG = ("A", "AV")
 MODPE = False
-LEAD = 5000.0
-SEED, NOISE = 1, 800.0
+LEAD = 10000.0
+SEED, NOISE = 1, 1300.0
 FALT = 300.0
-PASSES = 350
-SLACK = 2500.0
+LF = 1.35
+SPLITB = False
+PASSES = 700
+SLACK = 1500.0
 
 
 def meets(x, y):
@@ -67,7 +70,10 @@ def brev(x):
     return ((x & 1) << 3) | ((x & 2) << 1) | ((x & 4) >> 1) | ((x & 8) >> 3)
 
 
-def plan_order(ops):
+ORDER = {}
+
+
+def plan_order(ops, memo):
     hist = {}
     for i, o in enumerate(ops):
         deps = set(o["after"])
@@ -154,8 +160,8 @@ def plan_order(ops):
                     ready.append(s)
         return end, on
 
-    best = None
-    for it in range(PASSES):
+    best = memo.get("best")
+    for it in range(0 if best else PASSES):
         end, on = place(pred, succ, pr, False)
         span = max(end[i] + ops[i]["lat"] for i in range(n))
         if best is None or span <= best[0] + SLACK * (1.0 - it / PASSES):
@@ -167,6 +173,7 @@ def plan_order(ops):
             x = (x * 1103515245 + 12345) % 2147483648
             back.append(cur[1][i] + ops[i]["lat"] + NOISE * (x / 2147483648.0))
         pr, _ = place(succ, pred, back, True)
+    memo["best"] = best
     span, end, on = best
     for i, o in enumerate(ops):
         o["on"], o["st"] = on[i], end[i] - o["cost"]
@@ -189,7 +196,8 @@ def build(g, core, T, topo):
         return (ap, (nm, lo, hi, step), len(range(lo, hi, step)), SCRATCH[nm][2] in (BF, U16), nm in PSUM)
 
     def add(eng, fn, r, w, cost, lat=0.0, sem=None, cnt=0, after=(), alt=0.0):
-        ops.append({"eng": eng, "fn": fn, "r": [x[1] for x in r], "w": [x[1] for x in w], "cost": cost, "lat": lat,
+        ops.append({"eng": eng, "fn": fn, "r": [x[1] for x in r], "w": [x[1] for x in w], "cost": cost, "lat": lat * LF,
+                    "ga": any(x[1][0] in ("offx", "offy") for x in r),
                     "sem": sem, "cnt": cnt, "after": list(after), "alt": alt, "half": cur[0]})
         return len(ops) - 1
 
@@ -383,7 +391,7 @@ def build(g, core, T, topo):
     tt(R("Prm", 0, 256), R("tm2", 0, 256), R("mG", 0, 256), A.mult)
     mset(R("tt"), -2.0 ** 90)
     mset(R("ee"), 0.0)
-    mset(R("K32", 0, 1), 135168.0)
+    mset(R("K32", 0, 1), -2.0 ** 23)
     ts(R("junk"), R("ami"), -4096.0, A.add)
     for h in range(2):
         mm([(R("m%d" % h, 0, 128), R("PP"), R("junk", 128 * h, 128 * h + 128))])
@@ -441,9 +449,8 @@ def build(g, core, T, topo):
             mm([(R(M, 0, 128), R("Wblk"), ln("Z", h))])
             cp(ln("si", h), R(M, 0, 128))
             ts(ln("ui", h), ln("si", h), 1023, A.bitwise_and)
-            ts(ln("t5", h), ln("si", h), 31, A.bitwise_and)
             ts(R(M, 128, 256), ln("ui", h), 2.0, A.mult, 33.0, A.add)
-            ts(R(M, 256, 384), ln("t5", h), 8192.0, A.mult, R("K32", t, t + 1), A.add)
+            ts(R(M, 256, 384), R(M, 128, 256), 4096.0, A.mult, R("K32", t, t + 1), A.add)
             offsets(ln("nf", h, 256 * t), "offx", M, 128 * h, h)
         mm([(R("m0", 384, 400), R("Wband", 15 - il, 143 - il), R("Z", il, 256, 16)) for il in range(16)])
         cp(R("ci"), R("m0", 384, 400))
@@ -459,7 +466,7 @@ def build(g, core, T, topo):
                 cp(R("yxs", 512 * q, 512 * q + 512), R(bk), "AV")
         for h in H:
             cur[0] = h
-            items("offx", "xg", h, GX[h])
+            items("offx", "xg", h, GX[h] if t else GX0[h])
             keys("xg", "xa%d" % h, h, 0, True)
             keys("xg", "b%d" % h, h, 1, True)
             offsets(ln("bn", h, 256 * t), "offy", "m%d" % h, 256 + 128 * h, h)
@@ -520,7 +527,7 @@ def build(g, core, T, topo):
             add("V", lambda e: g.vector.tensor_copy(T.X[:].indirect(T.offc[:, 0:16]), T.xi[:]),
                 [R("xi"), R("offc", 0, 16)], [R("X")], vc(256, 3.8))
             mm([(R("m0", 384, 512), R("ones", 0, 128), ln("dA", h, 256 * t)) for h in H])
-            act(R("junk", 0, 128), R("m0", 384, 512), AF.Identity, bias=1056.0, scale=32.0, acc=R("K32", t + 1, t + 2))
+            act(R("junk", 0, 128), R("m0", 384, 512), AF.Identity, bias=-65536.0, scale=32.0, acc=R("K32", t + 1, t + 2))
         else:
             tt(R("xn"), R("xi"), R("xo"), A.subtract)
             for q in range(4):
@@ -543,14 +550,20 @@ def build(g, core, T, topo):
             cur[0] = h
             M = "m%d" % h
             w2 = lambda nm, lo=0, hi=256, st=1: R(nm, 256 * h + lo, 256 * h + hi, st)
-            act(w2("keep"), R(M, 128, 384), AF.Sign, bias=2.0 ** -84)
-            tt(w2("kf"), R(M, 128, 384), w2("TH"), A.is_ge)
+            for a_, b_ in (((128, 256), (0, 128)) if SPLITB else ((0, 256),)):
+                act(w2("keep", a_, b_), R(M, 128 + a_, 128 + b_), AF.Sign, bias=2.0 ** -84)
+                tt(w2("kf", a_, b_), R(M, 128 + a_, 128 + b_), w2("TH", a_, b_), A.is_ge)
             XA, YA = "xa%d" % h, "ya%d" % h
             Tt, P, O = R(XA, 0, 256), R(YA, 0, 256), R(XA, 256, 384)
             kA, kB, fA, fB = w2("keep", 0, 128), w2("keep", 128, 256), w2("kf", 0, 128), w2("kf", 128, 256)
             tgt = lambda o: [(o, R("ones", 0, 128, p=(0, 1)), R("rows", 0, 256, p=(0, 1))), (o, kA, R("Tri", 8, 264)),
                              (o, kB, R("Tri", 0, 256)), (o, fB, R("mG", 8, 264)), (o, fA, R("mG", 0, 256))]
-            mm(tgt(Tt)[0 if MODPE else 1:], wr=[R(XA)])
+            if SPLITB:
+                mm(tgt(Tt)[2:4], stop=False, wr=[R(XA)])
+                mm([(P, kB, R("D8", 0, 256)), (P, fB, R("D8", 0, 256))], start=False, stop=False)
+                mm(tgt(Tt)[1::3], start=False)
+            else:
+                mm(tgt(Tt)[0 if MODPE else 1:], wr=[R(XA)])
             if MODPE:
                 T2 = R("b%d" % h, 0, 256)
                 mm(tgt(T2), stop=False, wr=[R("b%d" % h)])
@@ -562,7 +575,7 @@ def build(g, core, T, topo):
                 ts(w2("k2"), w2("k1"), 15, A.bitwise_and)
                 ts(w2("k1"), w2("k2"), KM, A.mult)
             mm([(P, kA, R("D8", 8, 264)), (P, kB, R("D8", 0, 256)), (P, fA, R("D8", 8, 264)),
-                (P, fB, R("D8", 0, 256))], start=False)
+                (P, fB, R("D8", 0, 256))][::2 if SPLITB else 1], start=False)
             mm([(O, R("CD"), R("oneF"))], stop=False, wr=[R(XA)])
             ts(w2("k2"), w2("k1"), KMASK, A.bitwise_and)
             lo = lambda s, a=0, b=128, st=1: R("va", 256 * h + 128 * s + a, 256 * h + 128 * s + b, st)
@@ -592,7 +605,7 @@ def rank_program(g, core, T, topo):
     if T.rank_of(core) is None:
         return
     ops, nsent, Q = build(g, core, T, topo)
-    order, _ = plan_order(ops)
+    order, _ = plan_order(ops, ORDER)
     count = {"V": 0, "A": 0, "P": 0, "G": 0}
     seen = {}
     bank = {}

@@ -21,7 +21,7 @@ SCRATCH = {
     "tt": _sb(256, F32), "S": _sb(256, F32), "pen": _sb(256, BF),
     "c1": _sb(512, BF), "ee": _sb(576, BF), "sg": _sb(512, BF), "xo": _sb(256, BF),
     "Mb": _sb(256, BF), "Yb": _sb(256, BF), "ge": _sb(256, BF), "TH": _sb(512, BF),
-    "CD": _sb(128, F32), "oneF": _sb(128, F32),
+    "fin": ("sbuf", [128, 32, 16], F32), "CD": _sb(128, F32), "oneF": _sb(128, F32),
     "DS": _sb(4 * 768, BF), "keep": _sb(512, BF), "kf": _sb(512, BF),
     "k1": _sb(512, I32), "k2": _sb(512, I32), "va": _sb(512, F32), "vb": _sb(512, F32), "mg": _sb(256, F32),
     "r1": _sb(256, I32), "r2": _sb(256, I32), "yas": _sb(256, F32),
@@ -42,7 +42,7 @@ for _b in PSUM:
 SEMAPHORES = (["eV", "eA", "eP", "eG", "sent"] + ["d%d" % i for i in range(16)]
               + ["%s%d" % (s, i) for s in ("rn", "rd", "ro") for i in range(6)])
 
-CY, PECY, FIX, LAT, GA = 0.95, 0.48, 50.0, 120.0, 1.56
+CY, PECY, FIX, LAT, GA = 0.95, 0.48, 60.0, 115.0, 1.56
 GSPLIT = 2
 GX = (("A", "A"), ("A", "A"))
 GY = (("A", "A"), ("A", "A"))
@@ -50,14 +50,15 @@ GX0 = (("A", "V"), ("A", "A"))
 GALT = 0.0
 RENG = "AV"
 DENG = ("A", "AV")
-MODPE = False
+MODPE = True
 LEAD = 10000.0
-SEED, NOISE = 1, 1300.0
+SEED, NOISE = 7, 2500.0
 FALT = 300.0
 LF = 1.35
 SPLITB = False
-PASSES = 700
-SLACK = 1500.0
+PASSES = 2800
+SLACK = 700.0
+WIN, WARM = 12000.0, 100
 
 
 def meets(x, y):
@@ -169,9 +170,12 @@ def plan_order(ops, memo):
             if best is None or span < best[0]:
                 best = cur
         back = []
+        x = (x * 1103515245 + 12345) % 2147483648
+        w0 = (x / 2147483648.0) * (cur[0] + WIN) - WIN
         for i in range(n):
             x = (x * 1103515245 + 12345) % 2147483648
-            back.append(cur[1][i] + ops[i]["lat"] + NOISE * (x / 2147483648.0))
+            z = NOISE * (x / 2147483648.0 - 0.5) if it < WARM or w0 <= cur[1][i] <= w0 + WIN else 0.0
+            back.append(cur[1][i] + ops[i]["lat"] + z)
         pr, _ = place(succ, pred, back, True)
     memo["best"] = best
     span, end, on = best
@@ -313,8 +317,10 @@ def build(g, core, T, topo):
     iota(R("lin"), [[1, 256]])
     iota(R("idq"), [[1, 48], [0, 16]])
     for q in range(4):
-        iota(R("srev", 64 * q, 64 * q + 64), [[4, 2], [8, 2], [0, 16]], (q >> 1) + 2 * (q & 1))
-    iota(R("gl"), [[0, 16], [1, 16]])
+        iota(R("srev", 32 * q, 32 * q + 32), [[4, 2], [8, 2], [0, 8]], (q >> 1) + 2 * (q & 1))
+    iota(R("gl", 0, 128), [[0, 8], [1, 16]])
+    iota(R("gl", 128, 256), [[0, 16], [1, 8]])
+    iota(R("srev", 128, 256), [[1, 16], [0, 8]])
     iota(R("c32", 0, 16), [[512, 16]])
     iota(R("c32", 16, 32), [[0, 4], [512, 4]])
     ts(PI(1), PI(0), 15, A.bitwise_and)
@@ -356,7 +362,7 @@ def build(g, core, T, topo):
     ts(R("Wband"), R("lin", 0, 144), C(15), A.is_equal, C(18), A.mult)
     ts(R("diag", 0, 16), R("gl", 0, 16), C(1), A.is_equal)
     ts(R("seg"), R("gl", 0, 128), 0.0, A.is_equal, -2.0 ** 90, A.mult)
-    tt(R("tmp", 0, 16), R("diag", 0, 16), R("srev", 0, 256, 16), A.mult)
+    tt(R("tmp", 0, 16), R("diag", 0, 16), R("srev", 0, 128, 8), A.mult)
     add("V", lambda e: g.vector.tensor_reduce(T.col[:, 19:20], T.tmp[:, 0:16], AxisListType.X, A.add),
         [R("tmp", 0, 16)], [C(19)], vc(16))
     ts(C(20), C(19), C(14), A.add)
@@ -369,26 +375,24 @@ def build(g, core, T, topo):
     ts(R("CD"), R("IF"), C(22), A.mult)
     mset(R("oneF"), 1.0)
     mset(R("d0", 0, 1), 0.0)
-    tt(R("d0", 1, 16), R("srev", 16, 256, 16), R("srev", 0, 240, 16), A.subtract)
+    tt(R("d0", 1, 16), R("srev", 8, 128, 8), R("srev", 0, 120, 8), A.subtract)
     for w_ in (16, 32, 64):
         cp(R("d0", w_, 2 * w_), R("d0", 0, w_))
     mset(R("ones"), 1.0)
     mset(R("cc", p=(0, 32)), -2.0 ** 19)
     mset(R("cc", p=(32, 64)), 384.0)
-    mset(R("rows", 0, 256), -0.5)
     ts(R("rows", 256, 272), R("lin", 0, 16), 256.0, A.mult)
     ts(R("c32"), R("c32"), C(13), A.add)
-    for nm in ("mG", "Tri", "D8", "Prm"):
-        mset(R(nm, 256, 264), 0.0)
-    ts(R("mG", 0, 256), R("gl"), C(16), A.is_equal)
-    ts(R("tmp", 0, 256), R("srev"), C(17), A.is_equal, 8192.0, A.mult)
-    tt(R("D8", 0, 256), R("tmp", 0, 256), R("mG", 0, 256), A.mult)
-    ts(R("tm2", 0, 256), R("srev"), C(17), A.is_gt, 0.5, A.mult)
-    ts(R("tmp", 0, 256), R("tmp", 0, 256), C(1), A.mult, -0.5 / 8192, A.mult)
-    tt(R("tmp", 0, 256), R("tmp", 0, 256), R("tm2", 0, 256), A.add)
-    tt(R("Tri", 0, 256), R("tmp", 0, 256), R("mG", 0, 256), A.mult)
-    ts(R("tm2", 0, 256), R("idq", 0, 256), C(1), A.is_equal)
-    tt(R("Prm", 0, 256), R("tm2", 0, 256), R("mG", 0, 256), A.mult)
+    c8 = lambda nm: R(nm, 0, 128)
+    ts(c8("mG"), R("gl", 128, 256), C(2), A.is_equal)
+    ts(c8("tmp"), c8("srev"), C(17), A.is_equal, 8192.0, A.mult)
+    tt(c8("D8"), c8("tmp"), c8("mG"), A.mult)
+    ts(c8("tm2"), c8("srev"), C(17), A.is_gt, 0.5, A.mult)
+    ts(c8("tmp"), c8("tmp"), C(1), A.mult, -0.5 / 8192, A.mult)
+    tt(c8("tmp"), c8("tmp"), c8("tm2"), A.add)
+    tt(c8("Tri"), c8("tmp"), c8("mG"), A.mult)
+    ts(c8("tm2"), R("srev", 128, 256), C(1), A.is_equal)
+    tt(c8("Prm"), c8("tm2"), c8("mG"), A.mult)
     mset(R("tt"), -2.0 ** 90)
     mset(R("ee"), 0.0)
     mset(R("K32", 0, 1), -2.0 ** 23)
@@ -514,8 +518,9 @@ def build(g, core, T, topo):
             diffs(ln("Mb", h), "ya", h, 768 * (2 + h))
             keys("xg", "b%d" % h, h, 1, False)
             P = R("ya%d" % h, 0, 256)
-            mm([(P, R("cc", p=(0, 64)), R("ones", p=(0, 64))), (P, ln("nf", h, 256 * t), R("Prm", 8, 264)),
-                (P, ln("bn", h, 256 * t), R("Prm", 0, 256))], stop=False,
+            mm([(P, R("cc", p=(0, 64)), R("ones", p=(0, 64))),
+                (R("ya%d" % h, 0, 256, 2), ln("nf", h, 256 * t), c8("Prm")),
+                (R("ya%d" % h, 1, 256, 2), ln("bn", h, 256 * t), c8("Prm"))], stop=False,
                wr=[R("ya%d" % h)])
         cur[0] = 0
         gather(R("xo"), R("X"), R("offc", 0, 16), alt=FALT)
@@ -529,8 +534,9 @@ def build(g, core, T, topo):
             mm([(R("m0", 384, 512), R("ones", 0, 128), ln("dA", h, 256 * t)) for h in H])
             act(R("junk", 0, 128), R("m0", 384, 512), AF.Identity, bias=-65536.0, scale=32.0, acc=R("K32", t + 1, t + 2))
         else:
-            tt(R("xn"), R("xi"), R("xo"), A.subtract)
             for q in range(4):
+                if q % 2 == 0:
+                    tt(ln("xn", q // 2), ln("xi", q // 2), ln("xo", q // 2), A.subtract)
                 fix(q)
             for q in range(2):
                 dma("SA"[q], T.yx[:, 1024 * q:1024 * q + 1024], T.yxs[:, 1024 * q:1024 * q + 1024], [R("yxs")], [], 4000.0)
@@ -556,26 +562,21 @@ def build(g, core, T, topo):
             XA, YA = "xa%d" % h, "ya%d" % h
             Tt, P, O = R(XA, 0, 256), R(YA, 0, 256), R(XA, 256, 384)
             kA, kB, fA, fB = w2("keep", 0, 128), w2("keep", 128, 256), w2("kf", 0, 128), w2("kf", 128, 256)
-            tgt = lambda o: [(o, R("ones", 0, 128, p=(0, 1)), R("rows", 0, 256, p=(0, 1))), (o, kA, R("Tri", 8, 264)),
-                             (o, kB, R("Tri", 0, 256)), (o, fB, R("mG", 8, 264)), (o, fA, R("mG", 0, 256))]
-            if SPLITB:
-                mm(tgt(Tt)[2:4], stop=False, wr=[R(XA)])
-                mm([(P, kB, R("D8", 0, 256)), (P, fB, R("D8", 0, 256))], start=False, stop=False)
-                mm(tgt(Tt)[1::3], start=False)
-            else:
-                mm(tgt(Tt)[0 if MODPE else 1:], wr=[R(XA)])
+            tgt = lambda b: [(R(b, 0, 256, 2), kA, c8("Tri")), (R(b, 1, 256, 2), kB, c8("Tri")),
+                             (R(b, 0, 256, 2), fB, c8("mG")), (R(b, 1, 256, 2), fA, c8("mG"))]
+            mm(tgt(XA), wr=[R(XA)])
             if MODPE:
                 T2 = R("b%d" % h, 0, 256)
-                mm(tgt(T2), stop=False, wr=[R("b%d" % h)])
-                act(w2("sg"), Tt, AF.Sign, bias=-7.5)
+                mm(tgt("b%d" % h), stop=False, wr=[R("b%d" % h)])
+                act(w2("sg"), Tt, AF.Sign, bias=-8.0)
                 mm([(T2, IB(4), w2("sg"))], start=False)
-                ts(w2("k1"), T2, KM, A.mult)
+                ts(w2("k1"), T2, -0.5, A.add, KM, A.mult)
             else:
                 ts(w2("k1"), Tt, 7.5, A.add)
                 ts(w2("k2"), w2("k1"), 15, A.bitwise_and)
                 ts(w2("k1"), w2("k2"), KM, A.mult)
-            mm([(P, kA, R("D8", 8, 264)), (P, kB, R("D8", 0, 256)), (P, fA, R("D8", 8, 264)),
-                (P, fB, R("D8", 0, 256))][::2 if SPLITB else 1], start=False)
+            mm([(R(YA, 0, 256, 2), kA, c8("D8")), (R(YA, 1, 256, 2), kB, c8("D8")), (R(YA, 0, 256, 2), fA, c8("D8")),
+                (R(YA, 1, 256, 2), fB, c8("D8"))], start=False, wr=[P])
             mm([(O, R("CD"), R("oneF"))], stop=False, wr=[R(XA)])
             ts(w2("k2"), w2("k1"), KMASK, A.bitwise_and)
             lo = lambda s, a=0, b=128, st=1: R("va", 256 * h + 128 * s + a, 256 * h + 128 * s + b, st)
@@ -585,9 +586,13 @@ def build(g, core, T, topo):
             for st in range(4):
                 s, d = st & 1, 1 - (st & 1)
                 for q, dst in ((0, lo), (1, hi)):
-                    tt(dst(d, 0, 128, 2), lo(s, 64 * q, 64 * q + 64), hi(s, 64 * q, 64 * q + 64), A.min)
-                    tt(dst(d, 1, 128, 2), lo(s, 64 * q, 64 * q + 64), hi(s, 64 * q, 64 * q + 64), A.max)
-            tt(ln("mg", h), lo(0), hi(0), A.max)
+                    for b3, op in ((0, A.min), (1, A.max)):
+                        r0 = 16 * h + 8 * q
+                        o = dst(d, b3, 128, 2) if st < 3 else (T.fin[:, r0:r0 + 8, b3:16:2],
+                                                               ("fin", 16 * r0 + b3, 16 * r0 + 128, 2), 64, False, False)
+                        tt(o, lo(s, 64 * q, 64 * q + 64), hi(s, 64 * q, 64 * q + 64), op)
+            fin = lambda L_: (T.fin[:, 16 * h + L_:16 * h + 16:2, :], ("fin", 256 * h, 256 * h + 256, 1), 128, False, False)
+            tt(ln("mg", h), fin(0), fin(1), A.max)
             mm([(O, ln("mg", h), R("IF"))], start=False)
             tt(ln("r1", h), ln("f1", h), O, A.max)
             ts(ln("r2", h), ln("r1", h), V - 1, A.bitwise_and)

@@ -14,24 +14,25 @@ SCRATCH = {
     "ami": _sb(256, I32), "wti": _sb(4, I32), "Z": _sb(256, BF), "Zb": _sb(256, BF), "zf": _sb(256, F32),
     "nf": _sb(4 * 256, F32), "bn": _sb(3 * 256, F32), "dA": _sb(3 * 256, BF), "dB": _sb(3 * 256, BF),
     "offx": _sb(256, U16), "offy": _sb(256, U16), "offm": _sb(48, U16), "offb": _sb(48, U16),
-    "offc": _sb(32, U16), "D": _sb(256, F32),
-    "si": _sb(256, I32), "ui": _sb(256, I32), "t5": _sb(256, I32),
+    "offc": _sb(32, U16), "D": _sb(256, BF), "q0": _sb(256, BF), "Kb": _sb(128, BF), "Kp": _sb(288, F32),
     "p1": _sb(512, F32), "p2": _sb(512, I32), "p3": _sb(512, I32),
     "f1": _sb(256, I32), "f2": _sb(256, I32), "fb": _sb(256, F32),
-    "tt": _sb(256, F32), "S": _sb(256, F32), "pen": _sb(256, BF),
+    "tt": _sb(256, F32),
     "c1": _sb(512, BF), "ee": _sb(576, BF), "sg": _sb(512, BF), "xo": _sb(256, BF),
     "Mb": _sb(256, BF), "Yb": _sb(256, BF), "ge": _sb(256, BF), "TH": _sb(512, BF),
-    "fin": ("sbuf", [128, 32, 16], F32), "CD": _sb(128, F32), "oneF": _sb(128, F32),
+    "fin": ("sbuf", [128, 32, 16], F32), "CD": _sb(128, BF), "K16": _sb(4, F32),
     "DS": _sb(4 * 768, BF), "keep": _sb(512, BF), "kf": _sb(512, BF),
     "k1": _sb(512, I32), "k2": _sb(512, I32), "va": _sb(512, F32), "vb": _sb(512, F32), "mg": _sb(256, F32),
-    "r1": _sb(256, I32), "r2": _sb(256, I32), "yas": _sb(256, F32),
+    "yas": _sb(256, F32),
     "ci": _sb(16, I32), "cj": _sb(16, I32), "cf": _sb(16, F32), "xs": _sb(256, F32), "xi": _sb(256, I32),
-    "xn": _sb(256, F32), "junk": _sb(256, F32), "K32": _sb(4, F32),
+    "xn": _sb(256, F32), "junk": _sb(256, F32),
     "lin": _sb(256, F32), "idq": _sb(768, F32), "srev": _sb(256, F32), "gl": _sb(256, F32), "cm16": _sb(128, F32),
-    "pi": _sb(16, I32), "col": _sb(32, F32), "c32": _sb(32, F32),
+    "pi": _sb(16, I32), "col": _sb(48, F32), "c32": _sb(32, F32), "I165": _sb(128, F32),
+    "W32": _sb(128, BF), "s16": _sb(128, BF), "Fk": _sb(128, BF), "kb": _sb(128, F32), "blkn": _sb(128, BF),
+    "mGn": _sb(128, BF),
     "IB": _sb(10 * 128, BF), "IF": _sb(128, F32), "PP": _sb(128, F32), "Wrep": _sb(768, BF), "Wk": _sb(48, BF),
     "blk": _sb(128, BF), "Wblk": _sb(128, BF), "Wband": _sb(144, BF), "diag": _sb(128, BF), "seg": _sb(128, BF),
-    "d0": _sb(128, BF), "ones": _sb(256, BF), "cc": _sb(128, BF), "rows": _sb(272, BF),
+    "d0": _sb(128, BF), "ones": _sb(256, BF), "cc": _sb(384, BF), "rows": _sb(272, BF),
     "mG": _sb(264, BF), "Tri": _sb(264, BF), "D16": _sb(264, BF), "D8": _sb(264, BF), "Prm": _sb(264, F32),
     "tmp": _sb(264, F32), "tm2": _sb(264, F32),
 }
@@ -44,19 +45,20 @@ SEMAPHORES = (["eV", "eA", "eP", "eG", "sent"] + ["d%d" % i for i in range(16)]
 
 CY, PECY, FIX, LAT, GA = 0.95, 0.48, 60.0, 115.0, 1.56
 GSPLIT = 2
-GX = (("A", "A"), ("A", "A"))
+GX = (("A", "AV"), ("A", "AV"))
 GY = (("A", "A"), ("A", "A"))
-GX0 = (("A", "V"), ("A", "A"))
-GALT = 0.0
+GX0 = (("A", "V"), ("A", "AV"))
+GALT = 600.0
 RENG = "AV"
-DENG = ("A", "AV")
-MODPE = True
-LEAD = 10000.0
+DENG = ("AV", "AV")
+XT = 1
+LEAD = 3000.0
 SEED, NOISE = 7, 2500.0
 FALT = 300.0
 LF = 1.35
-SPLITB = False
-PASSES = 2800
+SPLITB = True
+PASSES = 80
+MOVES, TEMP, SOFT = 60000, 500.0, 1
 SLACK = 700.0
 WIN, WARM = 12000.0, 100
 
@@ -82,10 +84,12 @@ def plan_order(ops, memo):
             for (j, w, y) in hist.get(x[0], []):
                 if w and meets(x[1:], y):
                     deps.add(j)
+        raw = set(deps)
         for x in o["w"]:
             for (j, w, y) in hist.get(x[0], []):
                 if meets(x[1:], y):
                     deps.add(j)
+        o["soft"] = set(j for j in deps - raw if SOFT and ops[j]["eng"] == "P" and o["eng"] == "P" and (o["cont"] or SOFT > 1))
         for x in o["w"]:
             hist[x[0]] = [e for e in hist.get(x[0], [])
                           if not (x[1] <= e[2][0] and e[2][1] <= x[2] and (x[3] == 1 or x[1:] == e[2]))]
@@ -177,11 +181,118 @@ def plan_order(ops, memo):
             z = NOISE * (x / 2147483648.0 - 0.5) if it < WARM or w0 <= cur[1][i] <= w0 + WIN else 0.0
             back.append(cur[1][i] + ops[i]["lat"] + z)
         pr, _ = place(succ, pred, back, True)
+    if "best" not in memo:
+        span, end, on = best
+        order = sorted(range(n), key=lambda j: (end[j] - ops[j]["cost"], j))
+        best = refine(ops, order, list(on), x)
     memo["best"] = best
-    span, end, on = best
+    span, end, on, order = best
     for i, o in enumerate(ops):
         o["on"], o["st"] = on[i], end[i] - o["cost"]
-    return sorted(range(n), key=lambda j: (ops[j]["st"], j)), span
+    return order, span
+
+
+def refine(ops, order, on, x):
+    n = len(ops)
+    eid = {e: k for k, e in enumerate("VAPGSN")}
+    bid = {b: k for k, b in enumerate(PSUM)}
+    cost = [o["cost"] for o in ops]
+    lat = [o["lat"] + LAT for o in ops]
+    hard = [[d for d in o["deps"] if d not in o["soft"]] for o in ops]
+    soft = [list(o["soft"]) for o in ops]
+    deps = [set(o["deps"]) for o in ops]
+    banks = [[3 * bid[b] for b in o["banks"]] for o in ops]
+    engs = [[eid[e] for e in o["eng"]] for o in ops]
+    on = [eid[e] for e in on]
+    others = ((1, 2), (0, 2), (0, 1))
+
+    def run(order, on):
+        end, why, held = [0.0] * (n + 1), [n] * n, [False] * n
+        end[n] = -1e9
+        fin = [0.0] * n
+        last, bl = [n] * 6, [n] * (3 * len(PSUM))
+        top, ti = 0.0, 0
+        for i in order:
+            e = on[i]
+            t, p, q = 0.0, n, False
+            for d in hard[i]:
+                if fin[d] > t:
+                    t, p = fin[d], d
+            for d in soft[i]:
+                v = end[d] if on[d] == e else fin[d]
+                if v > t:
+                    t, p = v, d
+            for b in banks[i]:
+                for e2 in others[e]:
+                    d = bl[b + e2]
+                    if end[d] + LAT > t:
+                        t, p, q = end[d] + LAT, d, True
+                bl[b + e] = i
+            if e < 5:
+                d = last[e]
+                if end[d] > t:
+                    t, p, q = end[d], d, True
+                last[e] = i
+            t += cost[i]
+            end[i], why[i], held[i] = t, p, q
+            t += lat[i]
+            fin[i] = t
+            if t > top:
+                top, ti = t, i
+        path, i = [], ti
+        while i != n:
+            if held[i]:
+                path.append(i)
+            i = why[i]
+        return top - LAT, end, why, path
+
+    cur = run(order, on)
+    best = (cur[0], cur[1], on, order)
+    for it in range(MOVES):
+        x = (x * 1103515245 + 12345) % 2147483648
+        i = cur[3][(x >> 8) % len(cur[3])]
+        p = cur[2][i]
+        x = (x * 1103515245 + 12345) % 2147483648
+        kind = (x >> 8) % 8
+        on2, new = on, order
+        if kind == 0 and (len(engs[i]) > 1 or len(engs[p]) > 1):
+            j = i if len(engs[i]) > 1 and (len(engs[p]) == 1 or x & 64) else p
+            on2 = list(on)
+            on2[j] = engs[j][0] if on[j] != engs[j][0] else engs[j][1]
+        else:
+            a, b = order.index(p), order.index(i)
+            x = (x * 1103515245 + 12345) % 2147483648
+            far = ((x >> 8) % 24) if kind > 4 else 0
+            if kind & 1:
+                a = max(0, a - far)
+                mid = order[a:b + 1]
+                take = {i}
+                need = set(deps[i])
+                for j in reversed(mid[:-1]):
+                    if j in need:
+                        take.add(j)
+                        need |= deps[j]
+                if p in take:
+                    continue
+                new = order[:a] + [j for j in mid if j in take] + [j for j in mid if j not in take] + order[b + 1:]
+            else:
+                b = min(n - 1, b + far)
+                mid = order[a:b + 1]
+                take = {p}
+                for j in mid[1:]:
+                    if deps[j] & take:
+                        take.add(j)
+                if i in take:
+                    continue
+                new = order[:a] + [j for j in mid if j not in take] + [j for j in mid if j in take] + order[b + 1:]
+        res = run(new, on2)
+        x = (x * 1103515245 + 12345) % 2147483648
+        if res[0] <= cur[0] + TEMP * (1.0 - it / MOVES) * (x / 2147483648.0) ** 2:
+            end = res[1]
+            order, on, cur = sorted(new, key=lambda j: end[j] - cost[j]), on2, res
+            if res[0] < best[0]:
+                best = (res[0], end, on, order)
+    return best[0], best[1], ["VAPGSN"[e] for e in best[2]], best[3]
 
 
 def build(g, core, T, topo):
@@ -199,8 +310,8 @@ def build(g, core, T, topo):
         ap = t[:, lo:hi:step] if p is None else t[p[0]:p[1], lo:hi:step]
         return (ap, (nm, lo, hi, step), len(range(lo, hi, step)), SCRATCH[nm][2] in (BF, U16), nm in PSUM)
 
-    def add(eng, fn, r, w, cost, lat=0.0, sem=None, cnt=0, after=(), alt=0.0):
-        ops.append({"eng": eng, "fn": fn, "r": [x[1] for x in r], "w": [x[1] for x in w], "cost": cost, "lat": lat * LF,
+    def add(eng, fn, r, w, cost, lat=0.0, sem=None, cnt=0, after=(), alt=0.0, cont=False):
+        ops.append({"eng": eng, "cont": cont, "fn": fn, "r": [x[1] for x in r], "w": [x[1] for x in w], "cost": cost, "lat": lat * LF,
                     "ga": any(x[1][0] in ("offx", "offy") for x in r),
                     "sem": sem, "cnt": cnt, "after": list(after), "alt": alt, "half": cur[0]})
         return len(ops) - 1
@@ -267,7 +378,8 @@ def build(g, core, T, topo):
                 ins = g.tensor.matmul(o[0], l[0], r[0], start and k == 0, stop and k == len(lst) - 1)
             return ins
         cost = sum(max(64, r[2]) * (1 if r[3] else 4) * PECY for (o, l, r) in lst) + 40
-        return add("P", fn, [x[1] for x in lst] + [x[2] for x in lst], wr or [x[0] for x in lst], cost, after=after)
+        return add("P", fn, [x[1] for x in lst] + [x[2] for x in lst], wr or [x[0] for x in lst], cost, after=after,
+                   cont=not start)
 
     def relu(o, i):
         def fn(e):
@@ -330,7 +442,9 @@ def build(g, core, T, topo):
     ts(PI(4), PI(3), 5, A.arith_shift_right)
     cp(C(3), PI(4))
     ts(C(4), C(3), -3.0, A.mult, C(1), A.add)
-    ts(C(5), C(3), 8.0, A.mult, C(2), A.add)
+    ts(PI(7), PI(4), 1, A.arith_shift_right)
+    ts(C(26), PI(7), -40.0, A.mult, C(2), A.add)
+    ts(C(5), C(3), 24.0, A.mult, C(26), A.add)
     ts(C(6), C(4), 0.0, A.is_equal, -65535.0, A.mult)
     ts(C(7), C(4), 1.0, A.is_equal, -255.0, A.mult)
     ts(C(8), C(6), C(7), A.add, -1.0, A.add)
@@ -349,11 +463,12 @@ def build(g, core, T, topo):
     cp(C(18), R("wti", 0, 1))
     ts(R("IF"), R("lin", 0, 128), C(0), A.is_equal)
     ts(IB(0), R("lin", 0, 128), C(0), A.is_equal)
-    for j, c in ((1, -1.0), (2, -2.0 ** 86), (3, 2.0 ** -10), (4, -8.0)):
+    for j, c in ((1, -1.0), (2, -2.0 ** 86), (3, 2.0 ** -10), (4, -8.0), (5, -1.0 / 32), (6, -32.0), (7, -4096.0)):
         ts(IB(j), IB(0), c, A.mult)
     ts(R("Wk"), R("lin", 0, 48), C(5), A.is_equal, C(8), A.mult)
     for j in range(6):
-        ts(R("Wk", 8 * j, 8 * j + 8), R("Wk", 8 * j, 8 * j + 8), -2.0 ** (50 - 26 * j), A.mult)
+        c = 24 * (j & 1) + 8 * (j >> 1)
+        ts(R("Wk", c, c + 8), R("Wk", c, c + 8), -2.0 ** (50 - 26 * j), A.mult)
     add("V", lambda e: g.vector.tensor_reduce(T.col[:, 25:26], T.Wk[:], AxisListType.X, A.add, negate=True),
         [R("Wk")], [C(25)], vc(48))
     ts(R("Wrep"), R("idq"), C(5), A.is_equal, C(25), A.mult)
@@ -367,49 +482,65 @@ def build(g, core, T, topo):
         [R("tmp", 0, 16)], [C(19)], vc(16))
     ts(C(20), C(19), C(14), A.add)
     ts(R("PP"), R("lin", 0, 128), C(20), A.is_equal)
-    ts(C(21), C(19), 1184.0, A.mult)
+    ts(R("W32"), R("Wblk"), 32.0, A.mult)
+    ts(R("blkn"), R("blk"), -2.0 ** 14, A.mult)
+    ts(C(21), C(19), -15.5, A.add, 2.0 ** 15, A.mult)
+    ts(IB(8), IB(0), C(21), A.mult)
+    cp(R("kb", 0, 16), R("srev", 0, 128, 8))
+    for w_ in (16, 32, 64):
+        cp(R("kb", w_, 2 * w_), R("kb", 0, w_))
+    ts(C(27), C(0), 1.0, A.is_equal, 1024.0, A.mult)
+    ts(C(28), C(0), 2.0, A.is_equal, 160.0, A.mult)
+    tt(C(29), C(27), C(28), A.add)
+    ts(C(30), C(0), 0.0, A.is_equal, 3 * 2.0 ** 21, A.mult)
+    ts(R("Fk"), R("kb"), C(29), A.mult, C(30), A.add)
     KM, KMASK = float(0x1111 << 12), (1 << 24) | (1 << 21) | (1 << 18) | (1 << 15)
-    ts(PI(5), C(19), KM, A.mult)
-    ts(PI(6), PI(5), KMASK, A.bitwise_and)
-    ts(C(22), PI(6), -1.0, A.mult, 2.0 ** 24 - 8192.0, A.add)
-    ts(R("CD"), R("IF"), C(22), A.mult)
-    mset(R("oneF"), 1.0)
+    ts(R("k1", 0, 128), R("kb"), KM, A.mult)
+    ts(C(31), C(0), 0.0, A.is_equal, -1.0, A.mult)
+    ts(C(32), C(0), 1.0, A.is_equal, -1.0, A.mult)
+    for j, (mk, c) in enumerate(((KMASK - (1 << 15), -2.0 ** 24), (1 << 15, 16384.0))):
+        ts(R("k2", 128 * j, 128 * j + 128), R("k1", 0, 128), mk, A.bitwise_and)
+        ts(R("va", 128 * j, 128 * j + 128), R("k2", 128 * j, 128 * j + 128), c, A.add, C(31 + j), A.mult)
+    tt(R("CD"), R("va", 0, 128), R("va", 128, 256), A.add)
     mset(R("d0", 0, 1), 0.0)
     tt(R("d0", 1, 16), R("srev", 8, 128, 8), R("srev", 0, 120, 8), A.subtract)
     for w_ in (16, 32, 64):
         cp(R("d0", w_, 2 * w_), R("d0", 0, w_))
     mset(R("ones"), 1.0)
-    mset(R("cc", p=(0, 32)), -2.0 ** 19)
-    mset(R("cc", p=(32, 64)), 384.0)
+    mset(R("cc", 0, 128, p=(0, 32)), -2.0 ** 19)
+    mset(R("cc", 0, 128, p=(32, 64)), 256.0)
+    mset(R("cc", 256, 384, p=(0, 32)), 6144.0)
+    mset(R("K16", 0, 1), -2.0 ** 22 - 0.5)
     ts(R("rows", 256, 272), R("lin", 0, 16), 256.0, A.mult)
     ts(R("c32"), R("c32"), C(13), A.add)
     c8 = lambda nm: R(nm, 0, 128)
     ts(c8("mG"), R("gl", 128, 256), C(2), A.is_equal)
-    ts(c8("tmp"), c8("srev"), C(17), A.is_equal, 8192.0, A.mult)
+    ts(c8("tmp"), c8("srev"), C(17), A.is_equal, 4096.0, A.mult)
     tt(c8("D8"), c8("tmp"), c8("mG"), A.mult)
     ts(c8("tm2"), c8("srev"), C(17), A.is_gt, 0.5, A.mult)
-    ts(c8("tmp"), c8("tmp"), C(1), A.mult, -0.5 / 8192, A.mult)
+    ts(c8("tmp"), c8("tmp"), C(1), A.mult, -0.5 / 4096, A.mult)
     tt(c8("tmp"), c8("tmp"), c8("tm2"), A.add)
     tt(c8("Tri"), c8("tmp"), c8("mG"), A.mult)
     ts(c8("tm2"), R("srev", 128, 256), C(1), A.is_equal)
     tt(c8("Prm"), c8("tm2"), c8("mG"), A.mult)
     mset(R("tt"), -2.0 ** 90)
     mset(R("ee"), 0.0)
-    mset(R("K32", 0, 1), -2.0 ** 23)
-    ts(R("junk"), R("ami"), -4096.0, A.add)
+    mset(R("Kp", 15, 288, 144), 0.0)
+    cp(R("junk"), R("ami"))
     for h in range(2):
         mm([(R("m%d" % h, 0, 128), R("PP"), R("junk", 128 * h, 128 * h + 128))])
         cp(R("nf", 128 * h, 128 * h + 128), R("m%d" % h, 0, 128), "AV")
+    ONE = R("ones", 0, 128)
+    const = lambda out, j: (out, R("cc", 128 * j, 128 * j + 128, p=(0, 32)), R("ones", 0, out[2], p=(0, 32)))
 
     def plane(h, j, lo=0, hi=128):
-        if j < 4:
-            return R("xa%d" % h, 128 * j + lo, 128 * j + hi)
-        return R("b%d" % h, 128 * (j - 4) + lo, 128 * (j - 4) + hi)
+        return R(("xa%d", "b%d")[j & 1] % h, 128 * (j >> 1) + lo, 128 * (j >> 1) + hi)
 
-    def offsets(src, off, M, tmp, h):
+    def offsets(src, off, M, c, tmp, h, t):
+        ts(c, src, 16.5, A.mult, R("K16", t, t + 1), A.add)
         tt(R("p1", tmp, tmp + 128), src, R(M, 128, 256), A.mult)
-        tt(R("p2", tmp, tmp + 128), R("p1", tmp, tmp + 128), R(M, 256, 384), A.add)
-        ts(R("p3", tmp, tmp + 128), R("p2", tmp, tmp + 128), 5, A.arith_shift_right, V - 1, A.bitwise_and)
+        tt(R("p2", tmp, tmp + 128), R("p1", tmp, tmp + 128), c, A.add)
+        ts(R("p3", tmp, tmp + 128), R("p2", tmp, tmp + 128), 4, A.arith_shift_right, V - 1, A.bitwise_and)
         cp(R(off, 128 * h, 128 * h + 128), R("p3", tmp, tmp + 128))
 
     def items(off, buf, h, eng):
@@ -418,16 +549,19 @@ def build(g, core, T, topo):
             lo = 128 * h + w_ * q
             gather(R(buf, 16 * lo, 16 * (lo + w_)), R("X"), R(off, lo, lo + w_), BIAS, eng[q % len(eng)], alt=GALT)
 
-    def keys(buf, bank, h, part, stop):
-        n = (32, 16)[part]
-        mm([(R(bank, k, 16 * n, 16), R(buf, 2048 * h + 15 - brev(k), 2048 * h + 2048, 16),
-             R("Wk", 32 * part, 32 * part + n)) for k in range(16)], stop=stop, wr=[R(bank)])
+    def keys(buf, bank, h, part, stop, start=True):
+        mm([(R(bank, k, 384, 16), R(buf, 2048 * h + 15 - brev(k), 2048 * h + 2048, 16),
+             R("Wk", 24 * part, 24 * part + 24)) for k in range(16)], start=start, stop=stop, wr=[R(bank)])
 
-    def diffs(piv, a, h, ds):
-        mm([(R(a + str(h)), piv, R("Wrep", 0, 512))], start=False)
-        mm([(R("b%d" % h, 0, 256), piv, R("Wrep", 512, 768))], start=False)
-        cp(R("DS", ds, ds + 512), R(a + str(h)), DENG[0])
-        cp(R("DS", ds + 512, ds + 768), R("b%d" % h, 0, 256), DENG[1])
+    def diffs(piv, buf, a, h, ds, tiers):
+        bk = (a + str(h), "b%d" % h if tiers == 1 else a + str(h))
+        mm([(R(bk[0], 0, 384), piv, R("Wrep", 0, 384))], start=False, stop=tiers == 1, wr=[R(bk[0])])
+        if tiers == 2:
+            keys(buf, bk[1], h, 1, False, False)
+        else:
+            cp(R("DS", ds + 384, ds + 768), R(bk[0], 0, 384), DENG[1])
+        mm([(R(bk[1], 0, 384), piv, R("Wrep", 384, 768))], start=False, wr=[R(bk[1])])
+        cp(R("DS", ds, ds + 384), R(bk[1], 0, 384), DENG[0])
 
     def fix(q):
         off = T.offc[:, 16 + 4 * q:20 + 4 * q]
@@ -437,9 +571,9 @@ def build(g, core, T, topo):
         add("V", lambda e: g.vector.tensor_copy(T.yxs[:].indirect(off), a[0]),
             [a, R("offc", 16, 32)], [R("yxs")], vc(64, 3.8))
 
-    def order_sum(out, ds, dead, th):
-        mm([(out, R("DS", ds + 128 * j, ds + 128 * j + 128), IB(0)) for j in range(6)]
-           + [(out, dead, IB(2)), (out, IB(3), th)])
+    def order_sum(out, ds, n, dead, th):
+        mm([(out, IB(3), th), (out, dead, IB(2))]
+           + [(out, R("DS", ds + 128 * j, ds + 128 * j + 128), IB(0)) for j in range(n)])
 
     for t in range(RO):
         to = T.cores[(rank + 1 + t % (N - 1)) % N]
@@ -451,11 +585,11 @@ def build(g, core, T, topo):
             cur[0] = h
             M = "m%d" % h
             mm([(R(M, 0, 128), R("Wblk"), ln("Z", h))])
-            cp(ln("si", h), R(M, 0, 128))
-            ts(ln("ui", h), ln("si", h), 1023, A.bitwise_and)
-            ts(R(M, 128, 256), ln("ui", h), 2.0, A.mult, 33.0, A.add)
-            ts(R(M, 256, 384), R(M, 128, 256), 4096.0, A.mult, R("K32", t, t + 1), A.add)
-            offsets(ln("nf", h, 256 * t), "offx", M, 128 * h, h)
+            ts(ln("q0", h), R(M, 0, 128), 3 * 2.0 ** 16 - 511.5, A.add)
+            U = R(M, 128, 256)
+            mm([(U, R("Wblk"), ln("Z", h)), (U, IB(1), ln("q0", h)), const(U, 2)])
+            offsets(ln("nf", h, 256 * t), "offx", M, R("b%d" % h, 256, 384), 128 * h, h, t)
+        cur[0] = 0
         mm([(R("m0", 384, 400), R("Wband", 15 - il, 143 - il), R("Z", il, 256, 16)) for il in range(16)])
         cp(R("ci"), R("m0", 384, 400))
         ts(R("cj"), R("ci"), 31, A.bitwise_and)
@@ -473,52 +607,52 @@ def build(g, core, T, topo):
             items("offx", "xg", h, GX[h] if t else GX0[h])
             keys("xg", "xa%d" % h, h, 0, True)
             keys("xg", "b%d" % h, h, 1, True)
-            offsets(ln("bn", h, 256 * t), "offy", "m%d" % h, 256 + 128 * h, h)
+            offsets(ln("bn", h, 256 * t), "offy", "m%d" % h, R("m%d" % h, 0, 128), 256 + 128 * h, h, t)
             items("offy", "yg", h, GY[h])
             keys("yg", "ya%d" % h, h, 0, False)
         for h in H:
             cur[0] = h
             M = "m%d" % h
-            act(R(M, 0, 128), ln("nf", h, 256 * t), AF.Identity, bias=4128.0)
-            tt(ln("f1", h), ln("ui", h), R(M, 0, 128), A.mult)
-            ts(ln("f2", h), ln("f1", h), C(21), A.add)
-            ts(ln("f1", h), ln("f2", h), 5, A.arith_shift_right, V - 1, A.bitwise_and)
+            W = R(M, 384, 512)
+            mm([(W, R("W32"), ln("Z", h)), (W, IB(6), ln("q0", h)), (W, R("Fk"), ONE)])
+            tt(ln("f1", h), ln("p1", h), W, A.add)
+            ts(ln("f2", h), ln("f1", h), 5, A.arith_shift_right, V - 1, A.bitwise_and)
+            Km = R("Kp", 144 * h + 16, 144 * h + 144)
             for j in range(6):
-                Kp = plane(h, j)
-                sg = R("seg", 1, 128) if j == 0 else R("S", 128 * h + 1, 128 * h + 128)
-                scan(R("tt", 128 * h + 1, 128 * h + 128), plane(h, j, 0, 127), sg, A.max, A.min, -2.0 ** 90)
-                if j < 5:
-                    tt(ln("D", h), Kp, ln("tt", h), A.subtract)
-                    if RENG == "V":
-                        tt(ln("S", h), ln("tt", h), Kp, A.subtract)
-                    elif RENG == "A":
-                        act(ln("S", h), ln("D", h), AF.Identity, scale=-1.0)
-                    else:
-                        ts(ln("S", h), ln("D", h), -1.0, A.mult)
-                    tt(plane(h, j + 1), plane(h, j + 1), ln("D", h), A.min)
+                here, other = plane(h, 6 + (j & 1)), plane(h, 7 - (j & 1))
+                if j == 0:
+                    Kj, Tj = plane(h, 0), ln("tt", h)
+                    scan(R("tt", 128 * h + 1, 128 * h + 128), plane(h, 0, 0, 127), R("seg", 1, 128), A.max, A.min,
+                         -2.0 ** 90)
                 else:
-                    tt(ln("dA", h, 256 * t), Kp, ln("tt", h), A.is_lt)
+                    Kj, Tj = Km, here
+                    scan(Tj, R("Kp", 144 * h + 15, 144 * h + 143), other, A.max, A.min, -2.0 ** 90)
+                if j < 5:
+                    tt(ln("D", h), Kj, Tj, A.subtract)
+                    mm([(here, IB(1), ln("D", h))])
+                    tt(Km, plane(h, j + 1), ln("D", h), A.min)
+                else:
+                    tt(ln("dA", h, 256 * t), Kj, Tj, A.is_lt)
             dead, eb, om = ln("dA", h, 256 * t), 144 * h, 16 * t + 8 * h
             scan(ln("c1", h), R("d0"), dead, A.add, A.mult)
             cp(R("ee", eb + 16, eb + 144, 16), R("c1", 128 * h + 15, 128 * h + 128, 16), "VA")
-            mm([(R(M, 0, 8), R("ones", 0, 128, p=(0, 1)), R("rows", 256, 264, p=(0, 1)))]
-               + [(R(M, 0, 8), R("ee", eb + 16 - il, eb + 144 - il), R("IB", il, 128, 16)) for il in range(16)])
-            ts(R("offm", om, om + 8), R(M, 0, 8), C(12), A.add)
+            mm([(R(M, 256, 264), R("ones", 0, 128, p=(0, 1)), R("rows", 256, 264, p=(0, 1)))]
+               + [(R(M, 256, 264), R("ee", eb + 16 - il, eb + 144 - il), R("IB", il, 128, 16)) for il in range(16)])
+            ts(R("offm", om, om + 8), R(M, 256, 264), C(12), A.add)
             send(R("offm", om, om + 8), R("offb", om, om + 8), "ro%d" % (2 * t + h), to, 2200.0)
             send(dead, ln("dB", h, 256 * t), "rd%d" % (2 * t + h), to, 2500.0)
             gather(ln("Mb", h), R("xg", 2048 * h, 2048 * h + 2048), R("offm", om, om + 8), alt=FALT)
-            keys("yg", "b%d" % h, h, 1, False)
             keys("xg", "xa%d" % h, h, 0, False)
-            W = R(M, 384, 512)
+            if XT == 1:
+                keys("xg", "b%d" % h, h, 1, False)
             mm([(W, IB(0), ln("Z", h)), (W, IB(1), ln("Mb", h))])
             act(ln("ge", h), W, AF.Sign, bias=C(23))
             mm([(W, R("blk"), ln("ge", h))])
             act(R("TH", 256 * h, 256 * h + 128), W, AF.Relu, bias=-2.0 ** 90, scale=-2.0 ** 89)
             act(R("TH", 256 * h + 128, 256 * h + 256), W, AF.Relu, bias=2.0 ** 91, scale=2.0 ** 89)
-            diffs(ln("Mb", h), "ya", h, 768 * (2 + h))
-            keys("xg", "b%d" % h, h, 1, False)
+            diffs(ln("Mb", h), "yg", "ya", h, 768 * (2 + h), 2)
             P = R("ya%d" % h, 0, 256)
-            mm([(P, R("cc", p=(0, 64)), R("ones", p=(0, 64))),
+            mm([(P, R("cc", 0, 128, p=(0, 64)), R("ones", p=(0, 64))),
                 (R("ya%d" % h, 0, 256, 2), ln("nf", h, 256 * t), c8("Prm")),
                 (R("ya%d" % h, 1, 256, 2), ln("bn", h, 256 * t), c8("Prm"))], stop=False,
                wr=[R("ya%d" % h)])
@@ -531,8 +665,10 @@ def build(g, core, T, topo):
         if t < RO - 1:
             add("V", lambda e: g.vector.tensor_copy(T.X[:].indirect(T.offc[:, 0:16]), T.xi[:]),
                 [R("xi"), R("offc", 0, 16)], [R("X")], vc(256, 3.8))
-            mm([(R("m0", 384, 512), R("ones", 0, 128), ln("dA", h, 256 * t)) for h in H])
-            act(R("junk", 0, 128), R("m0", 384, 512), AF.Identity, bias=-65536.0, scale=32.0, acc=R("K32", t + 1, t + 2))
+            W = R("m0", 384, 512)
+            mm([(W, ONE, ln("dA", h, 256 * t)) for h in H]
+               + [(W, R("ones", 0, 128, p=(0, 1)), R("IB", 128 * 5, 128 * 6, p=(0, 1)))])
+            act(R("junk", 0, 128), W, AF.Identity, bias=-32768.0, scale=16.0, acc=R("K16", t + 1, t + 2))
         else:
             for q in range(4):
                 if q % 2 == 0:
@@ -544,9 +680,9 @@ def build(g, core, T, topo):
             cur[0] = h
             M, om = "m%d" % h, 16 * t + 8 * h
             gather(ln("Yb", h), R("yg", 2048 * h, 2048 * h + 2048), R("offb", om, om + 8), alt=FALT)
-            order_sum(R(M, 256, 384), 768 * (2 + h), ln("dB", h, 256 * t), R("TH", 256 * h + 128, 256 * h + 256))
-            diffs(ln("Yb", h), "xa", h, 768 * h)
-            order_sum(R(M, 128, 256), 768 * h, ln("dA", h, 256 * t), R("TH", 256 * h, 256 * h + 128))
+            order_sum(R(M, 256, 384), 768 * (2 + h), 3, ln("dB", h, 256 * t), R("TH", 256 * h + 128, 256 * h + 256))
+            diffs(ln("Yb", h), "xg", "xa", h, 768 * h, XT)
+            order_sum(R(M, 128, 256), 768 * h, 6 // XT, ln("dA", h, 256 * t), R("TH", 256 * h, 256 * h + 128))
             W = R(M, 384, 512)
             mm([(W, IB(0), ln("Z", h)), (W, IB(1), ln("Yb", h))])
             act(ln("Z" if t < RO - 1 else "zf", h), W, AF.Abs, bias=BIAS)
@@ -565,19 +701,17 @@ def build(g, core, T, topo):
             tgt = lambda b: [(R(b, 0, 256, 2), kA, c8("Tri")), (R(b, 1, 256, 2), kB, c8("Tri")),
                              (R(b, 0, 256, 2), fB, c8("mG")), (R(b, 1, 256, 2), fA, c8("mG"))]
             mm(tgt(XA), wr=[R(XA)])
-            if MODPE:
-                T2 = R("b%d" % h, 0, 256)
-                mm(tgt("b%d" % h), stop=False, wr=[R("b%d" % h)])
-                act(w2("sg"), Tt, AF.Sign, bias=-8.0)
-                mm([(T2, IB(4), w2("sg"))], start=False)
-                ts(w2("k1"), T2, -0.5, A.add, KM, A.mult)
-            else:
-                ts(w2("k1"), Tt, 7.5, A.add)
-                ts(w2("k2"), w2("k1"), 15, A.bitwise_and)
-                ts(w2("k1"), w2("k2"), KM, A.mult)
-            mm([(R(YA, 0, 256, 2), kA, c8("D8")), (R(YA, 1, 256, 2), kB, c8("D8")), (R(YA, 0, 256, 2), fA, c8("D8")),
-                (R(YA, 1, 256, 2), fB, c8("D8"))], start=False, wr=[P])
-            mm([(O, R("CD"), R("oneF"))], stop=False, wr=[R(XA)])
+            T2 = R("b%d" % h, 0, 256)
+            mm(tgt("b%d" % h), stop=False, wr=[R("b%d" % h)])
+            act(w2("sg"), Tt, AF.Sign, bias=-8.0)
+            mm([(T2, IB(4), w2("sg"))], start=False, wr=[R("b%d" % h)])
+            ts(w2("k1"), T2, -0.5, A.add, KM, A.mult)
+            mm([(R(YA, 0, 256, 2), kA, c8("D8")), (R(YA, 1, 256, 2), kB, c8("D8"))], start=False, stop=False, wr=[P])
+            mm([(P, IB(7), w2("sg"))], start=False)
+            G = R(M, 384, 512)
+            mm([(G, IB(8), ONE), (G, R("blkn"), kA), (G, R("blkn"), kB)])
+            tt(ln("fb", h), ln("f2", h), G, A.min)
+            mm([(O, R("CD"), ONE)], stop=False, wr=[R(XA)])
             ts(w2("k2"), w2("k1"), KMASK, A.bitwise_and)
             lo = lambda s, a=0, b=128, st=1: R("va", 256 * h + 128 * s + a, 256 * h + 128 * s + b, st)
             hi = lambda s, a=0, b=128, st=1: R(YA, 256 + 128 * s + a, 256 + 128 * s + b, st)
@@ -594,12 +728,8 @@ def build(g, core, T, topo):
             fin = lambda L_: (T.fin[:, 16 * h + L_:16 * h + 16:2, :], ("fin", 256 * h, 256 * h + 256, 1), 128, False, False)
             tt(ln("mg", h), fin(0), fin(1), A.max)
             mm([(O, ln("mg", h), R("IF"))], start=False)
-            tt(ln("r1", h), ln("f1", h), O, A.max)
-            ts(ln("r2", h), ln("r1", h), V - 1, A.bitwise_and)
-            if t < RO - 1:
-                ts(ln("nf", h, 256 * (t + 1)), ln("r2", h), -4096.0, A.add)
-            else:
-                cp(ln("nf", h, 256 * (t + 1)), ln("r2", h))
+            tt(ln("nf", h, 256 * (t + 1)), ln("fb", h), O, A.max)
+            if t == RO - 1:
                 mm([(R(M, 0, 128), R("PP"), ln("nf", h, 256 * (t + 1)))])
                 cp(ln("yas", h), R(M, 0, 128), "AV")
                 dma("S", T.ya[:, 128 * h:128 * h + 128], T.yas[:, 128 * h:128 * h + 128], [ln("yas", h)], [], 2000.0)
@@ -625,7 +755,7 @@ def rank_program(g, core, T, topo):
         e = o["on"]
         if e == "N":
             continue
-        need = list(o["deps"])
+        need = [d for d in o["deps"] if d not in o["soft"] or ops[d]["on"] != e]
         for b in o["banks"]:
             need += [j for e2, j in bank.get(b, {}).items() if e2 != e]
             bank.setdefault(b, {})[e] = i

@@ -11,30 +11,28 @@ def _sb(n, d):
 
 SCRATCH = {
     "X": _sb(V, BF), "xg": _sb(4096, BF), "yg": _sb(4096, BF), "yxs": _sb(2048, F32),
-    "ami": _sb(256, I32), "wti": _sb(4, I32), "Z": _sb(256, BF), "Zb": _sb(256, BF), "zf": _sb(256, F32),
+    "ami": _sb(256, I32), "wti": _sb(4, I32), "Z": _sb(768, BF), "zf": _sb(256, F32),
     "nf": _sb(4 * 256, F32), "bn": _sb(3 * 256, F32), "dA": _sb(3 * 256, BF), "dB": _sb(3 * 256, BF),
     "offx": _sb(256, U16), "offy": _sb(256, U16), "offm": _sb(48, U16), "offb": _sb(48, U16),
-    "offc": _sb(32, U16), "D": _sb(256, BF), "q0": _sb(256, BF), "Kb": _sb(128, BF), "Kp": _sb(288, F32),
+    "offc": _sb(32, U16), "D": _sb(256, BF), "q0": _sb(768, BF), "Kp": _sb(288, F32),
     "p1": _sb(512, F32), "p2": _sb(512, I32), "p3": _sb(512, I32),
     "f1": _sb(256, I32), "f2": _sb(256, I32), "fb": _sb(256, F32),
     "tt": _sb(256, F32),
-    "c1": _sb(512, BF), "ee": _sb(576, BF), "sg": _sb(512, BF), "xo": _sb(256, BF),
+    "c1": _sb(256, BF), "ee": _sb(288, BF), "sg": _sb(512, BF), "xo": _sb(256, BF),
     "Mb": _sb(256, BF), "Yb": _sb(256, BF), "ge": _sb(256, BF), "TH": _sb(512, BF),
     "fin": ("sbuf", [128, 32, 16], F32), "CD": _sb(128, BF), "K16": _sb(4, F32),
-    "DS": _sb(4 * 768, BF), "keep": _sb(512, BF), "kf": _sb(512, BF),
-    "k1": _sb(512, I32), "k2": _sb(512, I32), "va": _sb(512, F32), "vb": _sb(512, F32), "mg": _sb(256, F32),
-    "yas": _sb(256, F32),
+    "DS": _sb(4 * 384, BF), "keep": _sb(512, BF), "kf": _sb(512, BF),
+    "k1": _sb(512, I32), "k2": _sb(512, I32), "va": _sb(512, F32), "mg": _sb(256, F32), "yas": _sb(256, F32),
     "ci": _sb(16, I32), "cj": _sb(16, I32), "cf": _sb(16, F32), "xs": _sb(256, F32), "xi": _sb(256, I32),
-    "xn": _sb(256, F32), "junk": _sb(256, F32),
-    "lin": _sb(256, F32), "idq": _sb(768, F32), "srev": _sb(256, F32), "gl": _sb(256, F32), "cm16": _sb(128, F32),
-    "pi": _sb(16, I32), "col": _sb(48, F32), "c32": _sb(32, F32), "I165": _sb(128, F32),
-    "W32": _sb(128, BF), "s16": _sb(128, BF), "Fk": _sb(128, BF), "kb": _sb(128, F32), "blkn": _sb(128, BF),
-    "mGn": _sb(128, BF),
-    "IB": _sb(10 * 128, BF), "IF": _sb(128, F32), "PP": _sb(128, F32), "Wrep": _sb(768, BF), "Wk": _sb(48, BF),
-    "blk": _sb(128, BF), "Wblk": _sb(128, BF), "Wband": _sb(144, BF), "diag": _sb(128, BF), "seg": _sb(128, BF),
-    "d0": _sb(128, BF), "ones": _sb(256, BF), "cc": _sb(384, BF), "rows": _sb(272, BF),
-    "mG": _sb(264, BF), "Tri": _sb(264, BF), "D16": _sb(264, BF), "D8": _sb(264, BF), "Prm": _sb(264, F32),
-    "tmp": _sb(264, F32), "tm2": _sb(264, F32),
+    "junk": _sb(256, F32),
+    "lin": _sb(144, BF), "idq": _sb(768, BF), "srev": _sb(256, BF), "gl": _sb(128, BF),
+    "pi": _sb(16, I32), "col": _sb(32, F32), "c32": _sb(32, F32), "cb": _sb(8, BF),
+    "W32": _sb(128, BF), "Fk": _sb(128, BF), "blkn": _sb(128, BF),
+    "IB": _sb(9 * 128, BF), "IF": _sb(128, F32), "PP": _sb(128, F32), "Wrep": _sb(768, BF), "Wk": _sb(48, BF),
+    "blk": _sb(128, BF), "Wblk": _sb(128, BF), "Wband": _sb(144, BF), "diag": _sb(16, BF), "seg": _sb(128, BF),
+    "d0": _sb(128, BF), "ones": _sb(256, BF), "cc": _sb(256, BF), "rows": _sb(8, BF),
+    "mG": _sb(128, BF), "Tri": _sb(128, BF), "D8": _sb(128, BF), "Prm": _sb(128, F32),
+    "tmp": _sb(16, F32), "tmb": _sb(384, BF),
 }
 PSUM = ("xa0", "xa1", "b0", "ya0", "ya1", "b1", "m0", "m1")
 for _b in PSUM:
@@ -45,20 +43,19 @@ SEMAPHORES = (["eV", "eA", "eP", "eG", "sent"] + ["d%d" % i for i in range(16)]
 
 CY, PECY, FIX, LAT, GA = 0.95, 0.48, 60.0, 115.0, 1.56
 GSPLIT = 2
-GX = (("A", "AV"), ("A", "AV"))
+GX = (("A", "A"), ("A", "A"))
 GY = (("A", "A"), ("A", "A"))
 GX0 = (("A", "V"), ("A", "AV"))
 GALT = 600.0
-RENG = "AV"
-DENG = ("AV", "AV")
-XT = 1
+WB = ("b%d", "m%d", "m%d", "b%d")
+KS, PFIX = 4, 40.0
 LEAD = 3000.0
 SEED, NOISE = 7, 2500.0
 FALT = 300.0
-LF = 1.35
-SPLITB = True
-PASSES = 80
-MOVES, TEMP, SOFT = 60000, 500.0, 1
+LF = 0.8
+SPLITB = False
+PASSES = 20
+MOVES, TEMP, SOFT = 130000, 300.0, 1
 SLACK = 700.0
 WIN, WARM = 12000.0, 100
 
@@ -89,7 +86,8 @@ def plan_order(ops, memo):
             for (j, w, y) in hist.get(x[0], []):
                 if meets(x[1:], y):
                     deps.add(j)
-        o["soft"] = set(j for j in deps - raw if SOFT and ops[j]["eng"] == "P" and o["eng"] == "P" and (o["cont"] or SOFT > 1))
+        o["soft"] = set(j for j in deps - raw if (ops[j]["eng"] == "P" and o["eng"] == "P" and (o["cont"] or SOFT > 1))
+                        or (SOFT > 2 and ops[j]["sem"] is None and o["sem"] is None))
         for x in o["w"]:
             hist[x[0]] = [e for e in hist.get(x[0], [])
                           if not (x[1] <= e[2][0] and e[2][1] <= x[2] and (x[3] == 1 or x[1:] == e[2]))]
@@ -206,13 +204,32 @@ def refine(ops, order, on, x):
     on = [eid[e] for e in on]
     others = ((1, 2), (0, 2), (0, 1))
 
-    def run(order, on):
-        end, why, held = [0.0] * (n + 1), [n] * n, [False] * n
-        end[n] = -1e9
-        fin = [0.0] * n
+    anc = []
+    for i in range(n):
+        m = 0
+        for d in deps[i]:
+            m |= anc[d]
+        hard[i] = [d for d in hard[i] if not (m >> d & 1) or ops[d]["lat"] > 0]
+        for d in deps[i]:
+            m |= 1 << d
+        anc.append(m)
+    ends = [i for i in range(n) if not any(a_ >> i & 1 for a_ in anc)]
+
+    def run(order, on, old=None, a=0, z=0, limit=1e18):
+        if old is None:
+            end, why, held, fin = [0.0] * (n + 1), [n] * n, [False] * n, [0.0] * n
+            end[n] = -1e9
+        else:
+            end, why, held, fin = old[1][:], old[2][:], old[4][:], old[5][:]
         last, bl = [n] * 6, [n] * (3 * len(PSUM))
-        top, ti = 0.0, 0
-        for i in order:
+        for i in order[max(0, a - 150):a]:
+            e = on[i]
+            last[e] = i
+            for b in banks[i]:
+                bl[b + e] = i
+        k = a - z
+        for i in order[a:]:
+            k += 1
             e = on[i]
             t, p, q = 0.0, n, False
             for d in hard[i]:
@@ -233,20 +250,59 @@ def refine(ops, order, on, x):
                 if end[d] > t:
                     t, p, q = end[d], d, True
                 last[e] = i
+            if k > 1 and t + tail[i] > limit:
+                return None
             t += cost[i]
             end[i], why[i], held[i] = t, p, q
-            t += lat[i]
-            fin[i] = t
-            if t > top:
-                top, ti = t, i
-        path, i = [], ti
+            fin[i] = t + lat[i]
+        i = max(ends, key=lambda j: fin[j])
+        top, path = fin[i], []
         while i != n:
             if held[i]:
                 path.append(i)
             i = why[i]
-        return top - LAT, end, why, path
+        return top - LAT, end, why, path, held, fin
 
+    hs, ss = [[] for _ in range(n)], [[] for _ in range(n)]
+    for i in range(n):
+        for d in hard[i]:
+            hs[d].append(i)
+        for d in soft[i]:
+            ss[d].append(i)
+
+    def tails(order, on, z):
+        nxt, bn = [0.0] * 6, [-1e9] * (3 * len(PSUM))
+        for i in reversed(order[z + 1:z + 150]):
+            e = on[i]
+            nxt[e] = tail[i]
+            for b in banks[i]:
+                bn[b + e] = tail[i] + LAT
+        for i in reversed(order[:z + 1]):
+            e = on[i]
+            t = -LAT
+            for j in hs[i]:
+                if tail[j] > t:
+                    t = tail[j]
+            t += lat[i]
+            for j in ss[i]:
+                v = tail[j] if on[j] == e else tail[j] + lat[i]
+                if v > t:
+                    t = v
+            if e < 5 and nxt[e] > t:
+                t = nxt[e]
+            for b in banks[i]:
+                for e2 in others[e]:
+                    if bn[b + e2] > t:
+                        t = bn[b + e2]
+            t += cost[i]
+            tail[i] = nxt[e] = t
+            for b in banks[i]:
+                bn[b + e] = t + LAT
+
+    tail = [0.0] * n
     cur = run(order, on)
+    tails(order, on, n)
+    took = 0
     best = (cur[0], cur[1], on, order)
     for it in range(MOVES):
         x = (x * 1103515245 + 12345) % 2147483648
@@ -259,6 +315,7 @@ def refine(ops, order, on, x):
             j = i if len(engs[i]) > 1 and (len(engs[p]) == 1 or x & 64) else p
             on2 = list(on)
             on2[j] = engs[j][0] if on[j] != engs[j][0] else engs[j][1]
+            a = b = order.index(j)
         else:
             a, b = order.index(p), order.index(i)
             x = (x * 1103515245 + 12345) % 2147483648
@@ -285,11 +342,16 @@ def refine(ops, order, on, x):
                 if i in take:
                     continue
                 new = order[:a] + [j for j in mid if j not in take] + [j for j in mid if j in take] + order[b + 1:]
-        res = run(new, on2)
         x = (x * 1103515245 + 12345) % 2147483648
-        if res[0] <= cur[0] + TEMP * (1.0 - it / MOVES) * (x / 2147483648.0) ** 2:
+        limit = cur[0] + TEMP * (1.0 - it / MOVES) * (x / 2147483648.0) ** 2 + 0.01
+        res = run(new, on2, cur, a, b, limit)
+        if res is not None and res[0] <= limit:
             end = res[1]
-            order, on, cur = sorted(new, key=lambda j: end[j] - cost[j]), on2, res
+            tails(new, on2, b)
+            order, on, cur = new, on2, res
+            took += 1
+            if took % 8 == 0:
+                order = sorted(new, key=lambda j: end[j] - cost[j])
             if res[0] < best[0]:
                 best = (res[0], end, on, order)
     return best[0], best[1], ["VAPGSN"[e] for e in best[2]], best[3]
@@ -372,12 +434,21 @@ def build(g, core, T, topo):
         return add("G", fn, [], [o], 150 + 2 * o[2] * CY)
 
     def mm(lst, start=True, stop=True, wr=None, after=()):
+        cyc = [max(64, r[2]) * (1 if r[3] else 4) for (o, l, r) in lst]
+        if len(lst) > 1 and sum(cyc) > 64 * KS + 128:
+            k = 1
+            while sum(cyc[:k + 1]) <= 64 * KS:
+                k += 1
+            wr = [R(lst[0][0][1][0])]
+            mm(lst[:k], start, False, wr, after)
+            return mm(lst[k:], False, stop, wr)
+
         def fn(e):
             ins = None
             for k, (o, l, r) in enumerate(lst):
                 ins = g.tensor.matmul(o[0], l[0], r[0], start and k == 0, stop and k == len(lst) - 1)
             return ins
-        cost = sum(max(64, r[2]) * (1 if r[3] else 4) * PECY for (o, l, r) in lst) + 40
+        cost = sum(max(64, r[2]) * (1 if r[3] else 4) * PECY for (o, l, r) in lst) + (PFIX if stop else 0.0)
         return add("P", fn, [x[1] for x in lst] + [x[2] for x in lst], wr or [x[0] for x in lst], cost, after=after,
                    cont=not start)
 
@@ -421,18 +492,19 @@ def build(g, core, T, topo):
     IB = lambda j: R("IB", 128 * j, 128 * j + 128)
 
     dma("S", T.ami[:], T.am[:], [], [R("ami")], 2000.0)
-    dma("S", T.Z[:], T.zv[:], [], [R("Z")], 2000.0)
+    dma("S", T.Z[:, 0:256], T.zv[:], [], [R("Z", 0, 256)], 2000.0)
     dma("S", T.wti[:, 0:1], T.wt[:], [], [R("wti")], 2000.0)
     dma("A", T.X[:], T.xt[:], [], [R("X")], 8000.0)
 
     iota(PI(0), [[0, 1]], 0, 1)
-    iota(R("lin"), [[1, 256]])
-    iota(R("idq"), [[1, 48], [0, 16]])
+    iota(R("lin"), [[1, 144]])
+    iota(R("idq", 0, 128), [[1, 8], [0, 16]])
+    iota(R("idq", 128, 768), [[1, 40], [0, 16]], 8)
     for q in range(4):
-        iota(R("srev", 32 * q, 32 * q + 32), [[4, 2], [8, 2], [0, 8]], (q >> 1) + 2 * (q & 1))
-    iota(R("gl", 0, 128), [[0, 8], [1, 16]])
-    iota(R("gl", 128, 256), [[0, 16], [1, 8]])
-    iota(R("srev", 128, 256), [[1, 16], [0, 8]])
+        iota(R("srev", 32 * q, 32 * q + 32), [[4, 2], [8, 2], [16, 8]], (q >> 1) + 2 * (q & 1))
+    iota(R("gl"), [[0, 16], [1, 8]])
+    iota(R("srev", 128, 256), [[1, 16], [16, 8]])
+    iota(R("rows"), [[256, 8]])
     iota(R("c32", 0, 16), [[512, 16]])
     iota(R("c32", 16, 32), [[0, 4], [512, 4]])
     ts(PI(1), PI(0), 15, A.bitwise_and)
@@ -458,12 +530,11 @@ def build(g, core, T, topo):
     ts(C(13), C(1), 32.0, A.mult)
     ts(C(14), C(2), 16.0, A.mult)
     ts(C(15), C(14), 15.0, A.add)
-    ts(C(16), C(2), 8.0, A.add)
-    ts(C(17), C(1), -1.0, A.mult, 15.0, A.add)
+    ts(C(17), C(1), -1.0, A.mult, C(15), A.add)
     cp(C(18), R("wti", 0, 1))
-    ts(R("IF"), R("lin", 0, 128), C(0), A.is_equal)
     ts(IB(0), R("lin", 0, 128), C(0), A.is_equal)
-    for j, c in ((1, -1.0), (2, -2.0 ** 86), (3, 2.0 ** -10), (4, -8.0), (5, -1.0 / 32), (6, -32.0), (7, -4096.0)):
+    cp(R("IF"), IB(0), "AV")
+    for j, c in ((1, -1.0), (2, -2.0 ** 86), (3, 2.0 ** -10), (4, -8.0), (5, -1.0 / 32), (6, -32.0), (7, 4096.0)):
         ts(IB(j), IB(0), c, A.mult)
     ts(R("Wk"), R("lin", 0, 48), C(5), A.is_equal, C(8), A.mult)
     for j in range(6):
@@ -475,55 +546,50 @@ def build(g, core, T, topo):
     ts(R("blk"), R("idq", 0, 128), C(2), A.is_equal)
     ts(R("Wblk"), R("idq", 0, 128), C(2), A.is_equal, C(18), A.mult)
     ts(R("Wband"), R("lin", 0, 144), C(15), A.is_equal, C(18), A.mult)
-    ts(R("diag", 0, 16), R("gl", 0, 16), C(1), A.is_equal)
-    ts(R("seg"), R("gl", 0, 128), 0.0, A.is_equal, -2.0 ** 90, A.mult)
+    ts(R("diag", 0, 16), R("lin", 0, 16), C(1), A.is_equal)
+    mset(R("seg"), 0.0)
+    mset(R("seg", 0, 128, 16), -2.0 ** 90)
     tt(R("tmp", 0, 16), R("diag", 0, 16), R("srev", 0, 128, 8), A.mult)
     add("V", lambda e: g.vector.tensor_reduce(T.col[:, 19:20], T.tmp[:, 0:16], AxisListType.X, A.add),
         [R("tmp", 0, 16)], [C(19)], vc(16))
     ts(C(20), C(19), C(14), A.add)
     ts(R("PP"), R("lin", 0, 128), C(20), A.is_equal)
     ts(R("W32"), R("Wblk"), 32.0, A.mult)
-    ts(R("blkn"), R("blk"), -2.0 ** 14, A.mult)
-    ts(C(21), C(19), -15.5, A.add, 2.0 ** 15, A.mult)
+    ts(R("blkn"), R("blk"), 2.0 ** 14, A.mult)
+    ts(C(21), C(19), -15.5, A.add, -2.0 ** 15, A.mult)
     ts(IB(8), IB(0), C(21), A.mult)
-    cp(R("kb", 0, 16), R("srev", 0, 128, 8))
-    for w_ in (16, 32, 64):
-        cp(R("kb", w_, 2 * w_), R("kb", 0, w_))
-    ts(C(27), C(0), 1.0, A.is_equal, 1024.0, A.mult)
-    ts(C(28), C(0), 2.0, A.is_equal, 160.0, A.mult)
-    tt(C(29), C(27), C(28), A.add)
-    ts(C(30), C(0), 0.0, A.is_equal, 3 * 2.0 ** 21, A.mult)
-    ts(R("Fk"), R("kb"), C(29), A.mult, C(30), A.add)
     KM, KMASK = float(0x1111 << 12), (1 << 24) | (1 << 21) | (1 << 18) | (1 << 15)
-    ts(R("k1", 0, 128), R("kb"), KM, A.mult)
-    ts(C(31), C(0), 0.0, A.is_equal, -1.0, A.mult)
-    ts(C(32), C(0), 1.0, A.is_equal, -1.0, A.mult)
-    for j, (mk, c) in enumerate(((KMASK - (1 << 15), -2.0 ** 24), (1 << 15, 16384.0))):
-        ts(R("k2", 128 * j, 128 * j + 128), R("k1", 0, 128), mk, A.bitwise_and)
-        ts(R("va", 128 * j, 128 * j + 128), R("k2", 128 * j, 128 * j + 128), c, A.add, C(31 + j), A.mult)
-    tt(R("CD"), R("va", 0, 128), R("va", 128, 256), A.add)
-    mset(R("d0", 0, 1), 0.0)
-    tt(R("d0", 1, 16), R("srev", 8, 128, 8), R("srev", 0, 120, 8), A.subtract)
-    for w_ in (16, 32, 64):
-        cp(R("d0", w_, 2 * w_), R("d0", 0, w_))
+    CB = lambda j: R("cb", j, j + 1)
+    mset(CB(0), 3 * 2.0 ** 21)
+    ts(CB(1), C(19), 1024.0, A.mult)
+    ts(CB(2), C(19), 160.0, A.mult)
+    ts(PI(5), C(19), KM, A.mult)
+    ts(PI(6), PI(5), KMASK - (1 << 15), A.bitwise_and)
+    ts(PI(8), PI(5), 1 << 15, A.bitwise_and)
+    ts(CB(4), PI(6), -1.0, A.mult, 2.0 ** 24, A.add)
+    ts(CB(5), PI(8), -1.0, A.mult)
+    for nm, a, b in (("Fk", 0, 3), ("CD", 4, 6)):
+        mm([(R("b1", 0, 128, p=(0, b - a)), R("cb", a, b), IB(0))])
+        cp(R(nm, p=(0, b - a)), R("b1", 0, 128, p=(0, b - a)), "AV")
+    for a, st, c in ((1, 2, 8.0), (2, 4, -4.0), (4, 8, -10.0), (0, 8, -13.0)):
+        mset(R("d0", a, 128, st), c)
     mset(R("ones"), 1.0)
     mset(R("cc", 0, 128, p=(0, 32)), -2.0 ** 19)
     mset(R("cc", 0, 128, p=(32, 64)), 256.0)
-    mset(R("cc", 256, 384, p=(0, 32)), 6144.0)
+    mset(R("cc", 128, 256, p=(0, 32)), 6144.0)
     mset(R("K16", 0, 1), -2.0 ** 22 - 0.5)
-    ts(R("rows", 256, 272), R("lin", 0, 16), 256.0, A.mult)
     ts(R("c32"), R("c32"), C(13), A.add)
     c8 = lambda nm: R(nm, 0, 128)
-    ts(c8("mG"), R("gl", 128, 256), C(2), A.is_equal)
-    ts(c8("tmp"), c8("srev"), C(17), A.is_equal, 4096.0, A.mult)
-    tt(c8("D8"), c8("tmp"), c8("mG"), A.mult)
-    ts(c8("tm2"), c8("srev"), C(17), A.is_gt, 0.5, A.mult)
-    ts(c8("tmp"), c8("tmp"), C(1), A.mult, -0.5 / 4096, A.mult)
-    tt(c8("tmp"), c8("tmp"), c8("tm2"), A.add)
-    tt(c8("Tri"), c8("tmp"), c8("mG"), A.mult)
-    ts(c8("tm2"), R("srev", 128, 256), C(1), A.is_equal)
-    tt(c8("Prm"), c8("tm2"), c8("mG"), A.mult)
-    mset(R("tt"), -2.0 ** 90)
+    ts(c8("mG"), R("gl"), C(2), A.is_equal)
+    ts(c8("D8"), c8("srev"), C(17), A.is_equal, -4096.0, A.mult)
+    ts(R("tmb", 0, 128), c8("srev"), C(17), A.is_gt, 0.5, A.mult)
+    ts(R("tmb", 128, 256), c8("srev"), C(15), A.is_gt, -0.5, A.mult)
+    ts(C(16), C(1), 0.5 / 4096, A.mult)
+    ts(R("tmb", 256, 384), c8("D8"), C(16), A.mult)
+    mm([(R("b0", 0, 128), IB(0), R("tmb", 128 * j, 128 * j + 128)) for j in range(3)])
+    cp(c8("Tri"), R("b0", 0, 128), "AV")
+    ts(c8("Prm"), R("srev", 128, 256), C(0), A.is_equal)
+    mset(R("tt", 0, 256, 128), -2.0 ** 90)
     mset(R("ee"), 0.0)
     mset(R("Kp", 15, 288, 144), 0.0)
     cp(R("junk"), R("ami"))
@@ -543,9 +609,16 @@ def build(g, core, T, topo):
         ts(R("p3", tmp, tmp + 128), R("p2", tmp, tmp + 128), 4, A.arith_shift_right, V - 1, A.bitwise_and)
         cp(R(off, 128 * h, 128 * h + 128), R("p3", tmp, tmp + 128))
 
+    def fallback(h, W, out, t):
+        hl = lambda nm, b=0: R(nm, b + 128 * h, b + 128 * h + 128)
+        mm([(W, R("Fk", p=(0, 3)), R("ones", 0, 128, p=(0, 3))), (W, R("W32"), hl("Z", 256 * t)),
+            (W, IB(6), hl("q0", 256 * t))])
+        tt(hl("f1"), hl("p1"), W, A.add)
+        ts(out, hl("f1"), 5, A.arith_shift_right, V - 1, A.bitwise_and)
+
     def items(off, buf, h, eng):
-        w_ = 128 // GSPLIT
-        for q in range(GSPLIT):
+        w_ = 128 // len(eng)
+        for q in range(len(eng)):
             lo = 128 * h + w_ * q
             gather(R(buf, 16 * lo, 16 * (lo + w_)), R("X"), R(off, lo, lo + w_), BIAS, eng[q % len(eng)], alt=GALT)
 
@@ -553,27 +626,23 @@ def build(g, core, T, topo):
         mm([(R(bank, k, 384, 16), R(buf, 2048 * h + 15 - brev(k), 2048 * h + 2048, 16),
              R("Wk", 24 * part, 24 * part + 24)) for k in range(16)], start=start, stop=stop, wr=[R(bank)])
 
-    def diffs(piv, buf, a, h, ds, tiers):
-        bk = (a + str(h), "b%d" % h if tiers == 1 else a + str(h))
-        mm([(R(bk[0], 0, 384), piv, R("Wrep", 0, 384))], start=False, stop=tiers == 1, wr=[R(bk[0])])
-        if tiers == 2:
-            keys(buf, bk[1], h, 1, False, False)
-        else:
-            cp(R("DS", ds + 384, ds + 768), R(bk[0], 0, 384), DENG[1])
-        mm([(R(bk[1], 0, 384), piv, R("Wrep", 384, 768))], start=False, wr=[R(bk[1])])
-        cp(R("DS", ds, ds + 384), R(bk[1], 0, 384), DENG[0])
+    def diffs(piv, buf, bk, h, ds):
+        mm([(R(bk, 0, 384), piv, R("Wrep", 0, 384))], start=False, stop=False, wr=[R(bk)])
+        keys(buf, bk, h, 1, False, False)
+        mm([(R(bk, 0, 384), piv, R("Wrep", 384, 768))], start=False, wr=[R(bk)])
+        cp(R("DS", ds, ds + 384), R(bk, 0, 384), "AV")
 
     def fix(q):
         off = T.offc[:, 16 + 4 * q:20 + 4 * q]
-        a, b = R("xs", 64 * q, 64 * q + 64), R("xn", 64 * q, 64 * q + 64)
+        a, b = R("xs", 64 * q, 64 * q + 64), R("xi", 64 * q, 64 * q + 64)
         add("V", lambda e: g.vector.tensor_tensor(a[0], T.yxs[:].indirect(off), b[0], A.add),
             [R("yxs"), R("offc", 16, 32), b], [a], vc(64, GA))
         add("V", lambda e: g.vector.tensor_copy(T.yxs[:].indirect(off), a[0]),
             [a, R("offc", 16, 32)], [R("yxs")], vc(64, 3.8))
 
-    def order_sum(out, ds, n, dead, th):
+    def order_sum(out, ds, dead, th):
         mm([(out, IB(3), th), (out, dead, IB(2))]
-           + [(out, R("DS", ds + 128 * j, ds + 128 * j + 128), IB(0)) for j in range(n)])
+           + [(out, R("DS", ds + 128 * j, ds + 128 * j + 128), IB(0)) for j in range(3)])
 
     for t in range(RO):
         to = T.cores[(rank + 1 + t % (N - 1)) % N]
@@ -584,13 +653,13 @@ def build(g, core, T, topo):
         for h in H:
             cur[0] = h
             M = "m%d" % h
-            mm([(R(M, 0, 128), R("Wblk"), ln("Z", h))])
-            ts(ln("q0", h), R(M, 0, 128), 3 * 2.0 ** 16 - 511.5, A.add)
+            mm([(R(M, 0, 128), R("Wblk"), ln("Z", h, 256 * t))])
+            ts(ln("q0", h, 256 * t), R(M, 0, 128), 3 * 2.0 ** 16 - 511.5, A.add)
             U = R(M, 128, 256)
-            mm([(U, R("Wblk"), ln("Z", h)), (U, IB(1), ln("q0", h)), const(U, 2)])
+            mm([(U, R("Wblk"), ln("Z", h, 256 * t)), (U, IB(1), ln("q0", h, 256 * t)), const(U, 1)])
             offsets(ln("nf", h, 256 * t), "offx", M, R("b%d" % h, 256, 384), 128 * h, h, t)
         cur[0] = 0
-        mm([(R("m0", 384, 400), R("Wband", 15 - il, 143 - il), R("Z", il, 256, 16)) for il in range(16)])
+        mm([(R("m0", 384, 400), R("Wband", 15 - il, 143 - il), R("Z", 256 * t + il, 256 * t + 256, 16)) for il in range(16)])
         cp(R("ci"), R("m0", 384, 400))
         ts(R("cj"), R("ci"), 31, A.bitwise_and)
         tt(R("cf"), R("cj"), R("c32", 0, 16), A.add)
@@ -613,10 +682,7 @@ def build(g, core, T, topo):
         for h in H:
             cur[0] = h
             M = "m%d" % h
-            W = R(M, 384, 512)
-            mm([(W, R("W32"), ln("Z", h)), (W, IB(6), ln("q0", h)), (W, R("Fk"), ONE)])
-            tt(ln("f1", h), ln("p1", h), W, A.add)
-            ts(ln("f2", h), ln("f1", h), 5, A.arith_shift_right, V - 1, A.bitwise_and)
+            fallback(h, R(M, 384, 512), ln("f2", h), t)
             Km = R("Kp", 144 * h + 16, 144 * h + 144)
             for j in range(6):
                 here, other = plane(h, 6 + (j & 1)), plane(h, 7 - (j & 1))
@@ -636,21 +702,20 @@ def build(g, core, T, topo):
             dead, eb, om = ln("dA", h, 256 * t), 144 * h, 16 * t + 8 * h
             scan(ln("c1", h), R("d0"), dead, A.add, A.mult)
             cp(R("ee", eb + 16, eb + 144, 16), R("c1", 128 * h + 15, 128 * h + 128, 16), "VA")
-            mm([(R(M, 256, 264), R("ones", 0, 128, p=(0, 1)), R("rows", 256, 264, p=(0, 1)))]
+            mm([(R(M, 256, 264), R("ones", 0, 128, p=(0, 1)), R("rows", p=(0, 1)))]
                + [(R(M, 256, 264), R("ee", eb + 16 - il, eb + 144 - il), R("IB", il, 128, 16)) for il in range(16)])
             ts(R("offm", om, om + 8), R(M, 256, 264), C(12), A.add)
             send(R("offm", om, om + 8), R("offb", om, om + 8), "ro%d" % (2 * t + h), to, 2200.0)
             send(dead, ln("dB", h, 256 * t), "rd%d" % (2 * t + h), to, 2500.0)
             gather(ln("Mb", h), R("xg", 2048 * h, 2048 * h + 2048), R("offm", om, om + 8), alt=FALT)
             keys("xg", "xa%d" % h, h, 0, False)
-            if XT == 1:
-                keys("xg", "b%d" % h, h, 1, False)
-            mm([(W, IB(0), ln("Z", h)), (W, IB(1), ln("Mb", h))])
+            W = R(WB[0] % h, 384, 512)
+            mm([(W, IB(0), ln("Z", h, 256 * t)), (W, IB(1), ln("Mb", h))])
             act(ln("ge", h), W, AF.Sign, bias=C(23))
             mm([(W, R("blk"), ln("ge", h))])
             act(R("TH", 256 * h, 256 * h + 128), W, AF.Relu, bias=-2.0 ** 90, scale=-2.0 ** 89)
             act(R("TH", 256 * h + 128, 256 * h + 256), W, AF.Relu, bias=2.0 ** 91, scale=2.0 ** 89)
-            diffs(ln("Mb", h), "yg", "ya", h, 768 * (2 + h), 2)
+            diffs(ln("Mb", h), "yg", "ya%d" % h, h, 384 * (2 + h))
             P = R("ya%d" % h, 0, 256)
             mm([(P, R("cc", 0, 128, p=(0, 64)), R("ones", p=(0, 64))),
                 (R("ya%d" % h, 0, 256, 2), ln("nf", h, 256 * t), c8("Prm")),
@@ -659,20 +724,18 @@ def build(g, core, T, topo):
         cur[0] = 0
         gather(R("xo"), R("X"), R("offc", 0, 16), alt=FALT)
         for h in H:
-            W = R("m%d" % h, 384, 512)
-            mm([(W, IB(0), ln("xo", h)), (W, IB(0), ln("Mb", h))])
+            W = R(WB[1] % h, 256 if WB[1][0] == "b" else 384, 384 if WB[1][0] == "b" else 512)
+            mm([(W, IB(0 if t < RO - 1 else 1), ln("xo", h)), (W, IB(0), ln("Mb", h))])
             ts(ln("xi", h), W, 0.5, A.mult, C(11), A.subtract)
         if t < RO - 1:
             add("V", lambda e: g.vector.tensor_copy(T.X[:].indirect(T.offc[:, 0:16]), T.xi[:]),
                 [R("xi"), R("offc", 0, 16)], [R("X")], vc(256, 3.8))
-            W = R("m0", 384, 512)
+            W = R(WB[2] % 1, 384, 512)
             mm([(W, ONE, ln("dA", h, 256 * t)) for h in H]
                + [(W, R("ones", 0, 128, p=(0, 1)), R("IB", 128 * 5, 128 * 6, p=(0, 1)))])
             act(R("junk", 0, 128), W, AF.Identity, bias=-32768.0, scale=16.0, acc=R("K16", t + 1, t + 2))
         else:
             for q in range(4):
-                if q % 2 == 0:
-                    tt(ln("xn", q // 2), ln("xi", q // 2), ln("xo", q // 2), A.subtract)
                 fix(q)
             for q in range(2):
                 dma("SA"[q], T.yx[:, 1024 * q:1024 * q + 1024], T.yxs[:, 1024 * q:1024 * q + 1024], [R("yxs")], [], 4000.0)
@@ -680,12 +743,12 @@ def build(g, core, T, topo):
             cur[0] = h
             M, om = "m%d" % h, 16 * t + 8 * h
             gather(ln("Yb", h), R("yg", 2048 * h, 2048 * h + 2048), R("offb", om, om + 8), alt=FALT)
-            order_sum(R(M, 256, 384), 768 * (2 + h), 3, ln("dB", h, 256 * t), R("TH", 256 * h + 128, 256 * h + 256))
-            diffs(ln("Yb", h), "xg", "xa", h, 768 * h, XT)
-            order_sum(R(M, 128, 256), 768 * h, 6 // XT, ln("dA", h, 256 * t), R("TH", 256 * h, 256 * h + 128))
-            W = R(M, 384, 512)
-            mm([(W, IB(0), ln("Z", h)), (W, IB(1), ln("Yb", h))])
-            act(ln("Z" if t < RO - 1 else "zf", h), W, AF.Abs, bias=BIAS)
+            order_sum(R(M, 256, 384), 384 * (2 + h), ln("dB", h, 256 * t), R("TH", 256 * h + 128, 256 * h + 256))
+            diffs(ln("Yb", h), "xg", "xa%d" % h, h, 384 * h)
+            order_sum(R(M, 128, 256), 384 * h, ln("dA", h, 256 * t), R("TH", 256 * h, 256 * h + 128))
+            W = R(WB[3] % h, 384, 512)
+            mm([(W, IB(0), ln("Z", h, 256 * t)), (W, IB(1), ln("Yb", h))])
+            act(ln("Z", h, 256 * t + 256) if t < RO - 1 else ln("zf", h), W, AF.Abs, bias=BIAS)
         if t == RO - 1:
             dma("S", T.yz[:], T.zf[:], [R("zf")], [], 2000.0)
         for h in H:
@@ -702,21 +765,21 @@ def build(g, core, T, topo):
                              (R(b, 0, 256, 2), fB, c8("mG")), (R(b, 1, 256, 2), fA, c8("mG"))]
             mm(tgt(XA), wr=[R(XA)])
             T2 = R("b%d" % h, 0, 256)
+            G = R(M, 384, 512)
+            lo = lambda s, a=0, b=128, st=1: R("va", 256 * h + 128 * s + a, 256 * h + 128 * s + b, st)
+            hi = lambda s, a=0, b=128, st=1: R(YA, 256 + 128 * s + a, 256 + 128 * s + b, st)
             mm(tgt("b%d" % h), stop=False, wr=[R("b%d" % h)])
             act(w2("sg"), Tt, AF.Sign, bias=-8.0)
             mm([(T2, IB(4), w2("sg"))], start=False, wr=[R("b%d" % h)])
             ts(w2("k1"), T2, -0.5, A.add, KM, A.mult)
             mm([(R(YA, 0, 256, 2), kA, c8("D8")), (R(YA, 1, 256, 2), kB, c8("D8"))], start=False, stop=False, wr=[P])
             mm([(P, IB(7), w2("sg"))], start=False)
-            G = R(M, 384, 512)
-            mm([(G, IB(8), ONE), (G, R("blkn"), kA), (G, R("blkn"), kB)])
-            tt(ln("fb", h), ln("f2", h), G, A.min)
-            mm([(O, R("CD"), ONE)], stop=False, wr=[R(XA)])
             ts(w2("k2"), w2("k1"), KMASK, A.bitwise_and)
-            lo = lambda s, a=0, b=128, st=1: R("va", 256 * h + 128 * s + a, 256 * h + 128 * s + b, st)
-            hi = lambda s, a=0, b=128, st=1: R(YA, 256 + 128 * s + a, 256 + 128 * s + b, st)
             tt(lo(0), w2("k2", 0, 128), R(YA, 0, 128), A.add)
             tt(hi(0), w2("k2", 128, 256), R(YA, 128, 256), A.add)
+            mm([(G, IB(8), ONE), (G, R("blkn"), kA), (G, R("blkn"), kB)])
+            tt(ln("fb", h), ln("f2", h), G, A.max)
+            mm([(O, R("CD", p=(0, 2)), R("ones", 0, 128, p=(0, 2)))], stop=False, wr=[R(XA)])
             for st in range(4):
                 s, d = st & 1, 1 - (st & 1)
                 for q, dst in ((0, lo), (1, hi)):
@@ -726,9 +789,9 @@ def build(g, core, T, topo):
                                                                ("fin", 16 * r0 + b3, 16 * r0 + 128, 2), 64, False, False)
                         tt(o, lo(s, 64 * q, 64 * q + 64), hi(s, 64 * q, 64 * q + 64), op)
             fin = lambda L_: (T.fin[:, 16 * h + L_:16 * h + 16:2, :], ("fin", 256 * h, 256 * h + 256, 1), 128, False, False)
-            tt(ln("mg", h), fin(0), fin(1), A.max)
+            tt(ln("mg", h), fin(0), fin(1), A.min)
             mm([(O, ln("mg", h), R("IF"))], start=False)
-            tt(ln("nf", h, 256 * (t + 1)), ln("fb", h), O, A.max)
+            tt(ln("nf", h, 256 * (t + 1)), ln("fb", h), O, A.min)
             if t == RO - 1:
                 mm([(R(M, 0, 128), R("PP"), ln("nf", h, 256 * (t + 1)))])
                 cp(ln("yas", h), R(M, 0, 128), "AV")
@@ -759,12 +822,13 @@ def rank_program(g, core, T, topo):
         for b in o["banks"]:
             need += [j for e2, j in bank.get(b, {}).items() if e2 != e]
             bank.setdefault(b, {})[e] = i
-        want = {}
-        for d in need:
+        for d in sorted(need, key=lambda j: -ops[j]["st"]):
             s, n = ops[d]["sem"], ops[d]["cnt"]
-            want[s] = max(want.get(s, 0), n)
-        for s, n in sorted(want.items()):
-            wait(e, s, n)
+            if seen.get((e, s), 0) < n:
+                wait(e, s, n)
+                for s2, n2 in ops[d].get("knew", ()):
+                    seen[(e, s2)] = max(seen.get((e, s2), 0), n2)
+        o["knew"] = [(s, n) for (e2, s), n in seen.items() if e2 == e]
         ins = o["fn"](e)
         if o["sem"] is None:
             count[e] += 1

@@ -14,14 +14,14 @@ SCRATCH = {
     "ami": _sb(256, I32), "wti": _sb(4, I32), "Z": _sb(768, BF), "zf": _sb(256, F32),
     "nf": _sb(4 * 256, F32), "bn": _sb(3 * 256, F32), "dA": _sb(3 * 256, BF), "dB": _sb(3 * 256, BF),
     "offx": _sb(256, U16), "offy": _sb(256, U16), "offm": _sb(48, U16), "offb": _sb(48, U16),
-    "offc": _sb(32, U16), "D": _sb(256, BF), "q0": _sb(768, BF), "Kp": _sb(288, F32),
+    "offc": _sb(32, U16), "D": _sb(256, BF), "q0": _sb(768, BF), "Kp": _sb(1600, F32),
     "p1": _sb(512, F32), "p2": _sb(512, I32), "p3": _sb(512, I32),
     "f1": _sb(256, I32), "f2": _sb(256, I32), "fb": _sb(256, F32),
-    "tt": _sb(256, F32),
+    "tt": _sb(256, F32), "S": _sb(256, BF),
     "c1": _sb(256, BF), "ee": _sb(288, BF), "sg": _sb(512, BF), "xo": _sb(256, BF),
     "Mb": _sb(256, BF), "Yb": _sb(256, BF), "ge": _sb(256, BF), "TH": _sb(512, BF),
     "fin": ("sbuf", [128, 32, 16], F32), "CD": _sb(128, BF), "K16": _sb(4, F32),
-    "DS": _sb(4 * 384, BF), "keep": _sb(512, BF), "kf": _sb(512, BF),
+    "DS": _sb(6 * 384, BF), "keep": _sb(512, BF), "kf": _sb(512, BF),
     "k1": _sb(512, I32), "k2": _sb(512, I32), "va": _sb(512, F32), "mg": _sb(256, F32), "yas": _sb(256, F32),
     "ci": _sb(16, I32), "cj": _sb(16, I32), "cf": _sb(16, F32), "xs": _sb(256, F32), "xi": _sb(256, I32),
     "junk": _sb(256, F32),
@@ -41,21 +41,26 @@ for _b in PSUM:
 SEMAPHORES = (["eV", "eA", "eP", "eG", "sent"] + ["d%d" % i for i in range(16)]
               + ["%s%d" % (s, i) for s in ("rn", "rd", "ro") for i in range(6)])
 
-CY, PECY, FIX, LAT, GA = 0.95, 0.48, 60.0, 115.0, 1.56
+CY, PECY, FIX, LAT, GA = 0.96, 0.48, 20.0, 155.0, 1.6
 GSPLIT = 2
-GX = (("A", "A"), ("A", "A"))
-GY = (("A", "A"), ("A", "A"))
-GX0 = (("A", "V"), ("A", "AV"))
+GX = (("A", "A", "A", "AV"),) * 2
+GY = (("A", "A", "A", "AV"),) * 2
+GX0 = (("A", "V", "A", "V"), ("A", "A", "AV", "AV"))
 GALT = 600.0
-WB = ("b%d", "m%d", "m%d", "b%d")
-KS, PFIX = 4, 40.0
+WB = ("m%d", "m%d", "m%d", "m%d")
+KS, PFIX, MINC, AX = 4, 40.0, 55, 35.0
 LEAD = 3000.0
 SEED, NOISE = 7, 2500.0
 FALT = 300.0
-LF = 0.8
-SPLITB = False
+LF = 1.05
+XV, XI, AS = 1, 1, 0
+OCC, ORD, XLAT = 0.4, 0, 7000.0
+YS = ("xa%d", 384)
+QP = ((0, 128),)
 PASSES = 20
-MOVES, TEMP, SOFT = 130000, 300.0, 1
+MOVES, MANY, TEMP, SOFT = 170000, 50000, 300.0, 1
+COOL = 0.4
+CASES = ((1.0, 1.0, 1.0, 0.0, AX, LAT), (0.99, 0.98, 1.0, 15.0, 15.0, 150.0), (1.2, 1.15, 1.1, 8.0, 30.0, 150.0))
 SLACK = 700.0
 WIN, WARM = 12000.0, 100
 
@@ -194,8 +199,6 @@ def refine(ops, order, on, x):
     n = len(ops)
     eid = {e: k for k, e in enumerate("VAPGSN")}
     bid = {b: k for k, b in enumerate(PSUM)}
-    cost = [o["cost"] for o in ops]
-    lat = [o["lat"] + LAT for o in ops]
     hard = [[d for d in o["deps"] if d not in o["soft"]] for o in ops]
     soft = [list(o["soft"]) for o in ops]
     deps = [set(o["deps"]) for o in ops]
@@ -215,7 +218,8 @@ def refine(ops, order, on, x):
         anc.append(m)
     ends = [i for i in range(n) if not any(a_ >> i & 1 for a_ in anc)]
 
-    def run(order, on, old=None, a=0, z=0, limit=1e18):
+    def run(case, order, on, old=None, a=0, z=0, limit=1e18):
+        cost, lat, tail, _, LAT, extra = case
         if old is None:
             end, why, held, fin = [0.0] * (n + 1), [n] * n, [False] * n, [0.0] * n
             end[n] = -1e9
@@ -228,6 +232,8 @@ def refine(ops, order, on, x):
             for b in banks[i]:
                 bl[b + e] = i
         k = a - z
+        tick[0] += 1
+        stamp, open_ = tick[0], set()
         for i in order[a:]:
             k += 1
             e = on[i]
@@ -245,16 +251,21 @@ def refine(ops, order, on, x):
                     if end[d] + LAT > t:
                         t, p, q = end[d] + LAT, d, True
                 bl[b + e] = i
-            if e < 5:
-                d = last[e]
-                if end[d] > t:
-                    t, p, q = end[d], d, True
-                last[e] = i
+            d = last[e]
+            if end[d] > t:
+                t, p, q = end[d], d, True
+            last[e] = i
             if k > 1 and t + tail[i] > limit:
                 return None
-            t += cost[i]
+            t += cost[i] + extra[e]
+            if t != end[i] or k < 2:
+                moved[i] = stamp
+                open_.update(succ[i])
+            open_.discard(i)
             end[i], why[i], held[i] = t, p, q
             fin[i] = t + lat[i]
+            if k > 1 and not open_ and not (k & 7) and all(moved[j] != stamp for j in last + bl):
+                break
         i = max(ends, key=lambda j: fin[j])
         top, path = fin[i], []
         while i != n:
@@ -270,14 +281,19 @@ def refine(ops, order, on, x):
         for d in soft[i]:
             ss[d].append(i)
 
-    def tails(order, on, z):
+    pred = [hard[i] + soft[i] for i in range(n)]
+
+    def tails(case, order, on, z, a=0):
+        cost, lat, tail, _, LAT, extra = case
         nxt, bn = [0.0] * 6, [-1e9] * (3 * len(PSUM))
         for i in reversed(order[z + 1:z + 150]):
             e = on[i]
             nxt[e] = tail[i]
             for b in banks[i]:
                 bn[b + e] = tail[i] + LAT
+        k, calm, open_ = z + 1 - a, 0, set()
         for i in reversed(order[:z + 1]):
+            k -= 1
             e = on[i]
             t = -LAT
             for j in hs[i]:
@@ -288,24 +304,48 @@ def refine(ops, order, on, x):
                 v = tail[j] if on[j] == e else tail[j] + lat[i]
                 if v > t:
                     t = v
-            if e < 5 and nxt[e] > t:
+            if nxt[e] > t:
                 t = nxt[e]
             for b in banks[i]:
                 for e2 in others[e]:
                     if bn[b + e2] > t:
                         t = bn[b + e2]
-            t += cost[i]
+            t += cost[i] + extra[e]
+            open_.discard(i)
+            if k >= 0 or abs(t - tail[i]) > 1e-6:
+                calm = 0
+                open_.update(pred[i])
+            else:
+                calm += 1
+                if calm > 60 and not open_:
+                    break
             tail[i] = nxt[e] = t
             for b in banks[i]:
                 bn[b + e] = t + LAT
 
-    tail = [0.0] * n
-    cur = run(order, on)
-    tails(order, on, n)
+    succ = [hs[i] + ss[i] for i in range(n)]
+    moved, tick = [0] * (n + 1), [0]
+    cases = []
+    for (f, fg, fr, fix, ax, wake) in CASES:
+        cases.append(([o["cost"] * (fr if o["eng"] == "N" else f * (fg if o["ga"] else 1.0))
+                       + (fix if o["eng"][0] in "AV" else 0.0) for o in ops],
+                      [o["lat"] * (fr if o["eng"] == "N" else 1.0) + wake for o in ops], [0.0] * n, 1.0 / f,
+                      wake, (0.0, ax, 0.0, 0.0, 0.0, 0.0)))
     took = 0
-    best = (cur[0], cur[1], on, order)
-    for it in range(MOVES):
+    for it in range(MOVES + 1):
+        if it == 0 or it == MOVES - MANY:
+            if it:
+                on, order = best[2], best[3]
+            use = cases[:1] if it < MOVES - MANY else cases
+            curs = [run(c, order, on, None, 0, n) for c in use]
+            for c in use:
+                tails(c, order, on, n)
+            total = sum(r[0] * c[3] for r, c in zip(curs, use)) / len(use)
+            best = (total, curs[0][1], on, order)
+        if it == MOVES:
+            break
         x = (x * 1103515245 + 12345) % 2147483648
+        cur = curs[(x >> 20) % len(use)]
         i = cur[3][(x >> 8) % len(cur[3])]
         p = cur[2][i]
         x = (x * 1103515245 + 12345) % 2147483648
@@ -343,17 +383,27 @@ def refine(ops, order, on, x):
                     continue
                 new = order[:a] + [j for j in mid if j not in take] + [j for j in mid if j in take] + order[b + 1:]
         x = (x * 1103515245 + 12345) % 2147483648
-        limit = cur[0] + TEMP * (1.0 - it / MOVES) * (x / 2147483648.0) ** 2 + 0.01
-        res = run(new, on2, cur, a, b, limit)
-        if res is not None and res[0] <= limit:
-            end = res[1]
-            tails(new, on2, b)
-            order, on, cur = new, on2, res
+        left = COOL * (MOVES - it) / MANY if len(use) > 1 else (MOVES - MANY - it) / (MOVES - MANY)
+        room = (TEMP * left * (x / 2147483648.0) ** 2 + 0.01) * len(use)
+        res = []
+        for k, c in enumerate(use):
+            more = 400.0 if k < len(use) - 1 else 0.0
+            r = run(c, new, on2, curs[k], a, b, curs[k][0] + (room + more) / c[3])
+            if r is None:
+                break
+            room -= (r[0] - curs[k][0]) * c[3]
+            res.append(r)
+        if len(res) == len(use) and room >= 0:
+            for c in use:
+                tails(c, new, on2, b, a)
+            order, on, curs = new, on2, res
+            end, cost, extra = res[0][1], use[0][0], use[0][5]
             took += 1
             if took % 8 == 0:
-                order = sorted(new, key=lambda j: end[j] - cost[j])
-            if res[0] < best[0]:
-                best = (res[0], end, on, order)
+                order = sorted(new, key=lambda j: end[j] - cost[j] - extra[on[j]])
+            total = sum(r[0] * c[3] for r, c in zip(curs, use)) / len(use)
+            if total < best[0]:
+                best = (total, end, on, order)
     return best[0], best[1], ["VAPGSN"[e] for e in best[2]], best[3]
 
 
@@ -379,7 +429,7 @@ def build(g, core, T, topo):
         return len(ops) - 1
 
     def vc(n, f=1.0):
-        return FIX + max(n * f, 32) * CY
+        return FIX + max(n * f, MINC) * CY
 
     def sc(x):
         return x[0] if isinstance(x, tuple) else x
@@ -478,14 +528,15 @@ def build(g, core, T, topo):
 
     nsent = [0]
 
-    def send(src, dst, sem, to, lat):
+    def send(src, dst, sem, to, lat, after=()):
         rid, pid, _ = topo.addr(to)
         mask = topo.mask(core, to)
         ne = len(topo.engines(core, to))
         nsent[0] += ne
         i = add("G", lambda e: g.remote_dma(dst[0], src[0], T.sem[sem], T.sem.sent, pid, rid, mask), [src], [],
-                300.0, sem="-")
-        add("N", None, [], [dst], 1.0, lat=lat, sem=sem, cnt=ne, after=[i])
+                300.0, sem="-", after=after)
+        add("N", None, [], [dst], OCC * lat, lat=lat - OCC * lat / LF, sem=sem, cnt=ne, after=[i])
+        return i
 
     C = lambda j: R("col", j, j + 1)
     PI = lambda j: R("pi", j, j + 1)
@@ -494,7 +545,7 @@ def build(g, core, T, topo):
     dma("S", T.ami[:], T.am[:], [], [R("ami")], 2000.0)
     dma("S", T.Z[:, 0:256], T.zv[:], [], [R("Z", 0, 256)], 2000.0)
     dma("S", T.wti[:, 0:1], T.wt[:], [], [R("wti")], 2000.0)
-    dma("A", T.X[:], T.xt[:], [], [R("X")], 8000.0)
+    dma("A", T.X[:], T.xt[:], [], [R("X")], XLAT / LF)
 
     iota(PI(0), [[0, 1]], 0, 1)
     iota(R("lin"), [[1, 144]])
@@ -589,9 +640,9 @@ def build(g, core, T, topo):
     mm([(R("b0", 0, 128), IB(0), R("tmb", 128 * j, 128 * j + 128)) for j in range(3)])
     cp(c8("Tri"), R("b0", 0, 128), "AV")
     ts(c8("Prm"), R("srev", 128, 256), C(0), A.is_equal)
-    mset(R("tt", 0, 256, 128), -2.0 ** 90)
+    mset(R("tt", 0, 256, 64), -2.0 ** 90)
     mset(R("ee"), 0.0)
-    mset(R("Kp", 15, 288, 144), 0.0)
+    mset(R("Kp", 15, 1600, 400), 0.0)
     cp(R("junk"), R("ami"))
     for h in range(2):
         mm([(R("m%d" % h, 0, 128), R("PP"), R("junk", 128 * h, 128 * h + 128))])
@@ -603,11 +654,13 @@ def build(g, core, T, topo):
         return R(("xa%d", "b%d")[j & 1] % h, 128 * (j >> 1) + lo, 128 * (j >> 1) + hi)
 
     def offsets(src, off, M, c, tmp, h, t):
-        ts(c, src, 16.5, A.mult, R("K16", t, t + 1), A.add)
-        tt(R("p1", tmp, tmp + 128), src, R(M, 128, 256), A.mult)
-        tt(R("p2", tmp, tmp + 128), R("p1", tmp, tmp + 128), c, A.add)
-        ts(R("p3", tmp, tmp + 128), R("p2", tmp, tmp + 128), 4, A.arith_shift_right, V - 1, A.bitwise_and)
-        cp(R(off, 128 * h, 128 * h + 128), R("p3", tmp, tmp + 128))
+        for a, b in (QP if off == "offx" and t else ((0, 128),)):
+            sub = lambda x: R(x[1][0], x[1][1] + a, x[1][1] + b)
+            ts(sub(c), sub(src), 16.5, A.mult, R("K16", t, t + 1), A.add)
+            tt(R("p1", tmp + a, tmp + b), sub(src), R(M, 128 + a, 128 + b), A.mult)
+            tt(R("p2", tmp + a, tmp + b), R("p1", tmp + a, tmp + b), sub(c), A.add)
+            ts(R("p3", tmp + a, tmp + b), R("p2", tmp + a, tmp + b), 4, A.arith_shift_right, V - 1, A.bitwise_and)
+            cp(R(off, 128 * h + a, 128 * h + b), R("p3", tmp + a, tmp + b))
 
     def fallback(h, W, out, t):
         hl = lambda nm, b=0: R(nm, b + 128 * h, b + 128 * h + 128)
@@ -640,9 +693,16 @@ def build(g, core, T, topo):
         add("V", lambda e: g.vector.tensor_copy(T.yxs[:].indirect(off), a[0]),
             [a, R("offc", 16, 32)], [R("yxs")], vc(64, 3.8))
 
-    def order_sum(out, ds, dead, th):
+    ysum = lambda h: R(YS[0] % h, YS[1], YS[1] + 128)
+
+    def flags(h, a, sm):
+        w = lambda nm: R(nm, 256 * h + a, 256 * h + a + 128)
+        act(w("keep"), sm, AF.Sign, bias=2.0 ** -84)
+        tt(w("kf"), sm, w("TH"), A.is_ge)
+
+    def order_sum(out, ds, dead, th, n=3):
         mm([(out, IB(3), th), (out, dead, IB(2))]
-           + [(out, R("DS", ds + 128 * j, ds + 128 * j + 128), IB(0)) for j in range(3)])
+           + [(out, R("DS", ds + 128 * j, ds + 128 * j + 128), IB(0)) for j in range(n)])
 
     for t in range(RO):
         to = T.cores[(rank + 1 + t % (N - 1)) % N]
@@ -683,20 +743,35 @@ def build(g, core, T, topo):
             cur[0] = h
             M = "m%d" % h
             fallback(h, R(M, 384, 512), ln("f2", h), t)
-            Km = R("Kp", 144 * h + 16, 144 * h + 144)
-            for j in range(6):
+            kp = lambda j, d=0: R("Kp", 800 * h + 400 * (j & 1) + 128 * (j >> 1) + 16 - d,
+                                  800 * h + 400 * (j & 1) + 128 * (j >> 1) + 144 - d)
+            if XV:
+                cp(kp(0), plane(h, 0), "AV")
+            for j in range(6 if AS else 0):
+                for c in range(0, 128, 128 // AS):
+                    e_ = c + 128 // AS
+                    sb = lambda nm, a=0, b=0: R(nm, b + 128 * h + c + a, b + 128 * h + e_)
+                    scan(sb("tt", 1), plane(h, j, c, e_ - 1), R("seg", c + 1, e_) if j == 0 else sb("S", 1),
+                         A.max, A.min, -2.0 ** 90)
+                    if j < 5:
+                        tt(sb("D"), plane(h, j, c, e_), sb("tt"), A.subtract)
+                        tt(sb("S"), sb("tt"), plane(h, j, c, e_), A.subtract)
+                        tt(plane(h, j + 1, c, e_), plane(h, j + 1, c, e_), sb("D"), A.min)
+                    else:
+                        tt(sb("dA", 0, 256 * t), plane(h, j, c, e_), sb("tt"), A.is_lt)
+            for j in range(0 if AS else 6):
                 here, other = plane(h, 6 + (j & 1)), plane(h, 7 - (j & 1))
                 if j == 0:
                     Kj, Tj = plane(h, 0), ln("tt", h)
                     scan(R("tt", 128 * h + 1, 128 * h + 128), plane(h, 0, 0, 127), R("seg", 1, 128), A.max, A.min,
                          -2.0 ** 90)
                 else:
-                    Kj, Tj = Km, here
-                    scan(Tj, R("Kp", 144 * h + 15, 144 * h + 143), other, A.max, A.min, -2.0 ** 90)
+                    Kj, Tj = kp(j if XV else 1), here
+                    scan(Tj, kp(j if XV else 1, 1), other, A.max, A.min, -2.0 ** 90)
                 if j < 5:
                     tt(ln("D", h), Kj, Tj, A.subtract)
                     mm([(here, IB(1), ln("D", h))])
-                    tt(Km, plane(h, j + 1), ln("D", h), A.min)
+                    tt(kp(j + 1 if XV else 1), plane(h, j + 1), ln("D", h), A.min)
                 else:
                     tt(ln("dA", h, 256 * t), Kj, Tj, A.is_lt)
             dead, eb, om = ln("dA", h, 256 * t), 144 * h, 16 * t + 8 * h
@@ -705,25 +780,32 @@ def build(g, core, T, topo):
             mm([(R(M, 256, 264), R("ones", 0, 128, p=(0, 1)), R("rows", p=(0, 1)))]
                + [(R(M, 256, 264), R("ee", eb + 16 - il, eb + 144 - il), R("IB", il, 128, 16)) for il in range(16)])
             ts(R("offm", om, om + 8), R(M, 256, 264), C(12), A.add)
-            send(R("offm", om, om + 8), R("offb", om, om + 8), "ro%d" % (2 * t + h), to, 2200.0)
-            send(dead, ln("dB", h, 256 * t), "rd%d" % (2 * t + h), to, 2500.0)
+            first = send(R("offm", om, om + 8), R("offb", om, om + 8), "ro%d" % (2 * t + h), to, 2200.0)
+            send(dead, ln("dB", h, 256 * t), "rd%d" % (2 * t + h), to, 2500.0, [first] if ORD else [])
             gather(ln("Mb", h), R("xg", 2048 * h, 2048 * h + 2048), R("offm", om, om + 8), alt=FALT)
-            keys("xg", "xa%d" % h, h, 0, False)
+            if not XV:
+                keys("xg", "xa%d" % h, h, 0, False)
             W = R(WB[0] % h, 384, 512)
             mm([(W, IB(0), ln("Z", h, 256 * t)), (W, IB(1), ln("Mb", h))])
             act(ln("ge", h), W, AF.Sign, bias=C(23))
             mm([(W, R("blk"), ln("ge", h))])
             act(R("TH", 256 * h, 256 * h + 128), W, AF.Relu, bias=-2.0 ** 90, scale=-2.0 ** 89)
             act(R("TH", 256 * h + 128, 256 * h + 256), W, AF.Relu, bias=2.0 ** 91, scale=2.0 ** 89)
-            diffs(ln("Mb", h), "yg", "ya%d" % h, h, 384 * (2 + h))
+            diffs(ln("Mb", h), "yg", "ya%d" % h, h, 384 * (4 + h))
             P = R("ya%d" % h, 0, 256)
             mm([(P, R("cc", 0, 128, p=(0, 64)), R("ones", p=(0, 64))),
                 (R("ya%d" % h, 0, 256, 2), ln("nf", h, 256 * t), c8("Prm")),
                 (R("ya%d" % h, 1, 256, 2), ln("bn", h, 256 * t), c8("Prm"))], stop=False,
                wr=[R("ya%d" % h)])
         cur[0] = 0
-        gather(R("xo"), R("X"), R("offc", 0, 16), alt=FALT)
-        for h in H:
+        if XI:
+            op = A.add if t < RO - 1 else A.subtract
+            add("V", lambda e, op=op: g.vector.tensor_tensor(T.junk[:], T.X[:].indirect(T.offc[:, 0:16]), T.Mb[:], op),
+                [R("X"), R("offc", 0, 16), R("Mb")], [R("junk")], vc(256, GA))
+            ts(R("xi"), R("junk"), 0.5 if t < RO - 1 else -0.5, A.mult, C(11), A.subtract)
+        else:
+            gather(R("xo"), R("X"), R("offc", 0, 16), alt=FALT)
+        for h in (() if XI else H):
             W = R(WB[1] % h, 256 if WB[1][0] == "b" else 384, 384 if WB[1][0] == "b" else 512)
             mm([(W, IB(0 if t < RO - 1 else 1), ln("xo", h)), (W, IB(0), ln("Mb", h))])
             ts(ln("xi", h), W, 0.5, A.mult, C(11), A.subtract)
@@ -733,7 +815,7 @@ def build(g, core, T, topo):
             W = R(WB[2] % 1, 384, 512)
             mm([(W, ONE, ln("dA", h, 256 * t)) for h in H]
                + [(W, R("ones", 0, 128, p=(0, 1)), R("IB", 128 * 5, 128 * 6, p=(0, 1)))])
-            act(R("junk", 0, 128), W, AF.Identity, bias=-32768.0, scale=16.0, acc=R("K16", t + 1, t + 2))
+            act(R("xs", 0, 128), W, AF.Identity, bias=-32768.0, scale=16.0, acc=R("K16", t + 1, t + 2))
         else:
             for q in range(4):
                 fix(q)
@@ -743,9 +825,16 @@ def build(g, core, T, topo):
             cur[0] = h
             M, om = "m%d" % h, 16 * t + 8 * h
             gather(ln("Yb", h), R("yg", 2048 * h, 2048 * h + 2048), R("offb", om, om + 8), alt=FALT)
-            order_sum(R(M, 256, 384), 384 * (2 + h), ln("dB", h, 256 * t), R("TH", 256 * h + 128, 256 * h + 256))
-            diffs(ln("Yb", h), "xg", "xa%d" % h, h, 384 * h)
-            order_sum(R(M, 128, 256), 384 * h, ln("dA", h, 256 * t), R("TH", 256 * h, 256 * h + 128))
+            order_sum(ysum(h), 384 * (4 + h), ln("dB", h, 256 * t), R("TH", 256 * h + 128, 256 * h + 256))
+            flags(h, 128, ysum(h))
+            if XV:
+                for q in range(2):
+                    pv, a = plane(h, q, 0, 384), 800 * h + 400 * q + 16
+                    mm([(pv, ln("Yb", h), R("Wrep", 384 * q, 384 * q + 384))])
+                    tt(R("DS", 768 * h + 384 * q, 768 * h + 384 * q + 384), R("Kp", a, a + 384), pv, A.add)
+            else:
+                diffs(ln("Yb", h), "xg", "xa%d" % h, h, 768 * h)
+            order_sum(R(M, 128, 256), 768 * h, ln("dA", h, 256 * t), R("TH", 256 * h, 256 * h + 128), 6 if XV else 3)
             W = R(WB[3] % h, 384, 512)
             mm([(W, IB(0), ln("Z", h, 256 * t)), (W, IB(1), ln("Yb", h))])
             act(ln("Z", h, 256 * t + 256) if t < RO - 1 else ln("zf", h), W, AF.Abs, bias=BIAS)
@@ -755,9 +844,7 @@ def build(g, core, T, topo):
             cur[0] = h
             M = "m%d" % h
             w2 = lambda nm, lo=0, hi=256, st=1: R(nm, 256 * h + lo, 256 * h + hi, st)
-            for a_, b_ in (((128, 256), (0, 128)) if SPLITB else ((0, 256),)):
-                act(w2("keep", a_, b_), R(M, 128 + a_, 128 + b_), AF.Sign, bias=2.0 ** -84)
-                tt(w2("kf", a_, b_), R(M, 128 + a_, 128 + b_), w2("TH", a_, b_), A.is_ge)
+            flags(h, 0, R(M, 128, 256))
             XA, YA = "xa%d" % h, "ya%d" % h
             Tt, P, O = R(XA, 0, 256), R(YA, 0, 256), R(XA, 256, 384)
             kA, kB, fA, fB = w2("keep", 0, 128), w2("keep", 128, 256), w2("kf", 0, 128), w2("kf", 128, 256)
@@ -818,7 +905,7 @@ def rank_program(g, core, T, topo):
         e = o["on"]
         if e == "N":
             continue
-        need = [d for d in o["deps"] if d not in o["soft"] or ops[d]["on"] != e]
+        need = [d for d in o["deps"] if (d not in o["soft"] or ops[d]["on"] != e) and ops[d]["sem"] != "-"]
         for b in o["banks"]:
             need += [j for e2, j in bank.get(b, {}).items() if e2 != e]
             bank.setdefault(b, {})[e] = i

from concourse.bass import DstId, RemoteDMATransfer
from concourse.mybir import dt, AluOpType, AxisListType, ActivationFunctionType

V, L, RO, N = 8192, 256, 3, 4
F32, BF, I32, U16 = "float32", "bfloat16", "int32", "uint16"


def _sb(n, d):
    return ("sbuf", [128, n], d)


SCRATCH = {
    "X": _sb(V, BF), "xg": _sb(4096, BF), "yg": _sb(4096, BF), "yxs": _sb(2048, F32),
    "ami": _sb(256, I32), "wti": _sb(4, I32), "Z": _sb(768, BF), "zf": _sb(256, F32),
    "nf": _sb(4 * 256, F32), "bn": _sb(3 * 256, F32), "dA": _sb(3 * 256, BF), "dB": _sb(3 * 256, BF),
    "offx": _sb(256, U16), "offy": _sb(256, U16), "offm": _sb(48, U16), "offb": _sb(48, U16),
    "offc": _sb(32, U16), "D": _sb(256, BF), "q0": _sb(768, BF), "Kp": _sb(1600, F32),
    "p1": _sb(512, F32), "p2": _sb(512, I32), "p3": _sb(512, I32),
    "f1": _sb(256, I32), "f2": _sb(256, I32), "fb": _sb(256, F32),
    "tt": _sb(256, F32), "S": _sb(256, BF),
    "c1": _sb(256, BF), "ee": _sb(288, BF), "sg": _sb(512, BF), "xo": _sb(256, BF),
    "Mb": _sb(256, BF), "Yb": _sb(256, BF), "ge": _sb(256, BF), "TH": _sb(512, BF),
    "fin": ("sbuf", [128, 32, 16], F32), "CD": _sb(128, BF), "K16": _sb(4, F32),
    "DS": _sb(6 * 384, BF), "keep": _sb(512, BF), "kf": _sb(512, BF),
    "k1": _sb(512, I32), "k2": _sb(512, I32), "va": _sb(512, F32), "mg": _sb(256, F32), "yas": _sb(256, F32),
    "ci": _sb(16, I32), "cj": _sb(16, I32), "cf": _sb(16, F32), "xs": _sb(256, F32), "xi": _sb(256, I32),
    "junk": _sb(256, F32),
    "lin": _sb(144, BF), "idq": _sb(768, BF), "srev": _sb(256, BF), "gl": _sb(128, BF),
    "pi": _sb(16, I32), "col": _sb(32, F32), "c32": _sb(32, F32), "cb": _sb(8, BF),
    "W32": _sb(128, BF), "Fk": _sb(128, BF), "blkn": _sb(128, BF),
    "IB": _sb(9 * 128, BF), "IF": _sb(128, F32), "PP": _sb(128, F32), "Wrep": _sb(768, BF), "Wk": _sb(48, BF),
    "blk": _sb(128, BF), "Wblk": _sb(128, BF), "Wband": _sb(144, BF), "diag": _sb(16, BF), "seg": _sb(128, BF),
    "d0": _sb(128, BF), "ones": _sb(256, BF), "cc": _sb(256, BF), "rows": _sb(8, BF),
    "mG": _sb(128, BF), "Tri": _sb(128, BF), "D8": _sb(128, BF), "Prm": _sb(128, F32),
    "tmp": _sb(16, F32), "tmb": _sb(384, BF),
}
PSUM = ("xa0", "xa1", "b0", "ya0", "ya1", "b1", "m0", "m1")
for _b in PSUM:
    SCRATCH[_b] = ("psum", [128, 512], F32)

SEMAPHORES = (["eV", "eA", "eP", "eG", "sent"] + ["d%d" % i for i in range(16)]
              + ["%s%d" % (s, i) for s in ("rn", "rd", "ro") for i in range(6)])

CY, PECY, FIX, LAT, GA = 0.96, 0.48, 20.0, 155.0, 1.6
GSPLIT = 2
GX = (("A", "A", "A", "AV"),) * 2
GY = (("A", "A", "A", "AV"),) * 2
GX0 = (("A", "V", "A", "V"), ("A", "A", "AV", "AV"))
GALT = 600.0
WB = ("m%d", "m%d", "m%d", "m%d")
KS, PFIX, MINC, AX = 4, 40.0, 55, 35.0
LEAD = 3000.0
SEED, NOISE = 7, 2500.0
FALT = 300.0
LF = 1.05
XV, XI, AS = 1, 1, 0
OCC, ORD, XLAT = 0.4, 0, 7000.0
YS = ("xa%d", 384)
QP = ((0, 128),)
PASSES = 20
MOVES, MANY, TEMP, SOFT = 170000, 50000, 300.0, 1
COOL = 0.4
CASES = ((1.0, 1.0, 1.0, 0.0, AX, LAT), (0.99, 0.98, 1.0, 15.0, 15.0, 150.0), (1.2, 1.15, 1.1, 8.0, 30.0, 150.0))
SLACK = 700.0
WIN, WARM = 12000.0, 100


def meets(x, y):
    if x[1] <= y[0] or y[1] <= x[0]:
        return False
    return not (x[2] == y[2] and x[2] > 1 and x[0] % x[2] != y[0] % y[2])


def brev(x):
    return ((x & 1) << 3) | ((x & 2) << 1) | ((x & 4) >> 1) | ((x & 8) >> 3)


ORDER = {}


def plan_order(ops, memo):
    hist = {}
    for i, o in enumerate(ops):
        deps = set(o["after"])
        for x in o["r"]:
            for (j, w, y) in hist.get(x[0], []):
                if w and meets(x[1:], y):
                    deps.add(j)
        raw = set(deps)
        for x in o["w"]:
            for (j, w, y) in hist.get(x[0], []):
                if meets(x[1:], y):
                    deps.add(j)
        o["soft"] = set(j for j in deps - raw if (ops[j]["eng"] == "P" and o["eng"] == "P" and (o["cont"] or SOFT > 1))
                        or (SOFT > 2 and ops[j]["sem"] is None and o["sem"] is None))
        for x in o["w"]:
            hist[x[0]] = [e for e in hist.get(x[0], [])
                          if not (x[1] <= e[2][0] and e[2][1] <= x[2] and (x[3] == 1 or x[1:] == e[2]))]
        for x in o["r"]:
            hist.setdefault(x[0], []).append((i, False, x[1:]))
        for x in o["w"]:
            hist.setdefault(x[0], []).append((i, True, x[1:]))
        deps.discard(i)
        o["deps"] = sorted(deps)
        o["banks"] = sorted(set(x[0] for x in o["r"] + o["w"] if x[0] in PSUM))
    n = len(ops)
    succ = [[] for _ in range(n)]
    for i, o in enumerate(ops):
        for d in o["deps"]:
            succ[d].append(i)
    pr = [0.0] * n
    for i in range(n - 1, -1, -1):
        pr[i] = ops[i]["cost"] + ops[i]["lat"] + max([LAT + pr[s] for s in succ[i]] + [0.0])
    x = SEED
    for i in range(n):
        x = (x * 1103515245 + 12345) % 2147483648
        pr[i] += NOISE * (x / 2147483648.0) - LEAD * ops[i]["half"]
    pred = [o["deps"] for o in ops]

    def tail(lst, t):
        k = len(lst)
        while k and lst[k - 1][1] > t:
            k -= 1
        return lst[k:]

    def put(lst, v):
        k = len(lst)
        while k and lst[k - 1][0] > v[0]:
            k -= 1
        lst.insert(k, v)

    def place(pred, succ, pr, back):
        left = [len(p) for p in pred]
        ready = [i for i in range(n) if left[i] == 0]
        end, on, busy = [0.0] * n, [None] * n, {}
        while ready:
            i = max(ready, key=lambda j: pr[j])
            o = ops[i]
            c = o["cost"]
            if back:
                t0 = max([end[d] + LAT for d in pred[i]] + [0.0]) + o["lat"]
            else:
                t0 = max([end[d] + ops[d]["lat"] + LAT for d in pred[i]] + [0.0])
            best = None
            for e in o["eng"]:
                iv = tail(busy.get(e, []), t0)
                if o["banks"]:
                    for b in o["banks"]:
                        iv = iv + [(a - LAT, z + LAT) for (a, z, e2) in tail(busy.get(b, []), t0 - LAT) if e2 != e]
                    iv.sort()
                st = t0
                for (a, z) in iv:
                    if a >= st + c:
                        break
                    st = max(st, z)
                key = st + (0.0 if e == o["eng"][0] else o["alt"])
                if best is None or key < best[0]:
                    best = (key, e, st)
            _, e, st = best
            on[i], end[i] = e, st + c
            put(busy.setdefault(e, []), (st, st + c))
            for b in o["banks"]:
                put(busy.setdefault(b, []), (st, st + c, e))
            ready.remove(i)
            for s in succ[i]:
                left[s] -= 1
                if left[s] == 0:
                    ready.append(s)
        return end, on

    best = memo.get("best")
    for it in range(0 if best else PASSES):
        end, on = place(pred, succ, pr, False)
        span = max(end[i] + ops[i]["lat"] for i in range(n))
        if best is None or span <= best[0] + SLACK * (1.0 - it / PASSES):
            cur = (span, end, on)
            if best is None or span < best[0]:
                best = cur
        back = []
        x = (x * 1103515245 + 12345) % 2147483648
        w0 = (x / 2147483648.0) * (cur[0] + WIN) - WIN
        for i in range(n):
            x = (x * 1103515245 + 12345) % 2147483648
            z = NOISE * (x / 2147483648.0 - 0.5) if it < WARM or w0 <= cur[1][i] <= w0 + WIN else 0.0
            back.append(cur[1][i] + ops[i]["lat"] + z)
        pr, _ = place(succ, pred, back, True)
    if "best" not in memo:
        span, end, on = best
        order = sorted(range(n), key=lambda j: (end[j] - ops[j]["cost"], j))
        best = refine(ops, order, list(on), x)
    memo["best"] = best
    span, end, on, order = best
    for i, o in enumerate(ops):
        o["on"], o["st"] = on[i], end[i] - o["cost"]
    return order, span


def refine(ops, order, on, x):
    n = len(ops)
    eid = {e: k for k, e in enumerate("VAPGSN")}
    bid = {b: k for k, b in enumerate(PSUM)}
    hard = [[d for d in o["deps"] if d not in o["soft"]] for o in ops]
    soft = [list(o["soft"]) for o in ops]
    deps = [set(o["deps"]) for o in ops]
    banks = [[3 * bid[b] for b in o["banks"]] for o in ops]
    engs = [[eid[e] for e in o["eng"]] for o in ops]
    on = [eid[e] for e in on]
    others = ((1, 2), (0, 2), (0, 1))

    anc = []
    for i in range(n):
        m = 0
        for d in deps[i]:
            m |= anc[d]
        hard[i] = [d for d in hard[i] if not (m >> d & 1) or ops[d]["lat"] > 0]
        for d in deps[i]:
            m |= 1 << d
        anc.append(m)
    ends = [i for i in range(n) if not any(a_ >> i & 1 for a_ in anc)]

    def run(case, order, on, old=None, a=0, z=0, limit=1e18):
        cost, lat, tail, _, LAT, extra = case
        if old is None:
            end, why, held, fin = [0.0] * (n + 1), [n] * n, [False] * n, [0.0] * n
            end[n] = -1e9
        else:
            end, why, held, fin = old[1][:], old[2][:], old[4][:], old[5][:]
        last, bl = [n] * 6, [n] * (3 * len(PSUM))
        for i in order[max(0, a - 150):a]:
            e = on[i]
            last[e] = i
            for b in banks[i]:
                bl[b + e] = i
        k = a - z
        tick[0] += 1
        stamp, open_ = tick[0], set()
        for i in order[a:]:
            k += 1
            e = on[i]
            t, p, q = 0.0, n, False
            for d in hard[i]:
                if fin[d] > t:
                    t, p = fin[d], d
            for d in soft[i]:
                v = end[d] if on[d] == e else fin[d]
                if v > t:
                    t, p = v, d
            for b in banks[i]:
                for e2 in others[e]:
                    d = bl[b + e2]
                    if end[d] + LAT > t:
                        t, p, q = end[d] + LAT, d, True
                bl[b + e] = i
            d = last[e]
            if end[d] > t:
                t, p, q = end[d], d, True
            last[e] = i
            if k > 1 and t + tail[i] > limit:
                return None
            t += cost[i] + extra[e]
            if t != end[i] or k < 2:
                moved[i] = stamp
                open_.update(succ[i])
            open_.discard(i)
            end[i], why[i], held[i] = t, p, q
            fin[i] = t + lat[i]
            if k > 1 and not open_ and not (k & 7) and all(moved[j] != stamp for j in last + bl):
                break
        i = max(ends, key=lambda j: fin[j])
        top, path = fin[i], []
        while i != n:
            if held[i]:
                path.append(i)
            i = why[i]
        return top - LAT, end, why, path, held, fin

    hs, ss = [[] for _ in range(n)], [[] for _ in range(n)]
    for i in range(n):
        for d in hard[i]:
            hs[d].append(i)
        for d in soft[i]:
            ss[d].append(i)

    pred = [hard[i] + soft[i] for i in range(n)]

    def tails(case, order, on, z, a=0):
        cost, lat, tail, _, LAT, extra = case
        nxt, bn = [0.0] * 6, [-1e9] * (3 * len(PSUM))
        for i in reversed(order[z + 1:z + 150]):
            e = on[i]
            nxt[e] = tail[i]
            for b in banks[i]:
                bn[b + e] = tail[i] + LAT
        k, calm, open_ = z + 1 - a, 0, set()
        for i in reversed(order[:z + 1]):
            k -= 1
            e = on[i]
            t = -LAT
            for j in hs[i]:
                if tail[j] > t:
                    t = tail[j]
            t += lat[i]
            for j in ss[i]:
                v = tail[j] if on[j] == e else tail[j] + lat[i]
                if v > t:
                    t = v
            if nxt[e] > t:
                t = nxt[e]
            for b in banks[i]:
                for e2 in others[e]:
                    if bn[b + e2] > t:
                        t = bn[b + e2]
            t += cost[i] + extra[e]
            open_.discard(i)
            if k >= 0 or abs(t - tail[i]) > 1e-6:
                calm = 0
                open_.update(pred[i])
            else:
                calm += 1
                if calm > 60 and not open_:
                    break
            tail[i] = nxt[e] = t
            for b in banks[i]:
                bn[b + e] = t + LAT

    succ = [hs[i] + ss[i] for i in range(n)]
    moved, tick = [0] * (n + 1), [0]
    cases = []
    for (f, fg, fr, fix, ax, wake) in CASES:
        cases.append(([o["cost"] * (fr if o["eng"] == "N" else f * (fg if o["ga"] else 1.0))
                       + (fix if o["eng"][0] in "AV" else 0.0) for o in ops],
                      [o["lat"] * (fr if o["eng"] == "N" else 1.0) + wake for o in ops], [0.0] * n, 1.0 / f,
                      wake, (0.0, ax, 0.0, 0.0, 0.0, 0.0)))
    took = 0
    for it in range(MOVES + 1):
        if it == 0 or it == MOVES - MANY:
            if it:
                on, order = best[2], best[3]
            use = cases[:1] if it < MOVES - MANY else cases
            curs = [run(c, order, on, None, 0, n) for c in use]
            for c in use:
                tails(c, order, on, n)
            total = sum(r[0] * c[3] for r, c in zip(curs, use)) / len(use)
            best = (total, curs[0][1], on, order)
        if it == MOVES:
            break
        x = (x * 1103515245 + 12345) % 2147483648
        cur = curs[(x >> 20) % len(use)]
        i = cur[3][(x >> 8) % len(cur[3])]
        p = cur[2][i]
        x = (x * 1103515245 + 12345) % 2147483648
        kind = (x >> 8) % 8
        on2, new = on, order
        if kind == 0 and (len(engs[i]) > 1 or len(engs[p]) > 1):
            j = i if len(engs[i]) > 1 and (len(engs[p]) == 1 or x & 64) else p
            on2 = list(on)
            on2[j] = engs[j][0] if on[j] != engs[j][0] else engs[j][1]
            a = b = order.index(j)
        else:
            a, b = order.index(p), order.index(i)
            x = (x * 1103515245 + 12345) % 2147483648
            far = ((x >> 8) % 24) if kind > 4 else 0
            if kind & 1:
                a = max(0, a - far)
                mid = order[a:b + 1]
                take = {i}
                need = set(deps[i])
                for j in reversed(mid[:-1]):
                    if j in need:
                        take.add(j)
                        need |= deps[j]
                if p in take:
                    continue
                new = order[:a] + [j for j in mid if j in take] + [j for j in mid if j not in take] + order[b + 1:]
            else:
                b = min(n - 1, b + far)
                mid = order[a:b + 1]
                take = {p}
                for j in mid[1:]:
                    if deps[j] & take:
                        take.add(j)
                if i in take:
                    continue
                new = order[:a] + [j for j in mid if j not in take] + [j for j in mid if j in take] + order[b + 1:]
        x = (x * 1103515245 + 12345) % 2147483648
        left = COOL * (MOVES - it) / MANY if len(use) > 1 else (MOVES - MANY - it) / (MOVES - MANY)
        room = (TEMP * left * (x / 2147483648.0) ** 2 + 0.01) * len(use)
        res = []
        for k, c in enumerate(use):
            more = 400.0 if k < len(use) - 1 else 0.0
            r = run(c, new, on2, curs[k], a, b, curs[k][0] + (room + more) / c[3])
            if r is None:
                break
            room -= (r[0] - curs[k][0]) * c[3]
            res.append(r)
        if len(res) == len(use) and room >= 0:
            for c in use:
                tails(c, new, on2, b, a)
            order, on, curs = new, on2, res
            end, cost, extra = res[0][1], use[0][0], use[0][5]
            took += 1
            if took % 8 == 0:
                order = sorted(new, key=lambda j: end[j] - cost[j] - extra[on[j]])
            total = sum(r[0] * c[3] for r, c in zip(curs, use)) / len(use)
            if total < best[0]:
                best = (total, end, on, order)
    return best[0], best[1], ["VAPGSN"[e] for e in best[2]], best[3]


def build(g, core, T, topo):
    rank = T.rank_of(core)
    A, AF = AluOpType, ActivationFunctionType
    Q = {"V": g.vector, "A": g.scalar, "P": g.tensor, "G": g, "S": g.sync}
    ops = []
    ndma = [0]
    cur = [0]

    def R(nm, lo=0, hi=None, step=1, p=None):
        if hi is None:
            hi = SCRATCH[nm][1][1]
        t = T[nm]
        ap = t[:, lo:hi:step] if p is None else t[p[0]:p[1], lo:hi:step]
        return (ap, (nm, lo, hi, step), len(range(lo, hi, step)), SCRATCH[nm][2] in (BF, U16), nm in PSUM)

    def add(eng, fn, r, w, cost, lat=0.0, sem=None, cnt=0, after=(), alt=0.0, cont=False):
        ops.append({"eng": eng, "cont": cont, "fn": fn, "r": [x[1] for x in r], "w": [x[1] for x in w], "cost": cost, "lat": lat * LF,
                    "ga": any(x[1][0] in ("offx", "offy") for x in r),
                    "sem": sem, "cnt": cnt, "after": list(after), "alt": alt, "half": cur[0]})
        return len(ops) - 1

    def vc(n, f=1.0):
        return FIX + max(n * f, MINC) * CY

    def sc(x):
        return x[0] if isinstance(x, tuple) else x

    def tup(*xs):
        return [x for x in xs if isinstance(x, tuple)]

    def ts(o, i, s1, op0, s2=None, op1=None):
        fl = all(SCRATCH[x[1][0]][2] in (F32, BF) for x in (o, i))
        affine = fl and ((op0 == A.mult and (op1 is None or op1 == A.add)) or (op0 == A.add and op1 is None))

        def fn(e):
            if e == "A":
                if op0 == A.add:
                    return g.scalar.activation(o[0], i[0], AF.Identity, bias=sc(s1))
                return g.scalar.activation(o[0], i[0], AF.Identity, bias=0.0 if op1 is None else sc(s2), scale=sc(s1))
            if op1 is None:
                return g.vector.tensor_scalar(o[0], i[0], sc(s1), None, op0)
            return g.vector.tensor_scalar(o[0], i[0], sc(s1), sc(s2), op0, op1)
        return add("AV" if affine else "V", fn, tup(i, s1, s2), [o], vc(i[2], 0.5 if o[3] and i[3] else 1.0), alt=FALT)

    def tt(o, a, b, op):
        return add("V", lambda e: g.vector.tensor_tensor(o[0], a[0], b[0], op), [a, b], [o],
                   vc(a[2], 1.0 if a[4] or b[4] else 2.0))

    def cp(o, i, eng="V"):
        def fn(e):
            if e == "A":
                return g.scalar.activation(o[0], i[0], AF.Identity)
            return g.vector.tensor_copy(o[0], i[0])
        return add(eng, fn, [i], [o], vc(i[2]), alt=FALT if eng == "AV" else 0.0)

    def scan(o, a, b, op0, op1, init=0.0):
        return add("V", lambda e: g.vector.tensor_tensor_scan(o[0], a[0], b[0], init, op0, op1), [a, b], [o],
                   vc(a[2], 0.5 if o[3] and a[3] and b[3] else 1.0))

    def act(o, i, func, bias=0.0, scale=1.0, acc=None):
        def fn(e):
            if acc is None:
                return g.scalar.activation(o[0], i[0], func, bias=sc(bias), scale=scale)
            return g.scalar.activation(o[0], i[0], func, bias=sc(bias), scale=scale, accum_out=acc[0])
        return add("A", fn, tup(i, bias), tup(o, acc), vc(i[2]))

    def mset(o, c):
        return add("V", lambda e: g.vector.memset(o[0], c), [], [o], vc(o[2], 0.5 if o[3] else 1.0))

    def iota(o, pat, base=0, cm=0):
        def fn(e):
            if SCRATCH[o[1][0]][2] == I32:
                return g.iota(o[0], pat, base, cm)
            return g.iota(o[0], pat, base, cm, allow_small_or_imprecise_dtypes=True)
        return add("G", fn, [], [o], 150 + 2 * o[2] * CY)

    def mm(lst, start=True, stop=True, wr=None, after=()):
        cyc = [max(64, r[2]) * (1 if r[3] else 4) for (o, l, r) in lst]
        if len(lst) > 1 and sum(cyc) > 64 * KS + 128:
            k = 1
            while sum(cyc[:k + 1]) <= 64 * KS:
                k += 1
            wr = [R(lst[0][0][1][0])]
            mm(lst[:k], start, False, wr, after)
            return mm(lst[k:], False, stop, wr)

        def fn(e):
            ins = None
            for k, (o, l, r) in enumerate(lst):
                ins = g.tensor.matmul(o[0], l[0], r[0], start and k == 0, stop and k == len(lst) - 1)
            return ins
        cost = sum(max(64, r[2]) * (1 if r[3] else 4) * PECY for (o, l, r) in lst) + (PFIX if stop else 0.0)
        return add("P", fn, [x[1] for x in lst] + [x[2] for x in lst], wr or [x[0] for x in lst], cost, after=after,
                   cont=not start)

    def relu(o, i):
        def fn(e):
            if e == "A":
                return g.scalar.activation(o[0], i[0], AF.Relu)
            return g.vector.tensor_scalar(o[0], i[0], 0.0, None, A.max)
        return add(RENG, fn, [i], [o], vc(i[2]))

    def gather(o, win, off, bias=None, eng="AV", alt=0.0):
        def fn(e):
            src = win[0].indirect(off[0])
            if e == "A":
                if bias is None:
                    return g.scalar.activation(o[0], src, AF.Identity)
                return g.scalar.activation(o[0], src, AF.Identity, bias=bias[0])
            if bias is None:
                return g.vector.tensor_copy(o[0], src)
            return g.vector.tensor_scalar(o[0], src, bias[0], None, A.add)
        return add(eng, fn, tup(win, off, bias), [o], vc(o[2], GA), alt=alt)

    def dma(eng, o, i, r, w, lat):
        s = "d%d" % ndma[0]
        ndma[0] += 1
        return add(eng, lambda e: Q[e].dma_start(o, i), r, w, 60.0, lat=lat, sem=s, cnt=16)

    nsent = [0]

    def send(src, dst, sem, to, lat, after=()):
        rid, pid, _ = topo.addr(to)
        mask = topo.mask(core, to)
        ne = len(topo.engines(core, to))
        nsent[0] += ne
        i = add("G", lambda e: g.remote_dma(dst[0], src[0], T.sem[sem], T.sem.sent, pid, rid, mask), [src], [],
                300.0, sem="-", after=after)
        add("N", None, [], [dst], OCC * lat, lat=lat - OCC * lat / LF, sem=sem, cnt=ne, after=[i])
        return i

    C = lambda j: R("col", j, j + 1)
    PI = lambda j: R("pi", j, j + 1)
    IB = lambda j: R("IB", 128 * j, 128 * j + 128)

    dma("S", T.ami[:], T.am[:], [], [R("ami")], 2000.0)
    dma("S", T.Z[:, 0:256], T.zv[:], [], [R("Z", 0, 256)], 2000.0)
    dma("S", T.wti[:, 0:1], T.wt[:], [], [R("wti")], 2000.0)
    dma("A", T.X[:], T.xt[:], [], [R("X")], XLAT / LF)

    iota(PI(0), [[0, 1]], 0, 1)
    iota(R("lin"), [[1, 144]])
    iota(R("idq", 0, 128), [[1, 8], [0, 16]])
    iota(R("idq", 128, 768), [[1, 40], [0, 16]], 8)
    for q in range(4):
        iota(R("srev", 32 * q, 32 * q + 32), [[4, 2], [8, 2], [16, 8]], (q >> 1) + 2 * (q & 1))
    iota(R("gl"), [[0, 16], [1, 8]])
    iota(R("srev", 128, 256), [[1, 16], [16, 8]])
    iota(R("rows"), [[256, 8]])
    iota(R("c32", 0, 16), [[512, 16]])
    iota(R("c32", 16, 32), [[0, 4], [512, 4]])
    ts(PI(1), PI(0), 15, A.bitwise_and)
    ts(PI(2), PI(0), 4, A.arith_shift_right)
    cp(C(0), PI(0)); cp(C(1), PI(1)); cp(C(2), PI(2))
    ts(PI(3), PI(1), 11.0, A.mult)
    ts(PI(4), PI(3), 5, A.arith_shift_right)
    cp(C(3), PI(4))
    ts(C(4), C(3), -3.0, A.mult, C(1), A.add)
    ts(PI(7), PI(4), 1, A.arith_shift_right)
    ts(C(26), PI(7), -40.0, A.mult, C(2), A.add)
    ts(C(5), C(3), 24.0, A.mult, C(26), A.add)
    ts(C(6), C(4), 0.0, A.is_equal, -65535.0, A.mult)
    ts(C(7), C(4), 1.0, A.is_equal, -255.0, A.mult)
    ts(C(8), C(6), C(7), A.add, -1.0, A.add)
    ts(C(9), C(4), 2.0, A.is_equal)
    ts(C(10), C(1), 15.0, A.is_equal, C(9), A.add)
    BIAS = C(24)
    ts(BIAS, C(10), -1.0, A.mult, -255.0, A.add)
    ts(C(11), BIAS, 0.5, A.mult, 0.25, A.add)
    ts(C(23), BIAS, 0.5, A.add)
    ts(C(12), C(1), 16.0, A.mult)
    ts(C(13), C(1), 32.0, A.mult)
    ts(C(14), C(2), 16.0, A.mult)
    ts(C(15), C(14), 15.0, A.add)
    ts(C(17), C(1), -1.0, A.mult, C(15), A.add)
    cp(C(18), R("wti", 0, 1))
    ts(IB(0), R("lin", 0, 128), C(0), A.is_equal)
    cp(R("IF"), IB(0), "AV")
    for j, c in ((1, -1.0), (2, -2.0 ** 86), (3, 2.0 ** -10), (4, -8.0), (5, -1.0 / 32), (6, -32.0), (7, 4096.0)):
        ts(IB(j), IB(0), c, A.mult)
    ts(R("Wk"), R("lin", 0, 48), C(5), A.is_equal, C(8), A.mult)
    for j in range(6):
        c = 24 * (j & 1) + 8 * (j >> 1)
        ts(R("Wk", c, c + 8), R("Wk", c, c + 8), -2.0 ** (50 - 26 * j), A.mult)
    add("V", lambda e: g.vector.tensor_reduce(T.col[:, 25:26], T.Wk[:], AxisListType.X, A.add, negate=True),
        [R("Wk")], [C(25)], vc(48))
    ts(R("Wrep"), R("idq"), C(5), A.is_equal, C(25), A.mult)
    ts(R("blk"), R("idq", 0, 128), C(2), A.is_equal)
    ts(R("Wblk"), R("idq", 0, 128), C(2), A.is_equal, C(18), A.mult)
    ts(R("Wband"), R("lin", 0, 144), C(15), A.is_equal, C(18), A.mult)
    ts(R("diag", 0, 16), R("lin", 0, 16), C(1), A.is_equal)
    mset(R("seg"), 0.0)
    mset(R("seg", 0, 128, 16), -2.0 ** 90)
    tt(R("tmp", 0, 16), R("diag", 0, 16), R("srev", 0, 128, 8), A.mult)
    add("V", lambda e: g.vector.tensor_reduce(T.col[:, 19:20], T.tmp[:, 0:16], AxisListType.X, A.add),
        [R("tmp", 0, 16)], [C(19)], vc(16))
    ts(C(20), C(19), C(14), A.add)
    ts(R("PP"), R("lin", 0, 128), C(20), A.is_equal)
    ts(R("W32"), R("Wblk"), 32.0, A.mult)
    ts(R("blkn"), R("blk"), 2.0 ** 14, A.mult)
    ts(C(21), C(19), -15.5, A.add, -2.0 ** 15, A.mult)
    ts(IB(8), IB(0), C(21), A.mult)
    KM, KMASK = float(0x1111 << 12), (1 << 24) | (1 << 21) | (1 << 18) | (1 << 15)
    CB = lambda j: R("cb", j, j + 1)
    mset(CB(0), 3 * 2.0 ** 21)
    ts(CB(1), C(19), 1024.0, A.mult)
    ts(CB(2), C(19), 160.0, A.mult)
    ts(PI(5), C(19), KM, A.mult)
    ts(PI(6), PI(5), KMASK - (1 << 15), A.bitwise_and)
    ts(PI(8), PI(5), 1 << 15, A.bitwise_and)
    ts(CB(4), PI(6), -1.0, A.mult, 2.0 ** 24, A.add)
    ts(CB(5), PI(8), -1.0, A.mult)
    for nm, a, b in (("Fk", 0, 3), ("CD", 4, 6)):
        mm([(R("b1", 0, 128, p=(0, b - a)), R("cb", a, b), IB(0))])
        cp(R(nm, p=(0, b - a)), R("b1", 0, 128, p=(0, b - a)), "AV")
    for a, st, c in ((1, 2, 8.0), (2, 4, -4.0), (4, 8, -10.0), (0, 8, -13.0)):
        mset(R("d0", a, 128, st), c)
    mset(R("ones"), 1.0)
    mset(R("cc", 0, 128, p=(0, 32)), -2.0 ** 19)
    mset(R("cc", 0, 128, p=(32, 64)), 256.0)
    mset(R("cc", 128, 256, p=(0, 32)), 6144.0)
    mset(R("K16", 0, 1), -2.0 ** 22 - 0.5)
    ts(R("c32"), R("c32"), C(13), A.add)
    c8 = lambda nm: R(nm, 0, 128)
    ts(c8("mG"), R("gl"), C(2), A.is_equal)
    ts(c8("D8"), c8("srev"), C(17), A.is_equal, -4096.0, A.mult)
    ts(R("tmb", 0, 128), c8("srev"), C(17), A.is_gt, 0.5, A.mult)
    ts(R("tmb", 128, 256), c8("srev"), C(15), A.is_gt, -0.5, A.mult)
    ts(C(16), C(1), 0.5 / 4096, A.mult)
    ts(R("tmb", 256, 384), c8("D8"), C(16), A.mult)
    mm([(R("b0", 0, 128), IB(0), R("tmb", 128 * j, 128 * j + 128)) for j in range(3)])
    cp(c8("Tri"), R("b0", 0, 128), "AV")
    ts(c8("Prm"), R("srev", 128, 256), C(0), A.is_equal)
    mset(R("tt", 0, 256, 64), -2.0 ** 90)
    mset(R("ee"), 0.0)
    mset(R("Kp", 15, 1600, 400), 0.0)
    cp(R("junk"), R("ami"))
    for h in range(2):
        mm([(R("m%d" % h, 0, 128), R("PP"), R("junk", 128 * h, 128 * h + 128))])
        cp(R("nf", 128 * h, 128 * h + 128), R("m%d" % h, 0, 128), "AV")
    ONE = R("ones", 0, 128)
    const = lambda out, j: (out, R("cc", 128 * j, 128 * j + 128, p=(0, 32)), R("ones", 0, out[2], p=(0, 32)))

    def plane(h, j, lo=0, hi=128):
        return R(("xa%d", "b%d")[j & 1] % h, 128 * (j >> 1) + lo, 128 * (j >> 1) + hi)

    def offsets(src, off, M, c, tmp, h, t):
        for a, b in (QP if off == "offx" and t else ((0, 128),)):
            sub = lambda x: R(x[1][0], x[1][1] + a, x[1][1] + b)
            ts(sub(c), sub(src), 16.5, A.mult, R("K16", t, t + 1), A.add)
            tt(R("p1", tmp + a, tmp + b), sub(src), R(M, 128 + a, 128 + b), A.mult)
            tt(R("p2", tmp + a, tmp + b), R("p1", tmp + a, tmp + b), sub(c), A.add)
            ts(R("p3", tmp + a, tmp + b), R("p2", tmp + a, tmp + b), 4, A.arith_shift_right, V - 1, A.bitwise_and)
            cp(R(off, 128 * h + a, 128 * h + b), R("p3", tmp + a, tmp + b))

    def fallback(h, W, out, t):
        hl = lambda nm, b=0: R(nm, b + 128 * h, b + 128 * h + 128)
        mm([(W, R("Fk", p=(0, 3)), R("ones", 0, 128, p=(0, 3))), (W, R("W32"), hl("Z", 256 * t)),
            (W, IB(6), hl("q0", 256 * t))])
        tt(hl("f1"), hl("p1"), W, A.add)
        ts(out, hl("f1"), 5, A.arith_shift_right, V - 1, A.bitwise_and)

    def items(off, buf, h, eng):
        w_ = 128 // len(eng)
        for q in range(len(eng)):
            lo = 128 * h + w_ * q
            gather(R(buf, 16 * lo, 16 * (lo + w_)), R("X"), R(off, lo, lo + w_), BIAS, eng[q % len(eng)], alt=GALT)

    def keys(buf, bank, h, part, stop, start=True):
        mm([(R(bank, k, 384, 16), R(buf, 2048 * h + 15 - brev(k), 2048 * h + 2048, 16),
             R("Wk", 24 * part, 24 * part + 24)) for k in range(16)], start=start, stop=stop, wr=[R(bank)])

    def diffs(piv, buf, bk, h, ds):
        mm([(R(bk, 0, 384), piv, R("Wrep", 0, 384))], start=False, stop=False, wr=[R(bk)])
        keys(buf, bk, h, 1, False, False)
        mm([(R(bk, 0, 384), piv, R("Wrep", 384, 768))], start=False, wr=[R(bk)])
        cp(R("DS", ds, ds + 384), R(bk, 0, 384), "AV")

    def fix(q):
        off = T.offc[:, 16 + 4 * q:20 + 4 * q]
        a, b = R("xs", 64 * q, 64 * q + 64), R("xi", 64 * q, 64 * q + 64)
        add("V", lambda e: g.vector.tensor_tensor(a[0], T.yxs[:].indirect(off), b[0], A.add),
            [R("yxs"), R("offc", 16, 32), b], [a], vc(64, GA))
        add("V", lambda e: g.vector.tensor_copy(T.yxs[:].indirect(off), a[0]),
            [a, R("offc", 16, 32)], [R("yxs")], vc(64, 3.8))

    ysum = lambda h: R(YS[0] % h, YS[1], YS[1] + 128)

    def flags(h, a, sm):
        w = lambda nm: R(nm, 256 * h + a, 256 * h + a + 128)
        act(w("keep"), sm, AF.Sign, bias=2.0 ** -84)
        tt(w("kf"), sm, w("TH"), A.is_ge)

    def order_sum(out, ds, dead, th, n=3):
        mm([(out, IB(3), th), (out, dead, IB(2))]
           + [(out, R("DS", ds + 128 * j, ds + 128 * j + 128), IB(0)) for j in range(n)])

    for t in range(RO):
        to = T.cores[(rank + 1 + t % (N - 1)) % N]
        H = range(2)
        ln = lambda nm, h, base=0: R(nm, base + 128 * h, base + 128 * h + 128)
        for h in H:
            send(ln("nf", h, 256 * t), ln("bn", h, 256 * t), "rn%d" % (2 * t + h), to, 3500.0)
        for h in H:
            cur[0] = h
            M = "m%d" % h
            mm([(R(M, 0, 128), R("Wblk"), ln("Z", h, 256 * t))])
            ts(ln("q0", h, 256 * t), R(M, 0, 128), 3 * 2.0 ** 16 - 511.5, A.add)
            U = R(M, 128, 256)
            mm([(U, R("Wblk"), ln("Z", h, 256 * t)), (U, IB(1), ln("q0", h, 256 * t)), const(U, 1)])
            offsets(ln("nf", h, 256 * t), "offx", M, R("b%d" % h, 256, 384), 128 * h, h, t)
        cur[0] = 0
        mm([(R("m0", 384, 400), R("Wband", 15 - il, 143 - il), R("Z", 256 * t + il, 256 * t + 256, 16)) for il in range(16)])
        cp(R("ci"), R("m0", 384, 400))
        ts(R("cj"), R("ci"), 31, A.bitwise_and)
        tt(R("cf"), R("cj"), R("c32", 0, 16), A.add)
        cp(R("offc", 0, 16), R("cf"))
        if t == RO - 1:
            tt(R("cf"), R("cj"), R("c32", 16, 32), A.add)
            cp(R("offc", 16, 32), R("cf"))
            for q in range(4):
                bk = "ya%d" % (q & 1)
                mm([(R(bk), IB(0), R("X", 2048 * a + 512 * q, 2048 * a + 512 * q + 512)) for a in range(4)])
                cp(R("yxs", 512 * q, 512 * q + 512), R(bk), "AV")
        for h in H:
            cur[0] = h
            items("offx", "xg", h, GX[h] if t else GX0[h])
            keys("xg", "xa%d" % h, h, 0, True)
            keys("xg", "b%d" % h, h, 1, True)
            offsets(ln("bn", h, 256 * t), "offy", "m%d" % h, R("m%d" % h, 0, 128), 256 + 128 * h, h, t)
            items("offy", "yg", h, GY[h])
            keys("yg", "ya%d" % h, h, 0, False)
        for h in H:
            cur[0] = h
            M = "m%d" % h
            fallback(h, R(M, 384, 512), ln("f2", h), t)
            kp = lambda j, d=0: R("Kp", 800 * h + 400 * (j & 1) + 128 * (j >> 1) + 16 - d,
                                  800 * h + 400 * (j & 1) + 128 * (j >> 1) + 144 - d)
            if XV:
                cp(kp(0), plane(h, 0), "AV")
            for j in range(6 if AS else 0):
                for c in range(0, 128, 128 // AS):
                    e_ = c + 128 // AS
                    sb = lambda nm, a=0, b=0: R(nm, b + 128 * h + c + a, b + 128 * h + e_)
                    scan(sb("tt", 1), plane(h, j, c, e_ - 1), R("seg", c + 1, e_) if j == 0 else sb("S", 1),
                         A.max, A.min, -2.0 ** 90)
                    if j < 5:
                        tt(sb("D"), plane(h, j, c, e_), sb("tt"), A.subtract)
                        tt(sb("S"), sb("tt"), plane(h, j, c, e_), A.subtract)
                        tt(plane(h, j + 1, c, e_), plane(h, j + 1, c, e_), sb("D"), A.min)
                    else:
                        tt(sb("dA", 0, 256 * t), plane(h, j, c, e_), sb("tt"), A.is_lt)
            for j in range(0 if AS else 6):
                here, other = plane(h, 6 + (j & 1)), plane(h, 7 - (j & 1))
                if j == 0:
                    Kj, Tj = plane(h, 0), ln("tt", h)
                    scan(R("tt", 128 * h + 1, 128 * h + 128), plane(h, 0, 0, 127), R("seg", 1, 128), A.max, A.min,
                         -2.0 ** 90)
                else:
                    Kj, Tj = kp(j if XV else 1), here
                    scan(Tj, kp(j if XV else 1, 1), other, A.max, A.min, -2.0 ** 90)
                if j < 5:
                    tt(ln("D", h), Kj, Tj, A.subtract)
                    mm([(here, IB(1), ln("D", h))])
                    tt(kp(j + 1 if XV else 1), plane(h, j + 1), ln("D", h), A.min)
                else:
                    tt(ln("dA", h, 256 * t), Kj, Tj, A.is_lt)
            dead, eb, om = ln("dA", h, 256 * t), 144 * h, 16 * t + 8 * h
            scan(ln("c1", h), R("d0"), dead, A.add, A.mult)
            cp(R("ee", eb + 16, eb + 144, 16), R("c1", 128 * h + 15, 128 * h + 128, 16), "VA")
            mm([(R(M, 256, 264), R("ones", 0, 128, p=(0, 1)), R("rows", p=(0, 1)))]
               + [(R(M, 256, 264), R("ee", eb + 16 - il, eb + 144 - il), R("IB", il, 128, 16)) for il in range(16)])
            ts(R("offm", om, om + 8), R(M, 256, 264), C(12), A.add)
            first = send(R("offm", om, om + 8), R("offb", om, om + 8), "ro%d" % (2 * t + h), to, 2200.0)
            send(dead, ln("dB", h, 256 * t), "rd%d" % (2 * t + h), to, 2500.0, [first] if ORD else [])
            gather(ln("Mb", h), R("xg", 2048 * h, 2048 * h + 2048), R("offm", om, om + 8), alt=FALT)
            if not XV:
                keys("xg", "xa%d" % h, h, 0, False)
            W = R(WB[0] % h, 384, 512)
            mm([(W, IB(0), ln("Z", h, 256 * t)), (W, IB(1), ln("Mb", h))])
            act(ln("ge", h), W, AF.Sign, bias=C(23))
            mm([(W, R("blk"), ln("ge", h))])
            act(R("TH", 256 * h, 256 * h + 128), W, AF.Relu, bias=-2.0 ** 90, scale=-2.0 ** 89)
            act(R("TH", 256 * h + 128, 256 * h + 256), W, AF.Relu, bias=2.0 ** 91, scale=2.0 ** 89)
            diffs(ln("Mb", h), "yg", "ya%d" % h, h, 384 * (4 + h))
            P = R("ya%d" % h, 0, 256)
            mm([(P, R("cc", 0, 128, p=(0, 64)), R("ones", p=(0, 64))),
                (R("ya%d" % h, 0, 256, 2), ln("nf", h, 256 * t), c8("Prm")),
                (R("ya%d" % h, 1, 256, 2), ln("bn", h, 256 * t), c8("Prm"))], stop=False,
               wr=[R("ya%d" % h)])
        cur[0] = 0
        if XI:
            op = A.add if t < RO - 1 else A.subtract
            add("V", lambda e, op=op: g.vector.tensor_tensor(T.junk[:], T.X[:].indirect(T.offc[:, 0:16]), T.Mb[:], op),
                [R("X"), R("offc", 0, 16), R("Mb")], [R("junk")], vc(256, GA))
            ts(R("xi"), R("junk"), 0.5 if t < RO - 1 else -0.5, A.mult, C(11), A.subtract)
        else:
            gather(R("xo"), R("X"), R("offc", 0, 16), alt=FALT)
        for h in (() if XI else H):
            W = R(WB[1] % h, 256 if WB[1][0] == "b" else 384, 384 if WB[1][0] == "b" else 512)
            mm([(W, IB(0 if t < RO - 1 else 1), ln("xo", h)), (W, IB(0), ln("Mb", h))])
            ts(ln("xi", h), W, 0.5, A.mult, C(11), A.subtract)
        if t < RO - 1:
            add("V", lambda e: g.vector.tensor_copy(T.X[:].indirect(T.offc[:, 0:16]), T.xi[:]),
                [R("xi"), R("offc", 0, 16)], [R("X")], vc(256, 3.8))
            W = R(WB[2] % 1, 384, 512)
            mm([(W, ONE, ln("dA", h, 256 * t)) for h in H]
               + [(W, R("ones", 0, 128, p=(0, 1)), R("IB", 128 * 5, 128 * 6, p=(0, 1)))])
            act(R("xs", 0, 128), W, AF.Identity, bias=-32768.0, scale=16.0, acc=R("K16", t + 1, t + 2))
        else:
            for q in range(4):
                fix(q)
            for q in range(2):
                dma("SA"[q], T.yx[:, 1024 * q:1024 * q + 1024], T.yxs[:, 1024 * q:1024 * q + 1024], [R("yxs")], [], 4000.0)
        for h in H:
            cur[0] = h
            M, om = "m%d" % h, 16 * t + 8 * h
            gather(ln("Yb", h), R("yg", 2048 * h, 2048 * h + 2048), R("offb", om, om + 8), alt=FALT)
            order_sum(ysum(h), 384 * (4 + h), ln("dB", h, 256 * t), R("TH", 256 * h + 128, 256 * h + 256))
            flags(h, 128, ysum(h))
            if XV:
                for q in range(2):
                    pv, a = plane(h, q, 0, 384), 800 * h + 400 * q + 16
                    mm([(pv, ln("Yb", h), R("Wrep", 384 * q, 384 * q + 384))])
                    tt(R("DS", 768 * h + 384 * q, 768 * h + 384 * q + 384), R("Kp", a, a + 384), pv, A.add)
            else:
                diffs(ln("Yb", h), "xg", "xa%d" % h, h, 768 * h)
            order_sum(R(M, 128, 256), 768 * h, ln("dA", h, 256 * t), R("TH", 256 * h, 256 * h + 128), 6 if XV else 3)
            W = R(WB[3] % h, 384, 512)
            mm([(W, IB(0), ln("Z", h, 256 * t)), (W, IB(1), ln("Yb", h))])
            act(ln("Z", h, 256 * t + 256) if t < RO - 1 else ln("zf", h), W, AF.Abs, bias=BIAS)
        if t == RO - 1:
            dma("S", T.yz[:], T.zf[:], [R("zf")], [], 2000.0)
        for h in H:
            cur[0] = h
            M = "m%d" % h
            w2 = lambda nm, lo=0, hi=256, st=1: R(nm, 256 * h + lo, 256 * h + hi, st)
            flags(h, 0, R(M, 128, 256))
            XA, YA = "xa%d" % h, "ya%d" % h
            Tt, P, O = R(XA, 0, 256), R(YA, 0, 256), R(XA, 256, 384)
            kA, kB, fA, fB = w2("keep", 0, 128), w2("keep", 128, 256), w2("kf", 0, 128), w2("kf", 128, 256)
            tgt = lambda b: [(R(b, 0, 256, 2), kA, c8("Tri")), (R(b, 1, 256, 2), kB, c8("Tri")),
                             (R(b, 0, 256, 2), fB, c8("mG")), (R(b, 1, 256, 2), fA, c8("mG"))]
            mm(tgt(XA), wr=[R(XA)])
            T2 = R("b%d" % h, 0, 256)
            G = R(M, 384, 512)
            lo = lambda s, a=0, b=128, st=1: R("va", 256 * h + 128 * s + a, 256 * h + 128 * s + b, st)
            hi = lambda s, a=0, b=128, st=1: R(YA, 256 + 128 * s + a, 256 + 128 * s + b, st)
            mm(tgt("b%d" % h), stop=False, wr=[R("b%d" % h)])
            act(w2("sg"), Tt, AF.Sign, bias=-8.0)
            mm([(T2, IB(4), w2("sg"))], start=False, wr=[R("b%d" % h)])
            ts(w2("k1"), T2, -0.5, A.add, KM, A.mult)
            mm([(R(YA, 0, 256, 2), kA, c8("D8")), (R(YA, 1, 256, 2), kB, c8("D8"))], start=False, stop=False, wr=[P])
            mm([(P, IB(7), w2("sg"))], start=False)
            ts(w2("k2"), w2("k1"), KMASK, A.bitwise_and)
            tt(lo(0), w2("k2", 0, 128), R(YA, 0, 128), A.add)
            tt(hi(0), w2("k2", 128, 256), R(YA, 128, 256), A.add)
            mm([(G, IB(8), ONE), (G, R("blkn"), kA), (G, R("blkn"), kB)])
            tt(ln("fb", h), ln("f2", h), G, A.max)
            mm([(O, R("CD", p=(0, 2)), R("ones", 0, 128, p=(0, 2)))], stop=False, wr=[R(XA)])
            for st in range(4):
                s, d = st & 1, 1 - (st & 1)
                for q, dst in ((0, lo), (1, hi)):
                    for b3, op in ((0, A.min), (1, A.max)):
                        r0 = 16 * h + 8 * q
                        o = dst(d, b3, 128, 2) if st < 3 else (T.fin[:, r0:r0 + 8, b3:16:2],
                                                               ("fin", 16 * r0 + b3, 16 * r0 + 128, 2), 64, False, False)
                        tt(o, lo(s, 64 * q, 64 * q + 64), hi(s, 64 * q, 64 * q + 64), op)
            fin = lambda L_: (T.fin[:, 16 * h + L_:16 * h + 16:2, :], ("fin", 256 * h, 256 * h + 256, 1), 128, False, False)
            tt(ln("mg", h), fin(0), fin(1), A.min)
            mm([(O, ln("mg", h), R("IF"))], start=False)
            tt(ln("nf", h, 256 * (t + 1)), ln("fb", h), O, A.min)
            if t == RO - 1:
                mm([(R(M, 0, 128), R("PP"), ln("nf", h, 256 * (t + 1)))])
                cp(ln("yas", h), R(M, 0, 128), "AV")
                dma("S", T.ya[:, 128 * h:128 * h + 128], T.yas[:, 128 * h:128 * h + 128], [ln("yas", h)], [], 2000.0)
    return ops, nsent[0], Q


def rank_program(g, core, T, topo):
    if T.rank_of(core) is None:
        return
    ops, nsent, Q = build(g, core, T, topo)
    order, _ = plan_order(ops, ORDER)
    count = {"V": 0, "A": 0, "P": 0, "G": 0}
    seen = {}
    bank = {}

    def wait(e, sem, n):
        if seen.get((e, sem), 0) < n:
            Q[e].wait_ge(T.sem[sem], n)
            seen[(e, sem)] = n

    for i in order:
        o = ops[i]
        e = o["on"]
        if e == "N":
            continue
        need = [d for d in o["deps"] if (d not in o["soft"] or ops[d]["on"] != e) and ops[d]["sem"] != "-"]
        for b in o["banks"]:
            need += [j for e2, j in bank.get(b, {}).items() if e2 != e]
            bank.setdefault(b, {})[e] = i
        for d in sorted(need, key=lambda j: -ops[j]["st"]):
            s, n = ops[d]["sem"], ops[d]["cnt"]
            if seen.get((e, s), 0) < n:
                wait(e, s, n)
                for s2, n2 in ops[d].get("knew", ()):
                    seen[(e, s2)] = max(seen.get((e, s2), 0), n2)
        o["knew"] = [(s, n) for (e2, s), n in seen.items() if e2 == e]
        ins = o["fn"](e)
        if o["sem"] is None:
            count[e] += 1
            o["sem"], o["cnt"] = "e" + e, count[e]
            ins.then_inc(T.sem["e" + e], 1)
        elif o["sem"] != "-":
            ins.then_inc(T.sem[o["sem"]], 16)
    for e in ("V", "A", "P", "G"):
        wait("G", "e" + e, count[e])
    wait("G", "sent", nsent)
    for o in ops:
        if o["sem"] != "-":
            wait("G", o["sem"], o["cnt"])
